import numpy as np, ml_dtypes
CORES = [16,18,20,22]
N = 4
BF = ml_dtypes.bfloat16
def gentries(a):
    return np.ascontiguousarray(a.reshape(8, 16, -1).transpose(0, 2, 1)).reshape(8, -1)
def gtable(e):
    e = np.asarray(e); return np.ascontiguousarray(e.reshape(8, -1, 16).transpose(0, 2, 1)).reshape(128, -1).astype(np.int32)
V, G, LN, RO, SH = 2560, 256, 128, 3, 4
DS = [1, 3]
W = V + len(DS) * G
def graph(rng, share):
    s = rng.permutation(4 * V); n = int(4 * V * share); n = n + n % 2
    b = np.empty(4 * V, np.int64); b[s[:n]] = rng.integers(V, W, n); p = s[n:].reshape(2, -1)
    b[p[0]] = p[1] % V; b[p[1]] = p[0] % V
    return b
def marks(rng, size=1.0):
    return ((0.25 + 0.75 * rng.random((N, 8, 16, V))) * size).astype(np.float32)
def parts(rng):
    x = rng.integers(0, 4096, (N, 8, 16, V))
    nb = np.stack([np.stack([graph(rng, float(rng.choice(np.array([0.05, 0.15, 0.25])))) for g in range(8)]) for q in range(N)])
    z = (N, 8, RO, LN); k = rng.integers(0, 4, z); j = np.where(rng.random(z) < 0.95, (k + rng.integers(1, 4, z)) % 4, k)
    la = np.stack([rng.integers(0, V, z), j, k, rng.integers(0, 4, z), rng.integers(1, 17, z)])
    return x, marks(rng), nb, la
def pack(x, am, nb, la):
    d = {"x": np.ascontiguousarray(x.reshape(N, 128, V)).astype(np.int32), "am": np.ascontiguousarray(am.reshape(N, 128, V)).astype(BF), "nb": np.stack([gtable(t) for t in nb])}
    for i, name in enumerate(("lb", "pj", "pk", "pl", "hq")): d[name] = np.stack([gtable(t.reshape(8, -1)) for t in la[i]])
    return d
def setup_inputs(rng):
    return pack(*parts(rng))
def setup_inputs_spread(rng):
    x, am, nb, la = parts(rng)
    u = np.minimum(np.exp2(12.0 * rng.random(x.shape)).astype(np.int64) - 1, 4095); side = rng.random((N, 8, 1, V)) < 0.5
    return pack(np.where(side, 4095 - u, u), marks(rng, np.exp2(rng.integers(-1, 2, (N, 8, 1, V)).astype(np.float64))), nb, la)
def setup_inputs_ends(rng):
    x, am, nb, la = parts(rng); flip = rng.random(16) < 0.5; flip[0] = False; flip[15] = True; M = V // 8; late = np.arange(4, M - 1, 4)
    for q in range(N):
        for g in range(8):
            o = np.arange(1, V - 1); o = rng.permutation(o[o != G - 1])
            t = o[:4 * M].reshape(4, M).copy(); t[1, 0] = 0; t[1, 1] = V - 1; A, B, C, D = t
            col = rng.integers(0, 2, V); col[G - 1] = 1; cb = rng.integers(0, 2, M); cb[0] = 0; cb[1] = 1
            col[B] = cb; col[D] = cb; col[A] = 1 - cb; col[C] = 1 - cb
            col[A[late]] = cb[late]; col[D[late]] = 1 - cb[late]
            n = np.repeat(np.where(col == 0, W - 1, 0)[None], 4, 0); r = rng.random((4, V)) < 0.05; r[:, t.reshape(-1)] = False
            n = np.where(r, rng.integers(0, W, (4, V)), n)
            k = 3 * rng.integers(0, 2, M); j = 3 - k
            n[k, B] = A; n[j, B] = C; n[k, C] = D; n[j, C] = B; n[j, A] = B; n[k, D] = C
            nb[q, g] = n.reshape(-1)
            v = np.repeat(col[None], 16, 0); odd = t[:, 3:M - 1:2].reshape(-1); v[:, odd] = rng.integers(0, 2, (16, len(odd)))
            x[q, g] = 4095 * np.where(flip[:, None], 1 - v, v)
            b = np.where(rng.random((RO, LN)) < 0.7, rng.integers(0, 2, (RO, LN)), rng.integers(2, M - 1, (RO, LN))); b[:, LN - 1] = M - 1; b[:, LN - 2] = M - 4
            void = rng.random((RO, LN)) < 0.1; void[:, LN - 2:] = False
            la[0, q, g] = B[b]; la[2, q, g] = k[b]; la[3, q, g] = k[b]; la[1, q, g] = np.where(void, k[b], j[b])
    la[4] = np.where(rng.random(la[4].shape) < 0.5, 1, 16)
    am = rng.choice(np.array([0.125, 4.0], np.float32), am.shape)
    return pack(x, am, nb, la)
def tie(rng, n, t, more):
    p = np.argsort(rng.random((4, t.shape[1], 4)), axis=-1); A, B, C, D = t
    for i, names in enumerate(([B] + more[0], [A, C] + more[1], [B, D] + more[2], [C] + more[3])):
        for s, name in enumerate(names): n[p[i, :, s], t[i]] = name
    return p[1, :, 1], p[1, :, 0], p[2, :, 1]
def setup_inputs_calm(rng):
    x, am, nb, la = parts(rng); K = RO * LN; ki = np.arange(K) % 16; nl = K // 16; nk = 11 * nl; Q = 2 ** SH; late = np.arange(nl) * 16 // LN
    am = (0.125 + 0.125 * rng.random(am.shape)).astype(np.float32)
    a1 = 4 * nk; a2 = a1 + 12 * nl; a3 = a2 + 16 * nl; a4 = a3 + 6; a5 = a4 + RO * (3 * RO + 1) // 2
    for q in range(N):
        for g in range(8):
            o = rng.permutation(V); n = nb[q, g].reshape(4, V); xs = x[q, g]
            rest = o[a5:]; few = rest[rest >= G][:64]; fa, fb, fc, fd = few.reshape(4, 16)
            n[np.isin(n, fb)] = o[a3]
            own = np.concatenate([o[:a5], few]); n[:, own] = own
            L = np.zeros((5, K), np.int64)
            t = o[:a1].reshape(4, nk); A, B, C, D = t; m = ki < 11
            L[1, m], L[2, m], L[3, m] = tie(rng, n, t, [[A] * 3, [B] * 2, [C] * 2, [D] * 3])
            v = rng.choice(np.array([0, 1, 2, 3, 8, 15, 16]), nk); up = np.argsort(rng.random((16, nk)), axis=0) < v
            base = rng.integers(0, 2048, (16, nk)); flat = rng.integers(0, 4096, (16, nk))
            for i, step in enumerate((0, 1024, 2048, 2048)): xs[:, t[i]] = np.where(up, base + step, flat)
            L[0, m] = B; L[4, m] = np.clip(v + rng.integers(0, 2, nk), 1, 16)
            c = o[a1:a2].reshape(2, 6, nl); m = ki == 15
            for h in range(2):
                for i in range(6):
                    n[0, c[h, i]] = c[h, max(i - 1, 0)]; n[3, c[h, i]] = c[h, min(i + 1, 5)]; xs[:, c[h, i]] = 819 * i
            n[1, c[0, 2]] = c[1, 2]; n[2, c[1, 2]] = c[0, 2]
            L[0, m] = c[0, 2]; L[1, m] = 1; L[4, m] = 1
            p = rng.integers(2, 2049, 16); far = rng.integers(p + 2047, 4096)
            va = int(rng.choice(np.array([1, 2, 3, 8, 15, 16]))); act = (np.argsort(rng.random(16)) < va).astype(np.int64)
            xs[:, o[a3:a4]] = np.stack([p, p - 1, p + 1, p - 2, far - 1, p + 1025], axis=1)
            h0, hm, hp, h2, hc, one = [int(u) for u in o[a3:a4]]
            z = a4; tip = np.zeros(RO, np.int64)
            for r in range(RO):
                s = o[z:z + 3 * r + 2]; z += 3 * r + 2
                for i in range(3 * r + 2): xs[:, s[i]] = p + 1024 * (1 - i % 2) + i * (Q - 1)
                xs[:, s[-1]] = xs[:, s[-1]] + act
                n[0, s[:-1]] = s[1:]; tip[r] = s[0]
            for e in range(4):
                t = o[a2 + 4 * nl * e:a2 + 4 * nl * (e + 1)].reshape(4, nl); A, B, C, D = t; m = ki == 11 + e
                if e in (0, 3):
                    for i, at in enumerate((p, p - 1, far, p)): xs[:, t[i]] = at[:, None]
                    more = [[hm, hp, hp], [h2, h0], [hc, hc], [hm, hp, hp]]
                    if e == 3: more[0] = [hp, tip[late], one]
                else:
                    for i in range(4): xs[:, t[i]] = p[:, None]
                    more = [[A] * 3, [B] * 2, [C] * 2, [D] * 3]; w = rng.integers(1, 4, nl)
                    if e == 1: more[0] = [one, np.where(w > 1, one, A), np.where(w > 2, one, A)]
                    if e == 2: more[0] = [tip[late], A, A]
                L[1, m], L[2, m], L[3, m] = tie(rng, n, t, more); L[0, m] = B
                L[4, m] = rng.integers(1, 17, nl) if e < 2 else np.minimum(va + np.arange(nl) % 2, 16)
            d = 1024 + np.where(rng.random((16, 16)) < 0.5, -1, 1) * rng.integers(900, 1017, (16, 16)); mid = rng.integers(d, 4096 - d); side = np.where(rng.random((16, 16)) < 0.5, -1, 1)
            xs[:, fa] = mid; xs[:, fb] = mid + side * d; xs[:, fc] = mid - side * d; xs[:, fd] = mid + side * d
            n[0, fa] = fb; n[1, fa] = fc; n[2, fa] = fb; n[3, fa] = fc; n[:, fb] = fd
            am[q, g][:, fb] = 4.0
            la[:, q, g] = L.reshape(5, RO, LN)
    return pack(x, am, nb, la)
def setup_inputs_corners(rng):
    x, am, nb, la = parts(rng)
    am = np.where(rng.random(am.shape) < 0.06, 0.125, np.exp2(-3.0 + 2.0 * rng.random(am.shape))).astype(np.float32)
    x = np.where(rng.random(x.shape) < 0.8, rng.choice(np.array([0, 1, 1023, 1024, 1025, 2047, 2048, 4094, 4095]), x.shape), x)
    for q in range(N):
        for g in range(8):
            n = nb[q, g].reshape(4, V); ty = (g + q) % 6
            if ty == 0: n[:] = rng.integers(V, W, (4, V))
            if ty == 1:
                for k in (0, 1, 3):
                    m = rng.permutation(V).reshape(2, -1); n[k, m[0]] = m[1]; n[k, m[1]] = m[0]
                n[2] = n[0]
            if ty == 2:
                m = rng.permutation(V)[:5 * (V // 10)].reshape(5, -1)
                for i in range(5):
                    for k in range(4): n[k, m[i]] = m[(i + 1 + k) % 5]
            if ty == 3: n[:] = rng.integers(0, V, (4, V))
            if ty == 4: n[:] = np.where(rng.random((4, V)) < 0.1, np.arange(V)[None], n)
            if ty == 5: n[:] = np.where(rng.random((4, V)) < 0.3, rng.choice(np.array([0, V - 1, V, W - 1]), (4, V)), n)
    la[0] = np.where(rng.random(la[0].shape) < 0.1, rng.choice(np.array([0, V - 1]), la[0].shape), la[0])
    la[4] = rng.choice(np.array([1, 2, 15, 16]), la[4].shape)
    return pack(x, am, nb, la)
def block(n, a, b, c, d):
    n[0, b] = a; n[3, b] = c; n[2, c] = b; n[0, c] = d; n[1, a] = b; n[2, d] = c
def setup_inputs_crowd(rng):
    x, am, nb, la = parts(rng)
    for q in range(N):
        for g in range(8):
            n = nb[q, g].reshape(4, V); ty = (g + q) % 5; o = rng.permutation(V); L = la[:, q, g]; z = int(rng.integers(0, 4))
            if ty <= 1:
                at = o[:2 * LN + 9]; n[:, at] = rng.integers(V, W, (4, len(at)))
                h = o[0]; D = o[1:5]; B = o[5:5 + LN]; A = o[5 + LN:5 + 2 * LN]
                n[:, h] = D; n[0, D] = h; n[0, B] = A; n[3, B] = h; n[1, A] = B
                for t in range(RO): L[0, t] = rng.permutation(B)
                L[1] = 3; L[2] = 0; L[1, 0, :z] = 0
                if ty == 1:
                    a, b, c, d = o[5 + 2 * LN:9 + 2 * LN]; block(n, a, b, c, d); L[0, :, LN - 1] = b; L[3, :, LN - 1] = 0
            if ty == 2:
                n[:, o[:4]] = rng.integers(V, W, (4, 4)); block(n, o[0], o[1], o[2], o[3])
                L[0] = o[1]; L[1] = 3; L[2] = 0; L[3] = 0; L[1, :, :z] = 0
            if ty == 3:
                m = o[:3 * LN + 1]; n[:, m] = rng.integers(V, W, (4, len(m))); n[0, m[1:]] = m[:-1]; n[3, m[:-1]] = m[1:]
                for t in range(RO): L[0, t] = m[3 * (np.arange(LN) if t == 0 else rng.permutation(LN)) + 1]
                L[1] = 3; L[2] = 0; L[3] = 3
            if ty == 4:
                e = int(rng.integers(1, RO)); L[1, e] = L[2, e]; L[4, e - 1, ::2] = 1
    return pack(x, am, nb, la)
def check_ranges(d):
    bad = []
    for k, lo, hi in (("x", 0, 4095), ("nb", 0, W - 1), ("lb", 0, V - 1), ("pj", 0, 3), ("pk", 0, 3), ("pl", 0, 3), ("hq", 1, 16)):
        if np.min(d[k]) < lo or np.max(d[k]) > hi: bad.append("range of " + k)
    m = np.asarray(d["am"]).astype(np.float32)
    if not np.all((m >= 0.125) & (m <= 4.0)): bad.append("range of am")
    return bad
def full(s, r):
    return np.concatenate([s[r]] + [np.roll(s[(r - DS[b]) % N], -b, axis=0)[..., :G] for b in range(len(DS))], axis=2)
def pick(w, n):
    return np.stack([w[g][:, n[g].reshape(-1)] for g in range(8)]).reshape(8, 16, 4, V)
def pulls(w, n):
    d = pick(w, n) - w[:, :, None, :V]
    return np.clip(d - 1024 * np.sign(d), -1023, 1023)
def sweep(s, n, stress):
    new, e = [], []
    for r in range(N):
        p = pulls(full(s, r), n[r])
        if stress: e.append(np.sum(p * p, axis=2))
        new.append(np.clip(s[r] + (np.sum(p, axis=2) >> SH), 0, 4095).astype(np.int32))
    return np.stack(new), e
def winners(n, B, j, k, l):
    A = n[k, B]; C = n[j, B]; c = np.minimum(C, V - 1); D = n[l, c]; a = np.minimum(A, V - 1); d = np.minimum(D, V - 1)
    pa = n[:, a] == B; pd = n[:, d] == C
    good = (A < V) & (C < V) & (D < V) & (A != B) & (A != C) & (A != D) & (B != C) & (B != D) & (C != D)
    good = good & np.any(pa, axis=0) & np.any(pd, axis=0) & ~np.any(n[:, a] == C, axis=0) & ~np.any(n[:, d] == B, axis=0)
    who = np.stack([A, B, C, D]); i = np.arange(LN); first = np.full(W, LN)
    np.minimum.at(first, who[:, good], np.broadcast_to(i, (4, LN))[:, good])
    w = np.nonzero(good & np.all(first[who] >= i, axis=0))[0]
    port = np.stack([np.argmax(pa, axis=0), k, l, np.argmax(pd, axis=0)])
    return w, who[:, w], (port * V + who)[:, w], np.stack([C, D, A, B])[:, w]
def reference(x, am, nb, lb, pj, pk, pl, hq):
    s = x.astype(np.int32).reshape(N, 8, 16, V)
    n = np.stack([gentries(t) for t in nb]).astype(np.int64).reshape(N, 8, 4, V)
    la = [np.stack([gentries(t) for t in u]).astype(np.int64).reshape(N, 8, RO, LN) for u in (lb, pj, pk, pl, hq)]
    for t in range(RO):
        s, e1 = sweep(s, n, True)
        done = []
        for r in range(N):
            for g in range(8):
                w, who, at, name = winners(n[r, g], la[0][r, g, t], la[1][r, g, t], la[2][r, g, t], la[3][r, g, t])
                flat = n[r, g].reshape(-1); old = flat[at]; flat[at] = name; done.append((r, g, w, who, at, old))
        s, e2 = sweep(s, n, False)
        s, e3 = sweep(s, n, True)
        for r, g, w, who, at, old in done:
            worse = np.sum(e3[r][g][:, who], axis=1) > np.sum(e1[r][g][:, who], axis=1)
            back = np.sum(worse, axis=0) >= la[4][r, g, t, w]
            flat = n[r, g].reshape(-1); flat[at[:, back]] = old[:, back]
    m = am.astype(np.float32).astype(np.float64).reshape(N, 8, 16, V); y = []
    for r in range(N):
        p = pulls(full(s, r), n[r]).astype(np.float64)
        y.append(np.sum(pick(full(m, r), n[r]) * np.exp(p * p * (-2.0 ** -19)), axis=2).reshape(128, V))
    return {"y": np.stack(y).astype(np.float32)}

def check_inputs(d):
    bad = list(check_ranges(d))
    if not bad:
        for name, y in reference(**d).items():
            for q in range(N):
                v = np.abs(np.asarray(y[q], np.float64)); s = np.sqrt(np.mean(v * v))
                if v.max() > 5 * s or s < 2.0 ** -2: bad.append('%s of rank %d is uneven or too small' % (name, q))
    return bad

@@ -1,0 +1,738 @@
+import math
+import numpy as np
+from concourse.bass import DstId, RemoteDMATransfer
+from concourse.mybir import AluOpType as A, ActivationFunctionType as F
+
+NV, GH, NW, RO = 2560, 256, 3072, 3
+DSH = [1, 3]
+DUM0, FLW = 11008, 11648
+BIG = 20000.0
+I32, F32, F16, B16, U16 = "int32", "float32", "float16", "bfloat16", "uint16"
+SB = {
+    "w0": ([NW], I32), "w1": ([NW], I32), "w2": ([NW], I32), "w3": ([NW], I32),
+    "fl": ([FLW], I32), "iw": ([NW], F32), "aw": ([NW], B16),
+    "d1": ([4 * NV], F16), "d2": ([4 * NV], F16), "d3": ([2048], F16), "xn0": ([NV], F16), "xn1": ([NV], F16),
+    "n32": ([640], I32), "of0": ([640], U16), "of1": ([640], U16),
+    "rs0": ([GH], I32), "rs1": ([GH], I32), "ra": ([GH], B16),
+    "em": ([2048], F16), "onef": ([128], F32), "idf": ([128], F32), "id2": ([128], F32), "idm2": ([128], F32),
+    "bof": ([128], F32), "bo": ([128], B16), "i1": ([128], F16), "i16": ([128], F16), "im64": ([128], F16),
+    "im1": ([128], F16), "imk": ([128], F16), "rot": ([128], F16), "cb": ([128], F16), "ones": ([512], F16),
+    "thr": ([128], F32), "dum": ([32], F32), "i8": ([8], I32), "pg": ([1], I32), "pgf": ([1], F32),
+    "lnf": ([8], F32), "wc": ([8], F32), "wt": ([64], F32),
+    "li": ([120], I32), "hb": ([24], I32), "tb": ([24], F32), "ub": ([24], F32), "bb": ([24], F32),
+    "p160": ([72], F32), "ib": ([48], F32), "ibu": ([48], U16), "hq16": ([24], F32),
+    "r1": ([256], F16), "r2": ([128], F16), "r3": ([1024], F16), "r4": ([1024], F16),
+    "hi": ([16], I32), "tt": ([16], F32), "uu": ([16], F32), "vv": ([8], F32), "bc": ([8], F32),
+    "h2": ([8], I32), "t2": ([8], F32), "u2": ([8], F32),
+    "ic": ([8], F32), "icu": ([8], U16), "bad": ([16], F32), "lad": ([16], U16), "lbc": ([16], U16),
+    "wh": ([32], F32), "whu": ([32], U16), "yy": ([4, 32], F32), "z1": ([64], F32), "zz": ([4, 48], F32),
+    "z2": ([2, 48], F32), "z3": ([48], F32), "z4": ([16], F32), "z5": ([16], F32), "gd": ([8], F32),
+    "ww": ([8], F32), "ng": ([8], F32), "pa": ([16], F32), "iad": ([16], F32), "rw": ([512], U16),
+    "q0": ([8, 4, 16], B16), "q1": ([8, 4, 16], B16), "q2": ([8, 4, 16], B16),
+    "lz": ([128], F16), "lb1": ([8], F32), "lb2": ([8], F32), "lb3": ([8], F32), "lb4": ([8], F32),
+    "o1": ([32], F32), "o2": ([32], F32), "ou": ([32], U16), "sl": ([160], U16),
+    "xo": ([512], F16), "sd": ([1536], F16), "ss": ([1536], F16), "es": ([2048], F16), "sef": ([128], F32),
+    "sq0": ([8, 4, 16], F32), "sq1": ([8, 4, 16], F32), "f1": ([128], F32),
+    "e0": ([1024], F32), "e1": ([1024], F32), "e2": ([1024], F32),
+    "t0": ([1024], F32), "t1": ([1024], F32), "t3": ([1024], F32),
+}
+SCRATCH = {k: ("sbuf", [128] + s, d) for k, (s, d) in SB.items()}
+SCRATCH["ps"] = ("psum", [128, 4096], F32)
+NSEM = 80
+SEMAPHORES = ["qv", "qa", "qp", "qg"] + ["arr%d" % i for i in range(11)] + ["m%d" % i for i in range(NSEM - 15)]
+
+MODEL = dict(cyc=1.04, ga=1.56, sc=3.8, pe=0.52, fix=60.0, hop=120.0, same=60.0, gi=900.0, si=100.0, dl=1800.0,
+             bw=500.0, rl=2500.0)
+STR = [(0, 512), (512, 1536), (1536, 2560)]
+SBANK = [0, 1024, 0]
+GFILL, VFILL = 3072, 3072
+PLAN = {0: ('vaaaaaaaaaaa', (0, 7, 9, 10)), 1: ('vvaaavavaaaa', (7, 11)), 2: ('vaaavaaaaaaa', (6, 11)), 3: ('vvvvvvaaavaa', (2, 8)),
+        4: ('vaaa', (0, 1)), 5: ('vvvvv', ()), 6: ('vvvvaaaaaaaa', (1, 2, 3, 4, 5, 6, 7, 8, 9, 10)), 7: ('vvavvv', ())}
+LAST = [(0, 0), (0, 1), (1, 0), (2, 0), (1, 1), (2, 1), (0, 2), (1, 2), (2, 2), (1, 3), (2, 3), (0, 3)]
+BUMP = {'xn': 20000.0, 'L3': -10000.0, 'pair': -6000.0, 'y': 12500.0, 'wrap': 11500.0, 'add': 2500.0, 'rot': 2500.0, 'good': 2500.0,
+        '': -1000.0, 'L2': 14000.0, 'fill': -2500.0, 's': 500.0, 'sadd': 1500.0, 'sa': 1500.0, 'sq': 3000.0, 'sc': 2000.0,
+        'flat': -3000.0, 'gv': -1500.0, 'xo': -500.0, 'ss': -2000.0, 'sg': -1000.0, 'scatter': -1000.0, 'fe': -500.0, 'ga': -4000.0,
+        'L1': -3500.0, 'relisted': -500.0, 'fq': 500.0}
+
+
+def cost(o, M):
+    k, n = o["c"]
+    c = M["cyc"]
+    if k == "n":
+        return M["fix"] + max(64.0, n) * c
+    if k == "ga":
+        return M["fix"] + n * M["ga"] * c
+    if k == "sc":
+        return M["fix"] + n * M["sc"] * c
+    if k == "pe":
+        return n * M["pe"]
+    if k == "gc":
+        return 170.0 + 2 * n * c
+    if k == "dma":
+        return M["gi"] if o["e"] == "g" else M["si"]
+    if k == "rem":
+        return M["gi"]
+    return 0.0
+
+
+def finish(o, t, M, st):
+    k, n = o["c"]
+    if k == "dma":
+        st[0] = max(st[0], t + M["dl"] * 0.7) + n / M["bw"]
+        return st[0] + M["dl"] * 0.3
+    if k == "arr":
+        return t + M["rl"] * 0.5
+    if k == "rem":
+        return t + M["rl"] * 0.8
+    return t
+
+
+def delay(d, o, M):
+    if d["e"] == o["e"] and d["c"][0] not in ("dma", "rem"):
+        return 0.0 if (d["e"] == "p" or d["i"] not in o["raw"]) else M["same"]
+    return M["hop"]
+
+
+def schedule(ops, M, bump=None):
+    n = len(ops)
+    pr = [0.0] * n
+    succ = [[] for _ in ops]
+    for o in ops:
+        for j in o["dep"]:
+            succ[j].append(o["i"])
+    for o in reversed(ops):
+        own = cost(o, M)
+        own = finish(o, own, M, [0.0])
+        pr[o["i"]] = own + max([pr[j] + delay(o, ops[j], M) for j in succ[o["i"]]] + [0.0])
+    pr = [p + o.get("bump", 0.0) + (bump or {}).get(o["tag"].split(" ")[0], 0.0) for p, o in zip(pr, ops)]
+    left = [len(o["dep"]) for o in ops]
+    rdy = [o.get("rel", 0.0) for o in ops]
+    free = {}
+    pool = {}
+    for o in ops:
+        free[o["e"]] = 0.0
+        pool.setdefault(o["e"], [])
+        if not o["dep"]:
+            pool[o["e"]].append(o["i"])
+    order = []
+    st = [0.0]
+    end = 0.0
+    while len(order) < n:
+        best = None
+        for e, lst in pool.items():
+            if not lst:
+                continue
+            t = max(free[e], min(rdy[i] for i in lst))
+            if best is None or t < best[0]:
+                best = (t, e)
+        t, e = best
+        i = max((j for j in pool[e] if rdy[j] <= t + M.get("look", 0.0)), key=lambda j: (pr[j], -j))
+        t = max(t, rdy[i])
+        pool[e].remove(i)
+        o = ops[i]
+        t1 = t + cost(o, M)
+        if e != "x":
+            free[e] = t1
+        t2 = finish(o, t1, M, st)
+        end = max(end, t2)
+        order.append(i)
+        for j in succ[i]:
+            rdy[j] = max(rdy[j], t2 + delay(o, ops[j], M))
+            left[j] -= 1
+            if left[j] == 0:
+                pool[ops[j]["e"]].append(j)
+    return order, end
+
+
+def replay(ops, order, M):
+    free = {}
+    done = {}
+    busy = {}
+    st = [0.0]
+    for i in order:
+        o = ops[i]
+        t = max([free.get(o["e"], 0.0) if o["e"] != "x" else o.get("rel", 0.0)] + [done[j] + delay(ops[j], o, M) for j in o["dep"]])
+        c = cost(o, M)
+        free[o["e"]] = t + c
+        busy[o["e"]] = busy.get(o["e"], 0.0) + c
+        done[i] = finish(o, t + c, M, st)
+    return done, busy
+
+
+def build(g, core, T, topo, plan):
+    rank = T.rank_of(core)
+    cores = list(T.cores)
+    nr = len(cores)
+    ops = []
+    book = {}
+    grids = {}
+    ring = [0, 0]
+
+    def V(name, *idx):
+        shp = SCRATCH[name][1][1:]
+        if name not in grids:
+            grids[name] = np.arange(int(np.prod(shp))).reshape(shp)
+        el = grids[name][idx].reshape(-1) if idx else grids[name].reshape(-1)
+        lo, hi = int(el.min()), int(el.max()) + 1
+        st = None if hi - lo == len(el) else frozenset(el.tolist())
+        if name == "ps":
+            lo, hi, st = lo // 512 * 512, (hi + 511) // 512 * 512, None
+        return dict(ap=T[name][(slice(None),) + idx], reg=[(name, lo, hi, st)], n=len(el), two=SCRATCH[name][2] in (F16, B16, U16),
+                    ps=name == "ps", ind=None)
+
+    def C(name, a, b, s=None):
+        return V(name, slice(a, b, s))
+
+    def IND(name, a, b, off):
+        w = C(name, a, b)
+        return dict(ap=w["ap"].indirect(off["ap"]), reg=w["reg"], n=16 * off["n"], two=False, ps=False, ind=off["reg"])
+
+    def op(e, fn, rd, wr, c, acc=None, tag=""):
+        i = len(ops)
+        dep, raw = set(), set()
+        acts = []
+        for v in rd:
+            acts += [(r, False) for r in v["reg"]] + [(r, False) for r in (v["ind"] or [])]
+        for v in wr:
+            acts += [(r, True) for r in v["reg"]] + [(r, False) for r in (v["ind"] or [])]
+        new = []
+        for (name, lo, hi, st), w in acts:
+            keep = []
+            for ent in book.get(name, []):
+                l2, h2, s2, j, w2, e2, a2 = ent
+                hit = l2 < hi and lo < h2
+                if hit and st is not None and s2 is not None:
+                    hit = not st.isdisjoint(s2)
+                elif hit and st is not None and h2 - l2 < 600:
+                    hit = any(l2 <= u < h2 for u in st)
+                elif hit and s2 is not None and hi - lo < 600:
+                    hit = any(lo <= u < hi for u in s2)
+                if hit and (w or w2 or (name == "ps" and e != e2)) and not (acc is not None and a2 == acc):
+                    dep.add(j)
+                    if w2:
+                        raw.add(j)
+                if w and acc is None and ((st is None and lo <= l2 and h2 <= hi) or (st is not None and s2 is not None and s2 <= st)):
+                    continue
+                keep.append(ent)
+            book[name] = keep
+            new.append((name, (lo, hi, st, i, w, e, acc)))
+        for name, ent in new:
+            book.setdefault(name, []).append(ent)
+        ops.append(dict(i=i, e=e, fn=fn, dep=dep, raw=raw, c=c, acc=acc, tag=tag, stop=[True]))
+        return ops[-1]
+
+    def aps(x):
+        return x["ap"] if isinstance(x, dict) else x
+
+    def sc_rd(*xs):
+        return [x for x in xs if isinstance(x, dict)]
+
+    def kind(out, ins, full):
+        if out["ind"] is not None:
+            return ("sc", ins[0]["n"])
+        if ins[0]["ind"] is not None:
+            return ("ga", out["n"])
+        return ("n", out["n"] * full)
+
+    def ts(out, in0, s1, s2, o0, o1=None, tag=""):
+        def fn():
+            if o1 is None:
+                return g.vector.tensor_scalar(out["ap"], in0["ap"], aps(s1), None, o0)
+            return g.vector.tensor_scalar(out["ap"], in0["ap"], aps(s1), aps(s2), o0, o1)
+        return op("v", fn, [in0] + sc_rd(s1, s2), [out], kind(out, [in0], 0.5 if out["two"] and in0["two"] else 1.0), tag=tag)
+
+    def tt(out, in0, in1, o, tag=""):
+        return op("v", lambda: g.vector.tensor_tensor(out["ap"], in0["ap"], in1["ap"], o), [in0, in1], [out],
+                  kind(out, [in0], 1.0 if in0["ps"] or in1["ps"] else 2.0), tag=tag)
+
+    def cp(out, in0, tag=""):
+        return op("v", lambda: g.vector.tensor_copy(out["ap"], in0["ap"]), [in0], [out],
+                  kind(out, [in0], 0.5 if out["two"] and in0["two"] else 1.0), tag=tag)
+
+    def ms(out, val):
+        return op("v", lambda: g.vector.memset(out["ap"], val), [], [out], ("n", out["n"] * (0.5 if out["two"] else 1.0)))
+
+    def act(out, in0, f, bias=0.0, scale=1.0, tag=""):
+        return op("a", lambda: g.scalar.activation(out["ap"], in0["ap"], f, bias=bias, scale=scale), [in0], [out],
+                  kind(out, [in0], 1.0), tag=tag)
+
+    def lin(site, out, in0, scale, bias, tag=""):
+        if plan[7][0][site] == "a":
+            return act(out, in0, F.Identity, bias=bias, scale=scale, tag=tag)
+        return ts(out, in0, scale, bias, A.mult, A.add, tag=tag)
+
+    def mm(trip, start=True, acc=None, wide=1, tag=""):
+        o = {}
+
+        def fn():
+            r = None
+            for k, (out, l, rhs) in enumerate(trip):
+                r = g.tensor.matmul(out["ap"], l["ap"], rhs["ap"], start and k == 0, o["op"]["stop"][0] and k == len(trip) - 1)
+            return r
+        rd = [t[1] for t in trip] + [t[2] for t in trip]
+        o["op"] = op("p", fn, rd, [trip[0][0]], ("pe", sum(max(64, t[2]["n"]) * wide for t in trip)), acc=acc, tag=tag)
+        return o["op"]
+
+    def raw(ap, n=0, reg=()):
+        return dict(ap=ap, reg=list(reg), n=n, two=False, ps=False, ind=None)
+
+    def dma(e, out, in0, nbytes, add=False, grp=None, tag=""):
+        q = {"g": g, "s": g.sync, "a": g.scalar}[e]
+
+        def fn():
+            if add:
+                return q.dma_start(out["ap"], in0["ap"], accum_op=A.add)
+            return q.dma_start(out["ap"], in0["ap"])
+        o = op(e, fn, [in0] + ([out] if add else []), [out], ("dma", nbytes * (2 if add else 1)), acc=grp, tag=tag)
+        o["grp"] = grp
+        return o
+
+    def send(j, src0, src1, dname, guard, arrive):
+        def fn(lsem):
+            tr = []
+            for b, src in enumerate((src0, src1)):
+                dst = cores[(rank + DSH[b]) % nr]
+                en = topo.engines(core, dst)
+                h = len(en) // 2
+                rid, pid, _ = topo.addr(dst)
+                tr.append(RemoteDMATransfer(dst_ids=[DstId(rid=rid, pnc=pid)], dma_engine_mask=sum(1 << u for u in en[b * h:(b + 1) * h]),
+                                            remote_sem=T.sem["arr%d" % j], src=src["ap"],
+                                            dst=C(dname, NV + b * GH, NV + (b + 1) * GH)["ap"]))
+            g.remote_dma_fused(tr, local_sem=lsem)
+        cnt = sum(len(topo.engines(core, cores[(rank + d) % nr])) // 2 for d in DSH)
+        got = sum(len(topo.engines(cores[(rank - d) % nr], core)) // 2 for d in DSH)
+        o = op("g", fn, [src0, src1], guard, ("rem", 0), tag="send%d" % j)
+        o["cnt"] = cnt
+        a = op("x", None, [], [arrive], ("arr", 0), tag="arr%d" % j)
+        a["dep"].add(o["i"])
+        a["sem"] = ("arr%d" % j, got)
+        a["after"] = o["i"]
+
+    def wrap(out, src, n, mat="es"):
+        return mm([(out, C(mat, 128 * m, 128 * (m + 1)), C(src, m, 16 * n, 16)) for m in range(16)], tag="wrap")
+
+    W = ["w0", "w1", "w2", "w3"]
+    XN = ["xn0", "xn1"]
+    OF = ["of0", "of1"]
+
+    dma("s", C("w0", 0, GH), raw(T.x[:, 0:GH]), 128 * 1024)
+    dma("a", raw(T.rs0[0:112, :], reg=V("rs0")["reg"]), raw(T.x[16:128, 0:GH]), 112 * 1024, grp="rs")
+    dma("s", raw(T.rs0[112:128, :], reg=V("rs0")["reg"]), raw(T.x[0:16, 0:GH]), 16 * 1024, grp="rs")
+    send(0, C("w0", 0, GH), V("rs0"), "w0", [], C("w0", NV, NW))
+    ops[-1]["rel"] = 7000.0
+    for o in ops:
+        o["bump"] = 1e5
+    dma("s", C("w0", GH, NV), raw(T.x[:, GH:NV]), 128 * 4 * (NV - GH))
+    dma("a", V("n32"), raw(T.nb[:]), 128 * 2560)
+    cp(V("of0"), V("n32"))
+    for si, (a0, a1) in enumerate(STR):
+        if "v" in plan[6][0][4 * si:4 * si + 4]:
+            dma("a" if si == 0 else "s", C("w2", a0, a1), raw(T.x[:, a0:a1]), 128 * 4 * (a1 - a0))
+    for o in ops:
+        o["bump"] = o.get("bump", 0.0) + 1e5
+    for k, nm in enumerate(("lb", "pj", "pk", "pl", "hq")):
+        dma("s", C("li", 24 * k, 24 * (k + 1)), raw(T[nm][:]), 128 * 96, grp="li")
+    op("g", lambda: g.iota(T.fl[:, FLW - GFILL:FLW], [[0, GFILL]], 0, 0), [C("w0", 0, GH), V("rs0")],
+       [C("fl", FLW - GFILL, FLW)], ("gc", GFILL), tag="fill")
+    top = FLW - GFILL - VFILL
+    ms(C("fl", top, top + VFILL), 0)["bump"] = 5e4
+    for h in range(0, top, NV):
+        n = min(NV, top - h)
+        dma("s", C("fl", h, h + n), raw(T.x[:, 0:n]), 512 * n, grp="fl", tag="fill")["rel"] = 700.0
+    dma("s", raw(T.fl[0:127:18, 0:4 * NV], reg=C("fl", 0, 4 * NV)["reg"]), raw(T.nb[:]), 600000, tag="flat")
+    ms(V("onef"), 1.0)["bump"] = 1e5
+    op("g", lambda: g.affine_select(T.idf[:], T.onef[:], [[-1, 128]], A.is_equal, 0.0, 0, 1), [V("onef")], [V("idf")], ("gc", 128))
+    op("g", lambda: g.affine_select(T.bof[:], T.onef[:], [[-16, 8], [0, 16]], A.is_ge, 0.0, 0, 1), [V("onef")], [V("bof")], ("gc", 128))
+    op("g", lambda: g.affine_select(T.bof[:], T.bof[:], [[16, 8], [0, 16]], A.is_ge, 0.0, 15, -1), [V("bof")], [V("bof")], ("gc", 128))
+    op("g", lambda: g.iota(T.iw[:, 0:192], [[1, 192]], 0, 0, allow_small_or_imprecise_dtypes=True), [], [C("iw", 0, 192)], ("gc", 192))
+    op("g", lambda: g.iota(T.dum[:], [[16, 32]], DUM0, 1, allow_small_or_imprecise_dtypes=True), [], [V("dum")], ("gc", 32))
+    op("g", lambda: g.iota(T.i8[:], [[16, 8]], 0, 1), [], [V("i8")], ("gc", 8))
+    for k in range(4):
+        h = 192 << k
+        act(C("iw", h, 2 * h), C("iw", 0, h), F.Identity, bias=float(h))
+    for nm, val in (("i16", 1.0 / 16), ("im64", -64.0), ("im1", -1.0), ("i1", 1.0), ("imk", -1024.0), ("id2", 2.0), ("idm2", -2.0)):
+        act(V(nm), V("idf"), F.Identity, scale=val)
+    act(C("rot", 0, 112), C("idf", 16, 128), F.Identity, scale=-1.0)
+    act(C("rot", 112, 128), C("idf", 0, 16), F.Identity, scale=-1.0)
+    act(V("cb"), V("onef"), F.Identity, scale=-7.5 / 16)
+    ms(V("ones"), 1.0)
+    act(V("bo"), V("bof"), F.Identity)
+    ms(V("em"), 0.0)
+    for m in range(16):
+        act(C("em", 129 * m, 128 * (m + 1), 16), C("bof", m, 128, 16), F.Identity, scale=1.0 / 16)
+    op("g", lambda: g.affine_select(T.sef[:], T.onef[:], [[-18, 8], [0, 16]], A.is_equal, 0.0, 0, 1), [V("onef")], [V("sef")], ("gc", 128))
+    ms(V("es"), 0.0)
+    for m in range(16):
+        act(C("es", 129 * m, 128 * (m + 1), 16), C("sef", m, 128, 16), F.Identity)
+    ts(V("pg"), C("i8", 0, 1), 112, None, A.bitwise_and)
+    cp(V("pgf"), V("pg"))
+    ts(V("lnf"), V("i8"), V("pgf"), None, A.subtract)
+    act(V("wc"), V("lnf"), F.Exp, bias=69.85, scale=-1.1)
+    act(V("thr"), C("iw", 0, 128), F.Exp, bias=69.85 + math.log(6.5), scale=-1.1)
+    for p in range(4):
+        ms(C("wt", 16 * p, 16 * (p + 1)), (4 - p) / 4.0)
+    ms(V("zz"), 0.0)
+    LB = C("li", 0, 24)
+    ts(V("hb"), LB, -7.5, 1.0 / 16, A.add, A.mult)
+    ts(V("tb"), V("hb"), -10239.0, None, A.mult)
+    ts(V("ub"), LB, 640.0, None, A.mult)
+    tt(V("bb"), V("tb"), V("ub"), A.add)
+    ts(V("p160"), C("li", 24, 96), 160.0, None, A.mult)
+    tt(C("ib", 0, 24), V("bb"), C("p160", 24, 48), A.add)
+    tt(C("ib", 24, 48), V("bb"), C("p160", 0, 24), A.add)
+    cp(V("ibu"), V("ib"))
+    ts(V("hq16"), C("li", 96, 120), 1.0 / 16, None, A.mult)
+    for si, (a0, a1) in enumerate(STR):
+        if si == 0:
+            ts(C("xn0", a0, a1), C("w0", a0, a1), -1.0, 2048.0, A.mult, A.add)
+        else:
+            act(C("xn0", a0, a1), C("w0", a0, a1), F.Identity, bias=2048.0, scale=-1.0)
+
+    def marks():
+        dma("s", C("aw", 0, NV), raw(T.am[:]), 128 * 2 * NV)["rel"] = 40000.0
+        dma("s", raw(T.ra[0:112, :], reg=V("ra")["reg"]), raw(T.am[16:128, 0:GH]), 112 * 512, grp="ra")["rel"] = 40000.0
+        dma("s", raw(T.ra[112:128, :], reg=V("ra")["reg"]), raw(T.am[0:16, 0:GH]), 16 * 512, grp="ra")["rel"] = 40000.0
+        send(10, C("aw", 0, GH), V("ra"), "aw", [], C("aw", NV, NW))
+
+    def piece(k, of, si, p, kindk):
+        a0, a1 = STR[si]
+        who, sg = plan[kindk]
+        win = IND(W[k % 4], 0, NW, C(of, (p * NV + a0) // 16, (p * NV + a1) // 16))
+        d, s = C("d1", p * NV + a0, p * NV + a1), C("d2", p * NV + a0, p * NV + a1)
+        tag = "k%d s%d p%d" % (k, si, p)
+        if who[4 * si + p] == "v":
+            if k == 0:
+                tt(d, win, C("w2", a0, a1), A.subtract, tag="gv " + tag)
+            else:
+                tt(d, win, C(XN[k % 2], a0, a1), A.add, tag="gv " + tag)
+        else:
+            act(d, win, F.Identity, bias=-2048.0 if k == 0 else 0.0, tag="ga " + tag)
+            dma("g", d, C(XN[k % 2], a0, a1), 256 * (a1 - a0), add=True, tag="add " + tag)
+        if 4 * si + p in sg:
+            ring[0] += 1
+            h = 1024 * (ring[0] % 2)
+            ts(C("d3", h, h + a1 - a0), d, -2047.0, 2047.0, A.max, A.min, tag="c " + tag)
+            act(s, d, F.Sign, tag="s " + tag)
+            return ("d3", h - a0), ("d2", p * NV)
+        ts(s, d, -1.0, 1.0, A.max, A.min, tag="s " + tag)
+        ts(d, d, -2047.0, 2047.0, A.max, A.min, tag="c " + tag)
+        return ("d1", p * NV), ("d2", p * NV)
+
+    def sweep(k, of):
+        wn, xn, xo = W[(k + 1) % 4], XN[(k + 1) % 2], XN[k % 2]
+        for si, (a0, a1) in enumerate(STR):
+            blocks = [(b, min(b + 512, a1)) for b in range(a0, a1, 512)]
+            bank = [C("ps", SBANK[si] + b0 - a0, SBANK[si] + b1 - a0) for b0, b1 in blocks]
+            for (b0, b1), ps in zip(blocks, bank):
+                o = mm([(ps, V("im1"), C(xo, b0, b1)),
+                        (ps, raw(T.cb[0:1, :], reg=V("cb")["reg"]), raw(T.ones[0:1, 0:b1 - b0], n=b1 - b0, reg=V("ones")["reg"]))])
+                o["stop"][0] = False
+            for p in range(4):
+                cn, sn = piece(k, of, si, p, k % 3 if k else 6)
+                for (b0, b1), ps in zip(blocks, bank):
+                    mm([(ps, V("im64"), C(sn[0], sn[1] + b0, sn[1] + b1))], start=False, acc=(k, b0))
+                    mm([(ps, V("i16"), C(cn[0], cn[1] + b0, cn[1] + b1))], start=False, acc=(k, b0))
+            ts(C(wn, a0, a1), C("ps", SBANK[si], SBANK[si] + a1 - a0), -2048.0, 2047.0, A.max, A.min, tag="fin k%d b%d" % (k, a0))
+            act(C(xn, a0, a1), C(wn, a0, a1), F.Identity, scale=-1.0, tag="xn k%d b%d" % (k, a0))
+            if a0 == 0:
+                mm([(C("ps", 0, GH), V("rot"), C(xn, 0, GH))])
+                rs = "rs%d" % ((k + 1) % 2)
+                cp(V(rs), C("ps", 0, GH), tag="rot")
+                send(k + 1, C(wn, 0, GH), V(rs), wn, [C(W[(k + 2) % 4], NV, NW)], C(wn, NV, NW))
+
+    def relist(of):
+        dma("s", V("n32"), raw(T.fl[0:127:18, 0:4 * NV], reg=C("fl", 0, 4 * NV)["reg"]), 500000, tag="relist")
+        cp(V(of), V("n32"), tag="relisted")
+
+    def put(lose, src):
+        for r in range(4):
+            tt(C("o1", r, 32, 4), src[r], lose, A.max)
+        tt(V("o2"), V("o1"), V("dum"), A.min)
+        cp(V("ou"), V("o2"))
+        cp(IND("fl", 0, FLW, V("ou")), V("rw"), tag="scatter")
+
+    def lanes(t, of):
+        c0 = 8 * t
+        B4, B5 = 2048, 2560
+        act(C("r1", 0, 128), IND("fl", 0, FLW, C("ibu", c0, c0 + 8)), F.Identity, bias=-1024.0, tag="L1")
+        act(C("r1", 128, 256), IND("fl", 0, FLW, C("ibu", 24 + c0, 32 + c0)), F.Identity, bias=-1024.0)
+        wrap(C("ps", B4, B4 + 16), "r1", 16)
+        pa_, pc_, pac = C("ps", B4, B4 + 8), C("ps", B4 + 8, B4 + 16), C("ps", B4, B4 + 16)
+        ts(V("hi"), pac, 1016.5, 1.0 / 16, A.add, A.mult)
+        ts(V("uu"), pac, 640.0, 655360.0, A.mult, A.add)
+        ts(V("tt"), V("hi"), -10239.0, None, A.mult)
+        tt(V("vv"), C("uu", 8, 16), C("p160", 48 + c0, 56 + c0), A.add)
+        tt(V("ic"), C("tt", 8, 16), V("vv"), A.add)
+        cp(V("icu"), V("ic"))
+        lin(0, C("wh", 0, 32, 4), pa_, 1.0, 1024.0)
+        lin(0, C("wh", 3, 32, 4), pc_, 1.0, 1024.0)
+        lin(1, C("wh", 1, 32, 4), C("li", c0, c0 + 8), 1.0, 0.0)
+        lin(2, V("yy", 0, slice(1, 16, 2)), C("wh", 3, 32, 4), 1.0, -1024.0)
+        lin(2, V("yy", 0, slice(16, 32, 2)), C("wh", 3, 32, 4), 1.0, -1024.0)
+        lin(2, V("yy", 0, slice(0, 16, 2)), C("li", c0, c0 + 8), 1.0, -1024.0)
+        lin(2, V("yy", 0, slice(17, 32, 2)), C("li", c0, c0 + 8), 1.0, -1024.0)
+        lin(2, V("yy", 1), V("yy", 0), 1.0, 0.0)
+        lin(2, V("yy", slice(2, 4)), V("yy", slice(0, 2)), 1.0, 0.0)
+        tt(C("bad", 0, 16, 2), C("tt", 0, 8), C("uu", 0, 8), A.add)
+        tt(V("bc"), C("tt", 8, 16), C("uu", 8, 16), A.add)
+        cp(C("lbc", 1, 16, 2), V("bc"))
+        cp(C("lbc", 0, 16, 2), C("bb", c0, c0 + 8))
+        act(V("r2"), IND("fl", 0, FLW, V("icu")), F.Identity, bias=-1024.0, tag="L2")
+        pd_ = C("ps", B5, B5 + 8)
+        wrap(pd_, "r2", 8)
+        ts(V("h2"), pd_, 1016.5, 1.0 / 16, A.add, A.mult)
+        ts(V("u2"), pd_, 640.0, 655360.0, A.mult, A.add)
+        ts(V("t2"), V("h2"), -10239.0, None, A.mult)
+        tt(C("bad", 1, 16, 2), V("t2"), V("u2"), A.add)
+        cp(V("lad"), V("bad"))
+        lin(3, C("wh", 2, 32, 4), pd_, 1.0, 1024.0)
+        cp(V("whu"), V("wh"))
+        cp(V("rw"), IND("iw", 0, NW, V("whu")))
+        WA, WB, WD, WC = [C("wh", r, 32, 4) for r in range(4)]
+        tt(V("zz", 0, slice(32, 48, 2)), WA, WC, A.is_equal)
+        tt(V("zz", 1, slice(32, 48, 2)), WB, WD, A.is_equal)
+        tt(V("zz", 2, slice(32, 48, 2)), WC, WD, A.is_equal)
+        for r, u in enumerate((WA, WC, WD)):
+            ts(V("zz", r, slice(33, 48, 2)), u, float(NV), None, A.is_ge)
+        for p in range(4):
+            act(C("r3", 256 * p, 256 * (p + 1)), IND("fl", 160 * p, FLW, V("lad")), F.Identity, bias=-1024.0, tag="L3")
+        for p in range(4):
+            act(C("r4", 256 * p, 256 * (p + 1)), IND("fl", 160 * p, FLW, V("lbc")), F.Identity, bias=-1024.0)
+        pn = C("ps", B4, B4 + 64)
+        wrap(pn, "r3", 64)
+        tt(V("z1"), pn, V("yy", slice(None), slice(0, 16)), A.is_equal)
+        tt(V("zz", slice(None), slice(16, 32)), pn, V("yy", slice(None), slice(16, 32)), A.is_equal)
+        ts(C("sl", 0, 128, 2), pn, 1024.0, None, A.add)
+        tt(V("zz", slice(None), slice(0, 16)), V("z1"), V("wt"), A.mult)
+        tt(V("z2"), V("zz", slice(0, 2)), V("zz", slice(2, 4)), A.max)
+        tt(V("z3"), V("z2", 0), V("z2", 1), A.max)
+        tt(V("z4"), C("z3", 16, 32), C("z3", 32, 48), A.max)
+        tt(V("z5"), C("z3", 0, 16), V("z4"), A.is_gt)
+        tt(V("gd"), C("z5", 0, 16, 2), C("z5", 1, 16, 2), A.mult)
+        tt(V("ww"), V("gd"), V("wc"), A.mult, tag="good")
+        lin(4, V("ng"), V("gd"), -BIG, BIG)
+        lin(4, V("pa"), C("z3", 0, 16), -640.0, 640.0)
+        tt(V("iad"), V("pa"), V("bad"), A.add)
+        n = 0
+        for c in (0, 7, 6, 5, 4, 3, 2, 1, 0):
+            rs = (0,) if (c == 0 and n == 0) else ((1, 2, 3) if c == 0 else (0, 1, 2, 3))
+            for r in rs:
+                q = "q%d" % (n % 3)
+                ts(V(q, slice(c, 8)), C("rw", 64 * c, 512), C("wh", 4 * c + r, 4 * c + r + 1), C("ww", c, c + 1), A.is_equal, A.mult, tag="pair")
+                o = mm([(C("ps", B5 + 16 * c, B5 + 128), V("bo"), V(q, slice(c, 8), u)) for u in range(4)], start=n == 0)
+                o["stop"][0] = n == 31
+                n += 1
+        tt(V("lz"), C("ps", B5, B5 + 128), V("thr"), A.is_ge)
+        pl_ = C("ps", B4, B4 + 8)
+        wrap(pl_, "lz", 8)
+        lin(5, V("lb1"), pl_, BIG, 0.0)
+        tt(V("lb2"), V("lb1"), V("ng"), A.max)
+        iA, iD, iB, iC = C("iad", 0, 16, 2), C("iad", 1, 16, 2), C("ib", c0, c0 + 8), V("ic")
+        put(V("lb2"), [iC, iD, iB, iA])
+        relist(of)
+        pm = C("ps", B5, B5 + 64)
+        wrap(pm, "r4", 64)
+        ts(C("sl", 1, 128, 2), pm, 1024.0, None, A.add)
+        cp(C("sl", 129, 160), C("whu", 0, 31))
+        cp(C("sl", 128, 160, 4), C("whu", 3, 32, 4))
+        return [iB, iA, iC, iD]
+
+    def stress(k, last):
+        w = W[k % 4]
+        B5 = 2560
+        off = 2048.0 if k == 0 else 0.0
+        act(V("xo"), IND(w, 0, NW, V("whu")), F.Identity, bias=off, scale=-1.0, tag="xo")
+        tot = C("ps", B5, B5 + 128)
+        calls = ([4] if last else []) + [0, 1, 2, 3]
+        who, sg = plan[5 if last else 4]
+        for n, p in enumerate(calls):
+            ring[1] = (ring[1] + 512) % 1536
+            d, s = C("sd", ring[1], ring[1] + 512), C("ss", ring[1], ring[1] + 512)
+            win = IND(w, 0, NW, C("sl", 32 * p, 32 * (p + 1)))
+            if who[n] == "v" and k:
+                tt(d, win, V("xo"), A.add, tag="sg")
+            else:
+                act(d, win, F.Identity, bias=-off, tag="sa")
+                dma("g", d, V("xo"), 256 * 512, add=True, tag="sadd")
+            if n not in sg:
+                ts(s, d, -1.0, 1.0, A.max, A.min, tag="ss")
+                ts(d, d, -2047.0, 2047.0, A.max, A.min, tag="sc")
+            else:
+                ts(s, d, -2047.0, 2047.0, A.max, A.min, tag="sc")
+                act(d, d, F.Sign, tag="ss")
+                d, s = s, d
+            u = C("ps", 3072 + 512 * (n % 2), 3584 + 512 * (n % 2))
+            mm([(u, V("imk"), s), (u, V("i1"), d)])
+            sq = "sq%d" % (n % 2)
+            act(V(sq), u, F.Square, tag="sq")
+            wts = [(1, "idm2"), (3, "idm2"), (0, "id2"), (2, "id2")] if p == 4 else [(r, "idf") for r in range(4)]
+            o = mm([(tot, V(m), V(sq, slice(None), r)) for r, m in wts], start=n == 0, wide=4)
+            o["stop"][0] = n == len(calls) - 1
+        return tot
+
+    def votes(t, tot, old, of):
+        tt(V("lz"), tot, V("f1"), A.is_gt, tag="vote")
+        pv = C("ps", 2048, 2056)
+        wrap(pv, "lz", 8, "em")
+        tt(V("lb3"), pv, C("hq16", 8 * t, 8 * t + 8), A.is_lt)
+        ts(V("lb4"), V("lb3"), BIG, None, A.mult)
+        tt(V("lb3"), V("lb4"), V("lb2"), A.max)
+        put(V("lb3"), old)
+        relist(of)
+
+    def last(k, of):
+        n = 0
+        nb = 0
+        for si, p in LAST:
+            a0, a1 = STR[si]
+            if True:
+                cn, sn = piece(k, of, si, p, 3)
+                e, tn = "e%d" % (n % 3), ("t0", "t1", "t3")[n % 3]
+                nb = 1024 * (n % 4)
+                for b0 in range(a0, a1, 512):
+                    u = C("ps", nb + b0 - a0, nb + b0 - a0 + 512)
+                    mm([(u, V("imk"), C(sn[0], sn[1] + b0, sn[1] + b0 + 512)), (u, V("i1"), C(cn[0], cn[1] + b0, cn[1] + b0 + 512))])
+                ev, tv = C(e, 0, a1 - a0), C(tn, 0, a1 - a0)
+                act(ev, C("ps", nb, nb + a1 - a0), F.Square, tag="fq")
+                act(ev, ev, F.Exp, scale=-2.0 ** -19, tag="fe")
+                tt(tv, IND("aw", 0, NW, C(of, (p * NV + a0) // 16, (p * NV + a1) // 16)), ev, A.mult, tag="mk s%d p%d" % (si, p))
+                yv = raw(T.y[:, a0:a1], reg=[("y", a0, a1, None)])
+                dma("g" if p else "s", yv, tv, 512 * (a1 - a0), add=p > 0, tag="y")
+                n += 1
+
+    for t in range(RO):
+        k = 3 * t
+        sweep(k, OF[0])
+        if t == 0:
+            marks()
+        old = lanes(t, OF[1])
+        sweep(k + 1, OF[1])
+        tot = stress(k, False)
+        act(V("f1"), tot, F.Identity)
+        tot = stress(k + 2, True)
+        sweep(k + 2, OF[1])
+        votes(t, tot, old, OF[0])
+    last(3 * RO, OF[0])
+    return ops
+
+
+def emit(g, T, ops, order):
+    Q = {"g": g, "v": g.vector, "a": g.scalar, "p": g.tensor, "s": g.sync}
+    lastacc = {}
+    for i in order:
+        o = ops[i]
+        if o["e"] == "p" and o["acc"] is not None:
+            o["stop"][0] = False
+            lastacc[o["acc"]] = o
+    for o in lastacc.values():
+        o["stop"][0] = True
+    mark, seq, grp, total = {}, {}, {}, {}
+    nsem = [0]
+    for i in order:
+        o = ops[i]
+        k = o["c"][0]
+        if k == "arr":
+            mark[i] = o["sem"]
+            total[o["sem"][0]] = o["sem"][1]
+        elif k in ("dma", "rem"):
+            key = o.get("grp") or ("own", i)
+            if key not in grp:
+                grp[key] = "m%d" % nsem[0]
+                nsem[0] += 1
+            total[grp[key]] = total.get(grp[key], 0) + (16 if k == "dma" else o["cnt"])
+            mark[i] = (grp[key], None)
+        else:
+            seq[o["e"]] = seq.get(o["e"], 0) + 1
+            mark[i] = ("q" + o["e"], seq[o["e"]])
+    for i in order:
+        if mark[i][1] is None:
+            mark[i] = (mark[i][0], total[mark[i][0]])
+    known = {e: {} for e in Q}
+    clock = {}
+    waits = {}
+    need = set()
+    for i in order:
+        o = ops[i]
+        e = o["e"]
+        if e == "x":
+            clock[i] = {mark[i][0]: mark[i][1]}
+            continue
+        kn = known[e]
+        ws = {}
+        for j in sorted(o["dep"], key=lambda u: -mark[u][1] if mark[u][0][0] == "q" else 0):
+            s, c = mark[j]
+            if s == "q" + e and o["c"][0] not in ("dma", "rem") and (e == "p" or j not in o["raw"]):
+                continue
+            if kn.get(s, 0) >= c:
+                continue
+            ws[s] = max(ws.get(s, 0), c)
+            for s2, c2 in clock[j].items():
+                if kn.get(s2, 0) < c2:
+                    kn[s2] = c2
+        waits[i] = ws
+        for s, c in ws.items():
+            if s[0] == "q":
+                need.add((s, c))
+        clock[i] = dict(kn)
+        clock[i][mark[i][0]] = max(clock[i].get(mark[i][0], 0), mark[i][1])
+    count = {}
+    for s in ("qv", "qa", "qp", "qg"):
+        pl = sorted(c for s2, c in need if s2 == s)
+        for n, c in enumerate(pl):
+            count[(s, c)] = n + 1
+    users = {}
+    for i in order:
+        for s in waits.get(i, {}):
+            users.setdefault(s, []).append(i)
+    real, base, mine, used = {}, {}, [], 0
+    for i in order:
+        o = ops[i]
+        s = mark[i][0]
+        if o["c"][0] not in ("dma", "rem") or s in real:
+            continue
+        own = o["e"] == "g" and o["c"][0] == "dma"
+        for n, s0 in enumerate(mine if own else []):
+            if s0 in users and clock[i].get(s0, 0) >= total[s0] and all(clock[i].get(mark[u][0], 0) >= mark[u][1] and u != i for u in users[s0]):
+                real[s], base[s] = real[s0], base[s0] + total[s0]
+                mine.pop(n)
+                break
+        else:
+            real[s], base[s] = "m%d" % used, 0
+            used += 1
+        if own:
+            mine.append(s)
+    waited = {}
+    for i in order:
+        o = ops[i]
+        e = o["e"]
+        if e == "x":
+            continue
+        for s, c in waits[i].items():
+            Q[e].wait_ge(T.sem[real.get(s, s)], count.get((s, c), c) + base.get(s, 0))
+            waited[s] = max(waited.get(s, 0), c)
+        k = o["c"][0]
+        s = T.sem[real.get(mark[i][0], mark[i][0])]
+        if k == "rem":
+            o["fn"](s)
+        elif k == "dma":
+            o["fn"]().then_inc(s, 16)
+        else:
+            r = o["fn"]()
+            if mark[i] in count:
+                r.then_inc(s, 1)
+    for s, c in total.items():
+        if waited.get(s, 0) < c:
+            g.sync.wait_ge(T.sem[real.get(s, s)], c + base.get(s, 0))
+    return used
+
+
+ORDER = []
+
+
+def rank_program(g, core, T, topo):
+    if T.rank_of(core) is None:
+        return
+    ops = build(g, core, T, topo, PLAN)
+    if not ORDER:
+        ORDER.append(schedule(ops, MODEL, BUMP)[0])
+    emit(g, T, ops, ORDER[0])

@@ -5,54 +5,53 @@ from concourse.mybir import AluOpType as A, ActivationFunctionType as F
 
 NV, GH, NW, RO = 2560, 256, 3072, 3
 DSH = [1, 3]
-DUM0, FLW = 11008, 11648
-BIG = 20000.0
+TB, TREAL, TW = 161, 16 * 161, 3200
+CEN = 1024.0
+BIG = 8192.0
+SLOPE, TOPW = 17.625 / 16, 60.0
 I32, F32, F16, B16, U16 = "int32", "float32", "float16", "bfloat16", "uint16"
+MH = ["i1", "i16", "im64", "im1", "imk", "i161", "im527", "i4k", "l1", "l2", "l3", "lb", "lt", "luu", "lul"]
+MB = ["l4", "lpen", "lmu", "lml", "bo"]
+WH = ["xw1", "xwp", "xwm", "y2", "y3", "y6", "y10"]
 SB = {
     "w0": ([NW], I32), "w1": ([NW], I32), "w2": ([NW], I32), "w3": ([NW], I32),
-    "fl": ([FLW], I32), "iw": ([NW], F32), "aw": ([NW], B16),
-    "d1": ([4 * NV], F16), "d2": ([4 * NV], F16), "d3": ([2048], F16), "xn0": ([NV], F16), "xn1": ([NV], F16),
-    "n32": ([640], I32), "of0": ([640], U16), "of1": ([640], U16),
+    "tb": ([TW], F32), "aw": ([NW], B16),
+    "d1": ([4 * NV], F16), "d2": ([4 * NV], F16), "d3": ([4 * NV], F16), "xn0": ([NV], F16), "xn1": ([NV], F16),
+    "n32": ([664], I32), "na": ([664], F16), "nh": ([664], F16), "nf": ([4, TB], F32), "pf": ([4, TB], F32), "sf": ([2, TB], F32),
+    "of0": ([640], U16), "of1": ([640], U16),
     "rs0": ([GH], I32), "rs1": ([GH], I32), "ra": ([GH], B16),
-    "em": ([2048], F16), "onef": ([128], F32), "idf": ([128], F32), "id2": ([128], F32), "idm2": ([128], F32),
-    "bof": ([128], F32), "bo": ([128], B16), "i1": ([128], F16), "i16": ([128], F16), "im64": ([128], F16),
-    "im1": ([128], F16), "imk": ([128], F16), "rot": ([128], F16), "cb": ([128], F16), "ones": ([512], F16),
-    "thr": ([128], F32), "dum": ([32], F32), "i8": ([8], I32), "pg": ([1], I32), "pgf": ([1], F32),
-    "lnf": ([8], F32), "wc": ([8], F32), "wt": ([64], F32),
-    "li": ([120], I32), "hb": ([24], I32), "tb": ([24], F32), "ub": ([24], F32), "bb": ([24], F32),
-    "p160": ([72], F32), "ib": ([48], F32), "ibu": ([48], U16), "hq16": ([24], F32),
-    "r1": ([256], F16), "r2": ([128], F16), "r3": ([1024], F16), "r4": ([1024], F16),
-    "hi": ([16], I32), "tt": ([16], F32), "uu": ([16], F32), "vv": ([8], F32), "bc": ([8], F32),
-    "h2": ([8], I32), "t2": ([8], F32), "u2": ([8], F32),
-    "ic": ([8], F32), "icu": ([8], U16), "bad": ([16], F32), "lad": ([16], U16), "lbc": ([16], U16),
-    "wh": ([32], F32), "whu": ([32], U16), "yy": ([4, 32], F32), "z1": ([64], F32), "zz": ([4, 48], F32),
-    "z2": ([2, 48], F32), "z3": ([48], F32), "z4": ([16], F32), "z5": ([16], F32), "gd": ([8], F32),
-    "ww": ([8], F32), "ng": ([8], F32), "pa": ([16], F32), "iad": ([16], F32), "rw": ([512], U16),
-    "q0": ([8, 4, 16], B16), "q1": ([8, 4, 16], B16), "q2": ([8, 4, 16], B16),
-    "lz": ([128], F16), "lb1": ([8], F32), "lb2": ([8], F32), "lb3": ([8], F32), "lb4": ([8], F32),
-    "o1": ([32], F32), "o2": ([32], F32), "ou": ([32], U16), "sl": ([160], U16),
-    "xo": ([512], F16), "sd": ([1536], F16), "ss": ([1536], F16), "es": ([2048], F16), "sef": ([128], F32),
-    "sq0": ([8, 4, 16], F32), "sq1": ([8, 4, 16], F32), "f1": ([128], F32),
+    "mh": ([len(MH), 128], F16), "mb": ([len(MB), 128], B16), "wr": ([len(WH), 144], F16), "y2b": ([144], B16),
+    "onef": ([128], F32), "idf": ([128], F32), "id2": ([128], F32), "bof": ([128], F32), "cb": ([128], F16), "ones": ([512], F16),
+    "cf": ([TB], F32), "ki": ([2], I32), "kf": ([2], F32), "p16": ([16], F32), "r4": ([4], F32), "col": ([16], F32),
+    "tri": ([32], F32), "cw": ([8], F32), "thr": ([128], F32), "dum": ([32], F32), "cl": ([8], F16),
+    "li": ([96], I32), "lu": ([72], U16), "mk": ([3, 384], B16), "hq": ([24], F16), "pbu": ([24], U16), "pb": ([24], F16),
+    "t1": ([256], F16), "t2": ([128], F16), "plu": ([32], U16), "pl": ([32], F16), "gg": ([512], F16), "no1": ([512], F16),
+    "no": ([512], F16), "ee": ([256], B16), "fm": ([256], B16), "wh": ([4, 8], F32), "whu": ([48], U16), "ww": ([8], F32),
+    "rw": ([4, 128], F16), "q0": ([4, 128], B16), "q1": ([4, 128], B16), "q2": ([4, 128], B16),
+    "lz": ([128], F16), "vz": ([128], F16), "ls": ([8], F16), "o2": ([32], F32), "ou": ([32], U16), "sl": ([96], U16),
+    "xo": ([2, 512], F16), "sd": ([2, 1792], F16), "ss": ([2, 1792], F16), "sc": ([2, 1792], F16),
+    "sq0": ([512], F32), "sq1": ([512], F32), "f1": ([128], F32),
     "e0": ([1024], F32), "e1": ([1024], F32), "e2": ([1024], F32),
-    "t0": ([1024], F32), "t1": ([1024], F32), "t3": ([1024], F32),
+    "t0": ([1024], F32), "t3": ([1024], F32), "t4": ([1024], F32),
 }
+SB["hq16"] = SB.pop("hq")
+SB["pl16"] = SB.pop("pl")
 SCRATCH = {k: ("sbuf", [128] + s, d) for k, (s, d) in SB.items()}
 SCRATCH["ps"] = ("psum", [128, 4096], F32)
-NSEM = 80
+NSEM = 140
 SEMAPHORES = ["qv", "qa", "qp", "qg"] + ["arr%d" % i for i in range(11)] + ["m%d" % i for i in range(NSEM - 15)]
 
-MODEL = dict(cyc=1.04, ga=1.56, sc=3.8, pe=0.52, fix=60.0, hop=120.0, same=60.0, gi=900.0, si=100.0, dl=1800.0,
-             bw=500.0, rl=2500.0)
+MODEL = dict(cyc=0.95, ga=1.4, sc=3.5, pe=0.48, fix=60.0, hop=120.0, same=60.0, gi=900.0, si=100.0, dl=1800.0,
+             bw=500.0, rl=2500.0, look=100.0)
 STR = [(0, 512), (512, 1536), (1536, 2560)]
 SBANK = [0, 1024, 0]
-GFILL, VFILL = 3072, 3072
-PLAN = {0: ('vaaaaaaaaaaa', (0, 7, 9, 10)), 1: ('vvaaavavaaaa', (7, 11)), 2: ('vaaavaaaaaaa', (6, 11)), 3: ('vvvvvvaaavaa', (2, 8)),
-        4: ('vaaa', (0, 1)), 5: ('vvvvv', ()), 6: ('vvvvaaaaaaaa', (1, 2, 3, 4, 5, 6, 7, 8, 9, 10)), 7: ('vvavvv', ())}
-LAST = [(0, 0), (0, 1), (1, 0), (2, 0), (1, 1), (2, 1), (0, 2), (1, 2), (2, 2), (1, 3), (2, 3), (0, 3)]
-BUMP = {'xn': 20000.0, 'L3': -10000.0, 'pair': -6000.0, 'y': 12500.0, 'wrap': 11500.0, 'add': 2500.0, 'rot': 2500.0, 'good': 2500.0,
-        '': -1000.0, 'L2': 14000.0, 'fill': -2500.0, 's': 500.0, 'sadd': 1500.0, 'sa': 1500.0, 'sq': 3000.0, 'sc': 2000.0,
-        'flat': -3000.0, 'gv': -1500.0, 'xo': -500.0, 'ss': -2000.0, 'sg': -1000.0, 'scatter': -1000.0, 'fe': -500.0, 'ga': -4000.0,
-        'L1': -3500.0, 'relisted': -500.0, 'fq': 500.0}
+GFILL = 1024
+PIECE = [(p, 0, 512) for p in range(4)] + [(p, 512, 2560) for p in range(2)] + [(p, a, a + 1024) for a in (512, 1536) for p in (2, 3)]
+LAST = [(0, 0, 512), (1, 0, 512), (0, 512, 1536), (0, 1536, 2560), (1, 512, 1536), (1, 1536, 2560), (2, 0, 512), (2, 512, 1536),
+        (2, 1536, 2560), (3, 512, 1536), (3, 1536, 2560), (3, 0, 512)]
+PLAN = {0: ("aaaaaaavaa", (0, 4, 8, 9)), 1: ("vvaaavvaaa", (0, 1, 8, 9)), 2: ("vavavaaava", (1, 2, 7, 8, 9)), 3: ("vvvavavaavva", (6, 7, 10, 11)),
+        4: ("aavv", (1,)), 5: ("vavv", ()), 6: ("vvvvaaaavv", (3, 5, 6, 7, 8))}
+BUMP = {"whu": 4000.0, "": -500.0, "fill": -3000.0, "m0": -1500.0, "fu": 12000.0, "arr": 500.0, "mask": 3500.0, "relist": -7000.0, "tab": 1000.0, "lose": 3500.0, "c": -500.0, "L1": 4500.0, "sl": 7500.0, "y": -2000.0, "pl": 7500.0, "relisted": -1000.0, "L2": 1000.0, "turn": 2000.0, "s": 500.0, "good": 8500.0, "ss": -500.0, "fe": 4000.0, "send": -8000.0, "sadd": -1000.0, "add": 1500.0, "wrap": -1000.0, "k": -1000.0, "xo": 500.0, "new": 1000.0}
 
 
 def cost(o, M):
@@ -93,70 +92,59 @@ def delay(d, o, M):
     return M["hop"]
 
 
-def schedule(ops, M, bump=None):
+def lists(ops, M, pr, back):
     n = len(ops)
-    pr = [0.0] * n
-    succ = [[] for _ in ops]
+    nxt = [[] for _ in ops]
+    left = [0] * n
     for o in ops:
         for j in o["dep"]:
-            succ[j].append(o["i"])
-    for o in reversed(ops):
-        own = cost(o, M)
-        own = finish(o, own, M, [0.0])
-        pr[o["i"]] = own + max([pr[j] + delay(o, ops[j], M) for j in succ[o["i"]]] + [0.0])
-    pr = [p + o.get("bump", 0.0) + (bump or {}).get(o["tag"].split(" ")[0], 0.0) for p, o in zip(pr, ops)]
-    left = [len(o["dep"]) for o in ops]
-    rdy = [o.get("rel", 0.0) for o in ops]
-    free = {}
-    pool = {}
+            a, b = (o["i"], j) if back else (j, o["i"])
+            nxt[a].append(b)
+            left[b] += 1
+    co = [cost(o, M) for o in ops]
+    lat = [finish(o, 0.0, M, [0.0]) for o in ops]
+    rdy = [lat[i] if back else ops[i].get("rel", 0.0) for i in range(n)]
+    free, pool = {}, {}
     for o in ops:
         free[o["e"]] = 0.0
         pool.setdefault(o["e"], [])
-        if not o["dep"]:
+        if not left[o["i"]]:
             pool[o["e"]].append(o["i"])
-    order = []
-    st = [0.0]
-    end = 0.0
+    order, st, end = [], [0.0], [0.0] * n
     while len(order) < n:
-        best = None
-        for e, lst in pool.items():
-            if not lst:
-                continue
-            t = max(free[e], min(rdy[i] for i in lst))
-            if best is None or t < best[0]:
-                best = (t, e)
-        t, e = best
-        i = max((j for j in pool[e] if rdy[j] <= t + M.get("look", 0.0)), key=lambda j: (pr[j], -j))
-        t = max(t, rdy[i])
+        t, e = min((max(free[e], min(rdy[i] for i in lst)), e) for e, lst in pool.items() if lst)
+        i = max((j for j in pool[e] if rdy[j] <= t + M["look"]), key=lambda j: (pr[j], -j))
         pool[e].remove(i)
-        o = ops[i]
-        t1 = t + cost(o, M)
+        t1 = max(t, rdy[i]) + co[i]
         if e != "x":
             free[e] = t1
-        t2 = finish(o, t1, M, st)
-        end = max(end, t2)
+        end[i] = t1 if back else finish(ops[i], t1, M, st)
         order.append(i)
-        for j in succ[i]:
-            rdy[j] = max(rdy[j], t2 + delay(o, ops[j], M))
+        for j in nxt[i]:
+            d = delay(ops[j], ops[i], M) + lat[j] if back else delay(ops[i], ops[j], M)
+            rdy[j] = max(rdy[j], end[i] + d)
             left[j] -= 1
             if left[j] == 0:
                 pool[ops[j]["e"]].append(j)
     return order, end
 
 
-def replay(ops, order, M):
-    free = {}
-    done = {}
-    busy = {}
-    st = [0.0]
-    for i in order:
-        o = ops[i]
-        t = max([free.get(o["e"], 0.0) if o["e"] != "x" else o.get("rel", 0.0)] + [done[j] + delay(ops[j], o, M) for j in o["dep"]])
-        c = cost(o, M)
-        free[o["e"]] = t + c
-        busy[o["e"]] = busy.get(o["e"], 0.0) + c
-        done[i] = finish(o, t + c, M, st)
-    return done, busy
+def schedule(ops, M, bump, rounds=3):
+    pr = [0.0] * len(ops)
+    succ = [[] for _ in ops]
+    for o in ops:
+        for j in o["dep"]:
+            succ[j].append(o["i"])
+    for o in reversed(ops):
+        pr[o["i"]] = finish(o, cost(o, M), M, [0.0]) + max([pr[j] + delay(o, ops[j], M) for j in succ[o["i"]]] + [0.0])
+    add = [o.get("bump", 0.0) + bump.get(o["tag"].split(" ")[0], 0.0) for o in ops]
+    best = None
+    for r in range(rounds):
+        order, end = lists(ops, M, [p + a for p, a in zip(pr, add)], False)
+        if best is None or max(end) < best[1]:
+            best = (order, max(end))
+        pr = lists(ops, M, end, True)[1]
+    return best
 
 
 def build(g, core, T, topo, plan):
@@ -166,7 +154,6 @@ def build(g, core, T, topo, plan):
     ops = []
     book = {}
     grids = {}
-    ring = [0, 0]
 
     def V(name, *idx):
         shp = SCRATCH[name][1][1:]
@@ -182,6 +169,18 @@ def build(g, core, T, topo, plan):
 
     def C(name, a, b, s=None):
         return V(name, slice(a, b, s))
+
+    def R(name, r, a=None, b=None, s=None):
+        return V(name, r, slice(a, b, s))
+
+    def P(a, n):
+        return C("ps", a, a + n)
+
+    def M(name, a=None, b=None, s=None):
+        for buf, names in (("mh", MH), ("mb", MB), ("wr", WH)):
+            if name in names:
+                return R(buf, names.index(name), a, b, s)
+        return C(name, a, b, s)
 
     def IND(name, a, b, off):
         w = C(name, a, b)
@@ -249,19 +248,24 @@ def build(g, core, T, topo, plan):
         return op("v", lambda: g.vector.tensor_copy(out["ap"], in0["ap"]), [in0], [out],
                   kind(out, [in0], 0.5 if out["two"] and in0["two"] else 1.0), tag=tag)
 
-    def ms(out, val):
-        return op("v", lambda: g.vector.memset(out["ap"], val), [], [out], ("n", out["n"] * (0.5 if out["two"] else 1.0)))
+    def ms(out, val, tag="k"):
+        return op("v", lambda: g.vector.memset(out["ap"], val), [], [out], ("n", out["n"] * (0.5 if out["two"] else 1.0)), tag=tag)
 
     def act(out, in0, f, bias=0.0, scale=1.0, tag=""):
-        return op("a", lambda: g.scalar.activation(out["ap"], in0["ap"], f, bias=bias, scale=scale), [in0], [out],
-                  kind(out, [in0], 1.0), tag=tag)
+        return op("a", lambda: g.scalar.activation(out["ap"], in0["ap"], f, bias=aps(bias), scale=aps(scale)), [in0] + sc_rd(bias, scale),
+                  [out], kind(out, [in0], 1.0), tag=tag)
 
-    def lin(site, out, in0, scale, bias, tag=""):
-        if plan[7][0][site] == "a":
-            return act(out, in0, F.Identity, bias=bias, scale=scale, tag=tag)
-        return ts(out, in0, scale, bias, A.mult, A.add, tag=tag)
+    def iota(out, pattern, base, mult, whole=False):
+        def fn():
+            if whole:
+                return g.iota(out["ap"], pattern, base, mult)
+            return g.iota(out["ap"], pattern, base, mult, allow_small_or_imprecise_dtypes=True)
+        return op("g", fn, [], [out], ("gc", out["n"]), tag="k")
 
-    def mm(trip, start=True, acc=None, wide=1, tag=""):
+    def sel(out, in0, pattern, cmp, fill, base, mult):
+        return op("g", lambda: g.affine_select(out["ap"], in0["ap"], pattern, cmp, fill, base, mult), [in0], [out], ("gc", out["n"]), tag="k")
+
+    def mm(trip, start=True, stop=True, acc=None, wide=1, tag=""):
         o = {}
 
         def fn():
@@ -271,6 +275,7 @@ def build(g, core, T, topo, plan):
             return r
         rd = [t[1] for t in trip] + [t[2] for t in trip]
         o["op"] = op("p", fn, rd, [trip[0][0]], ("pe", sum(max(64, t[2]["n"]) * wide for t in trip)), acc=acc, tag=tag)
+        o["op"]["stop"][0] = stop
         return o["op"]
 
     def raw(ap, n=0, reg=()):
@@ -292,332 +297,327 @@ def build(g, core, T, topo, plan):
             tr = []
             for b, src in enumerate((src0, src1)):
                 dst = cores[(rank + DSH[b]) % nr]
-                en = topo.engines(core, dst)
-                h = len(en) // 2
                 rid, pid, _ = topo.addr(dst)
-                tr.append(RemoteDMATransfer(dst_ids=[DstId(rid=rid, pnc=pid)], dma_engine_mask=sum(1 << u for u in en[b * h:(b + 1) * h]),
+                tr.append(RemoteDMATransfer(dst_ids=[DstId(rid=rid, pnc=pid)], dma_engine_mask=sum(1 << u for u in topo.engines(core, dst)[b::2]),
                                             remote_sem=T.sem["arr%d" % j], src=src["ap"],
                                             dst=C(dname, NV + b * GH, NV + (b + 1) * GH)["ap"]))
             g.remote_dma_fused(tr, local_sem=lsem)
         cnt = sum(len(topo.engines(core, cores[(rank + d) % nr])) // 2 for d in DSH)
         got = sum(len(topo.engines(cores[(rank - d) % nr], core)) // 2 for d in DSH)
-        o = op("g", fn, [src0, src1], guard, ("rem", 0), tag="send%d" % j)
+        o = op("g", fn, [src0, src1], guard, ("rem", 0), tag="send %d" % j)
         o["cnt"] = cnt
-        a = op("x", None, [], [arrive], ("arr", 0), tag="arr%d" % j)
+        a = op("x", None, [], [arrive], ("arr", 0), tag="arr %d" % j)
         a["dep"].add(o["i"])
         a["sem"] = ("arr%d" % j, got)
-        a["after"] = o["i"]
 
-    def wrap(out, src, n, mat="es"):
-        return mm([(out, C(mat, 128 * m, 128 * (m + 1)), C(src, m, 16 * n, 16)) for m in range(16)], tag="wrap")
+    def turn(qs, name, src, grp, tag="turn"):
+        nb_ = 2 if SCRATCH[name][2] == B16 else 4
+        return [dma(q, raw(T[name][a:b, :], reg=V(name)["reg"]), raw(src[0][c:d, 0:GH], reg=src[1]), (b - a) * GH * nb_, grp=grp, tag=tag)
+                for q, (a, b, c, d) in zip(qs, ((0, 112, 16, 128), (112, 128, 0, 16)))]
+
+    def wrap(out, mat, src, a, n):
+        return [(out, M(mat, 15 - m, 143 - m), C(src, a + m, a + 16 * n, 16)) for m in range(16)]
+
+    def rows(r):
+        return raw(T.tb[r:128:16, 0:TREAL], reg=C("tb", 0, TREAL)["reg"])
 
     W = ["w0", "w1", "w2", "w3"]
     XN = ["xn0", "xn1"]
     OF = ["of0", "of1"]
+    B4, B5, B6, B7 = 2048, 2560, 3072, 3584
 
     dma("s", C("w0", 0, GH), raw(T.x[:, 0:GH]), 128 * 1024)
-    dma("a", raw(T.rs0[0:112, :], reg=V("rs0")["reg"]), raw(T.x[16:128, 0:GH]), 112 * 1024, grp="rs")
-    dma("s", raw(T.rs0[112:128, :], reg=V("rs0")["reg"]), raw(T.x[0:16, 0:GH]), 16 * 1024, grp="rs")
+    turn("as", "rs0", (T.x, []), "rs")
     send(0, C("w0", 0, GH), V("rs0"), "w0", [], C("w0", NV, NW))
     ops[-1]["rel"] = 7000.0
+    dma("a", C("n32", 0, 640), raw(T.nb[:]), 128 * 2560, grp="n32")
+    dma("s", C("n32", 640, 664), raw(T.lb[:]), 128 * 96, grp="n32")
     for o in ops:
         o["bump"] = 1e5
+    for k, nm in enumerate(("pk", "pj", "pl", "hq")):
+        dma("s", C("li", 24 * k, 24 * (k + 1)), raw(T[nm][:]), 128 * 96, grp="li")
     dma("s", C("w0", GH, NV), raw(T.x[:, GH:NV]), 128 * 4 * (NV - GH))
-    dma("a", V("n32"), raw(T.nb[:]), 128 * 2560)
-    cp(V("of0"), V("n32"))
-    for si, (a0, a1) in enumerate(STR):
-        if "v" in plan[6][0][4 * si:4 * si + 4]:
-            dma("a" if si == 0 else "s", C("w2", a0, a1), raw(T.x[:, a0:a1]), 128 * 4 * (a1 - a0))
+    for (p, a0, a1), e in zip(PIECE, plan[6][0]):
+        if e == "v" and not any(u == "v" and (b0, b1) == (a0, a1) and q < p for (q, b0, b1), u in zip(PIECE, plan[6][0])):
+            dma("s", C("w2", a0, a1), raw(T.x[:, a0:a1]), 128 * 4 * (a1 - a0))
     for o in ops:
         o["bump"] = o.get("bump", 0.0) + 1e5
-    for k, nm in enumerate(("lb", "pj", "pk", "pl", "hq")):
-        dma("s", C("li", 24 * k, 24 * (k + 1)), raw(T[nm][:]), 128 * 96, grp="li")
-    op("g", lambda: g.iota(T.fl[:, FLW - GFILL:FLW], [[0, GFILL]], 0, 0), [C("w0", 0, GH), V("rs0")],
-       [C("fl", FLW - GFILL, FLW)], ("gc", GFILL), tag="fill")
-    top = FLW - GFILL - VFILL
-    ms(C("fl", top, top + VFILL), 0)["bump"] = 5e4
-    for h in range(0, top, NV):
-        n = min(NV, top - h)
-        dma("s", C("fl", h, h + n), raw(T.x[:, 0:n]), 512 * n, grp="fl", tag="fill")["rel"] = 700.0
-    dma("s", raw(T.fl[0:127:18, 0:4 * NV], reg=C("fl", 0, 4 * NV)["reg"]), raw(T.nb[:]), 600000, tag="flat")
+    cp(V("of0"), C("n32", 0, 640), tag="of0")
     ms(V("onef"), 1.0)["bump"] = 1e5
-    op("g", lambda: g.affine_select(T.idf[:], T.onef[:], [[-1, 128]], A.is_equal, 0.0, 0, 1), [V("onef")], [V("idf")], ("gc", 128))
-    op("g", lambda: g.affine_select(T.bof[:], T.onef[:], [[-16, 8], [0, 16]], A.is_ge, 0.0, 0, 1), [V("onef")], [V("bof")], ("gc", 128))
-    op("g", lambda: g.affine_select(T.bof[:], T.bof[:], [[16, 8], [0, 16]], A.is_ge, 0.0, 15, -1), [V("bof")], [V("bof")], ("gc", 128))
-    op("g", lambda: g.iota(T.iw[:, 0:192], [[1, 192]], 0, 0, allow_small_or_imprecise_dtypes=True), [], [C("iw", 0, 192)], ("gc", 192))
-    op("g", lambda: g.iota(T.dum[:], [[16, 32]], DUM0, 1, allow_small_or_imprecise_dtypes=True), [], [V("dum")], ("gc", 32))
-    op("g", lambda: g.iota(T.i8[:], [[16, 8]], 0, 1), [], [V("i8")], ("gc", 8))
-    for k in range(4):
-        h = 192 << k
-        act(C("iw", h, 2 * h), C("iw", 0, h), F.Identity, bias=float(h))
-    for nm, val in (("i16", 1.0 / 16), ("im64", -64.0), ("im1", -1.0), ("i1", 1.0), ("imk", -1024.0), ("id2", 2.0), ("idm2", -2.0)):
-        act(V(nm), V("idf"), F.Identity, scale=val)
-    act(C("rot", 0, 112), C("idf", 16, 128), F.Identity, scale=-1.0)
-    act(C("rot", 112, 128), C("idf", 0, 16), F.Identity, scale=-1.0)
-    act(V("cb"), V("onef"), F.Identity, scale=-7.5 / 16)
+    sel(V("idf"), V("onef"), [[-1, 128]], A.is_equal, 0.0, 0, 1)
+    sel(V("bof"), V("onef"), [[-16, 8], [0, 16]], A.is_ge, 0.0, 0, 1)
+    sel(V("bof"), V("bof"), [[16, 8], [0, 16]], A.is_ge, 0.0, 15, -1)
+    iota(V("cf"), [[1, TB]], 0, 0)
+    iota(V("ki"), [[0, 2]], 0, 1, True)
+    iota(V("dum"), [[16, 32]], TREAL - int(CEN), 1)
+    op("g", lambda: g.iota(T.tb[:, TW - GFILL:TW], [[0, GFILL]], 0, 0, allow_small_or_imprecise_dtypes=True), [], [C("tb", TW - GFILL, TW)],
+       ("gc", GFILL), tag="fill")
+    ms(C("tb", 0, TW - GFILL), 0.0, tag="fill")
+    ms(V("mh", slice(MH.index("l1"), None)), 0.0)
+    ms(V("mb"), 0.0)
+    ms(V("wr"), 0.0)
+    ms(V("y2b"), 0.0)
     ms(V("ones"), 1.0)
-    act(V("bo"), V("bof"), F.Identity)
-    ms(V("em"), 0.0)
-    for m in range(16):
-        act(C("em", 129 * m, 128 * (m + 1), 16), C("bof", m, 128, 16), F.Identity, scale=1.0 / 16)
-    op("g", lambda: g.affine_select(T.sef[:], T.onef[:], [[-18, 8], [0, 16]], A.is_equal, 0.0, 0, 1), [V("onef")], [V("sef")], ("gc", 128))
-    ms(V("es"), 0.0)
-    for m in range(16):
-        act(C("es", 129 * m, 128 * (m + 1), 16), C("sef", m, 128, 16), F.Identity)
-    ts(V("pg"), C("i8", 0, 1), 112, None, A.bitwise_and)
-    cp(V("pgf"), V("pg"))
-    ts(V("lnf"), V("i8"), V("pgf"), None, A.subtract)
-    act(V("wc"), V("lnf"), F.Exp, bias=69.85, scale=-1.1)
-    act(V("thr"), C("iw", 0, 128), F.Exp, bias=69.85 + math.log(6.5), scale=-1.1)
+    ms(V("nf", slice(None), 160), -CEN - 1)
+    ms(V("pf", slice(None), 160), 160 - CEN)
+    ms(V("cw"), 0.0)
+    ts(C("ki", 0, 1), C("ki", 0, 1), 15, None, A.bitwise_and, tag="k")
+    ts(C("ki", 1, 2), C("ki", 1, 2), 3, None, A.bitwise_and, tag="k")
+    cp(V("kf"), V("ki"), tag="k")
+    KM = C("kf", 0, 1)
+    ts(V("p16"), C("cf", 0, 16), KM, None, A.is_equal, tag="k")
+    ts(V("r4"), C("cf", 0, 4), C("kf", 1, 2), None, A.is_equal, tag="k")
+
+    def S(a):
+        return C("p16", a, a + 1)
+
+    def R4(r):
+        return C("r4", r, r + 1)
+
+    def K(n):
+        return C("col", n, n + 1)
+
+    def kon(out, in0, s1, s2=None, o1=A.mult):
+        if s2 is None:
+            return act(out, in0, F.Identity, scale=s1, tag="k")
+        if o1 == A.add:
+            return act(out, in0, F.Identity, scale=s1, bias=s2, tag="k")
+        return ts(out, in0, s1, s2, A.mult, o1, tag="k")
+    ID, BO = (lambda a, s: C("idf", a, 128, s)), (lambda a, s: C("bof", a, 128, s))
+    for nm, val in (("i161", 161.0), ("im527", -527.0), ("imk", -1024.0), ("i16", 1.0 / 16), ("im64", -64.0), ("im1", -1.0), ("i1", 1.0),
+                    ("i4k", 4096.0), ("id2", 2.0)):
+        kon(M(nm), V("idf"), val)
+    kon(V("cb"), V("onef"), -7.5 / 16)
+    kon(K(0), R4(2), -1.0, 1.0, A.add)
+    kon(K(1), R4(2), 30000.0)
+    kon(K(2), KM, 1.0, -CEN, A.add)
+    kon(K(3), KM, float(TB), -CEN, A.add)
+    kon(K(4), KM, -SLOPE, TOPW - 512.0, A.add)
+    kon(K(5), S(6), BIG / 8)
+    kon(K(6), S(6), -BIG / 8)
+    kon(K(7), S(3), -1.0)
+    ts(K(8), S(6), S(2), 1e28, A.subtract, A.mult, tag="k")
+    ts(K(9), R4(1), R4(2), -8.0, A.add, A.mult, tag="k")
+    kon(K(10), K(9), 1.0, R4(0), A.add)
+    kon(K(11), R4(0), -1.0)
+    kon(R("sf", 0), V("cf"), 16.0, K(2), A.add)
+    kon(R("sf", 1), V("cf"), 1.0, K(3), A.add)
+    kon(C("cw", 0, 4), C("p16", 1, 16, 4), 1.0, S(6), A.add)
+    kon(V("cl"), C("cf", 0, 8), -16 * SLOPE / 256)
+    act(V("thr"), C("cf", 0, 128), F.Exp, bias=TOPW + math.log(6.5), scale=-SLOPE, tag="k")
+    for nm, a, s, src, f in (("l1", 0, 4, ID(0, 4), 1.0), ("l1", 1, 4, ID(0, 4), 1.0), ("l1", 2, 4, BO(2, 4), S(3)),
+                             ("l2", 0, 4, BO(0, 4), K(7)), ("l2", 6, 8, BO(6, 8), K(7)), ("l3", 1, 4, BO(1, 4), K(7)), ("l3", 2, 8, BO(2, 8), K(7)),
+                             ("lb", 0, 1, BO(0, 1), S(3)), ("lt", 0, 4, BO(0, 4), S(3)), ("lt", 1, 4, BO(1, 4), S(7)),
+                             ("luu", 2, 4, BO(2, 4), S(12)), ("lul", 2, 4, ID(0, 4), 1.0),
+                             ("l4", 2, 16, BO(2, 16), K(10)), ("l4", 6, 16, ID(3, 16), 1.0), ("lpen", 0, 1, BO(0, 1), K(8)),
+                             ("bo", 0, 1, BO(0, 1), 1.0), ("lml", 2, 4, ID(1, 4), -BIG)):
+        kon(M(nm, a, 128, s), src, f)
+    for nm, a, f, c in (("lmu", 0, -BIG, 5), ("lmu", 1, -BIG, 5), ("lmu", 2, BIG, 6), ("lmu", 3, 0.0, 5),
+                        ("lml", 0, BIG, 6), ("lml", 1, BIG, 6), ("lml", 3, 0.0, 6)):
+        ts(M(nm, a, 128, 4), ID(1, 4), f, K(c), A.mult, A.add, tag="k")
+    kon(V("tri"), BO(1, 4), K(11))
+    sel(V("tri"), V("tri"), [[4, 32]], A.is_gt, 0.0, 0, -1)
+    sel(V("tri"), V("tri"), [[4, 32]], A.not_equal, 1.0, 0, -1)
+    cp(M("l4", 1, 128, 4), V("tri"), tag="k")
+    for nm, src, f in (("xw1", BO(0, 16), R4(1)), ("xwp", BO(0, 16), 4096.0), ("xwm", BO(0, 16), -4096.0), ("y2", ID(2, 16), 1.0),
+                       ("y3", ID(3, 16), 1.0), ("y6", ID(6, 16), 1.0), ("y10", ID(10, 16), 1.0), ("y2b", ID(2, 16), 1.0)):
+        ts(M(nm, 15, 143, 16), src, f, None, A.mult, tag="k")
+    act(V("nf", slice(None), slice(0, 160)), C("n32", 0, 640), F.Identity, bias=-CEN, tag="tab")
+    ts(V("na"), V("n32"), float(NV), CEN, A.min, A.subtract, tag="tab")
+    ts(V("nh"), V("na"), 1.0 / 16, 1100 + 64 - 7.5 / 16, A.mult, A.add, tag="tab")
+    for a, b in ((0, 480), (480, 664)):
+        o = B6 if a == 0 else B7
+        mm([(P(o, b - a), M(m), C(s, a, b)) for m, s in (("i161", "na"), ("imk", "nh"), ("imk", "nh"), ("im527", "nh"))], tag="tab")
+    c0 = TB * CEN + 2575.0 * 1100 - CEN
+    act(V("pf", slice(0, 3), slice(0, 160)), P(B6, 480), F.Identity, bias=c0, tag="tab")
+    act(R("pf", 3, 0, 160), P(B7, 160), F.Identity, bias=c0, tag="tab")
+    act(V("pb"), P(B7 + 160, 24), F.Identity, bias=c0, tag="tab")
+    ts(V("pbu"), V("pb"), CEN, None, A.add, tag="tab")
     for p in range(4):
-        ms(C("wt", 16 * p, 16 * (p + 1)), (4 - p) / 4.0)
-    ms(V("zz"), 0.0)
-    LB = C("li", 0, 24)
-    ts(V("hb"), LB, -7.5, 1.0 / 16, A.add, A.mult)
-    ts(V("tb"), V("hb"), -10239.0, None, A.mult)
-    ts(V("ub"), LB, 640.0, None, A.mult)
-    tt(V("bb"), V("tb"), V("ub"), A.add)
-    ts(V("p160"), C("li", 24, 96), 160.0, None, A.mult)
-    tt(C("ib", 0, 24), V("bb"), C("p160", 24, 48), A.add)
-    tt(C("ib", 24, 48), V("bb"), C("p160", 0, 24), A.add)
-    cp(V("ibu"), V("ib"))
-    ts(V("hq16"), C("li", 96, 120), 1.0 / 16, None, A.mult)
-    for si, (a0, a1) in enumerate(STR):
-        if si == 0:
-            ts(C("xn0", a0, a1), C("w0", a0, a1), -1.0, 2048.0, A.mult, A.add)
-        else:
-            act(C("xn0", a0, a1), C("w0", a0, a1), F.Identity, bias=2048.0, scale=-1.0)
+        dma("s", rows(4 * p), R("nf", p), 200000, grp="tab", tag="tab")
+        dma("s", rows(4 * p + 1), R("pf", p), 200000, grp="tab", tag="tab")
+    for r in range(2):
+        dma("s", rows(4 * r + 3), R("sf", r), 200000, grp="tab", tag="tab")
+    cp(V("lu"), C("li", 0, 72), tag="tab")
+    for u in range(3):
+        act(R("mk", u), IND("cw", 0, 8, C("lu", 24 * u, 24 * u + 24)), F.Identity, tag="mask")
+    act(V("hq16"), C("li", 72, 96), F.Identity, tag="k")
+    for a0, a1 in STR:
+        act(C("xn0", a0, a1), C("w0", a0, a1), F.Identity, bias=2048.0, scale=-1.0, tag="xn")
 
     def marks():
         dma("s", C("aw", 0, NV), raw(T.am[:]), 128 * 2 * NV)["rel"] = 40000.0
-        dma("s", raw(T.ra[0:112, :], reg=V("ra")["reg"]), raw(T.am[16:128, 0:GH]), 112 * 512, grp="ra")["rel"] = 40000.0
-        dma("s", raw(T.ra[112:128, :], reg=V("ra")["reg"]), raw(T.am[0:16, 0:GH]), 16 * 512, grp="ra")["rel"] = 40000.0
+        for o in turn("ss", "ra", (T.am, []), "ra"):
+            o["rel"] = 40000.0
         send(10, C("aw", 0, GH), V("ra"), "aw", [], C("aw", NV, NW))
 
-    def piece(k, of, si, p, kindk):
-        a0, a1 = STR[si]
-        who, sg = plan[kindk]
+    def clips(d, s, c, by_scalar, tag):
+        if by_scalar:
+            ts(c, d, -2047.0, 2047.0, A.max, A.min, tag="c" + tag)
+            act(s, d, F.Sign, tag="s" + tag)
+            return 1
+        ts(s, d, -1.0, 1.0, A.max, A.min, tag="s" + tag)
+        ts(d, d, -2047.0, 2047.0, A.max, A.min, tag="c" + tag)
+        return 0
+
+    def piece(k, of, p, a0, a1, who, sg):
         win = IND(W[k % 4], 0, NW, C(of, (p * NV + a0) // 16, (p * NV + a1) // 16))
-        d, s = C("d1", p * NV + a0, p * NV + a1), C("d2", p * NV + a0, p * NV + a1)
-        tag = "k%d s%d p%d" % (k, si, p)
-        if who[4 * si + p] == "v":
+        d, s, c = (C(u, p * NV + a0, p * NV + a1) for u in ("d1", "d2", "d3"))
+        tag = " k%d a%d p%d" % (k, a0, p)
+        if who == "v":
             if k == 0:
-                tt(d, win, C("w2", a0, a1), A.subtract, tag="gv " + tag)
+                tt(d, win, C("w2", a0, a1), A.subtract, tag="gv" + tag)
             else:
-                tt(d, win, C(XN[k % 2], a0, a1), A.add, tag="gv " + tag)
+                tt(d, win, C(XN[k % 2], a0, a1), A.add, tag="gv" + tag)
         else:
-            act(d, win, F.Identity, bias=-2048.0 if k == 0 else 0.0, tag="ga " + tag)
-            dma("g", d, C(XN[k % 2], a0, a1), 256 * (a1 - a0), add=True, tag="add " + tag)
-        if 4 * si + p in sg:
-            ring[0] += 1
-            h = 1024 * (ring[0] % 2)
-            ts(C("d3", h, h + a1 - a0), d, -2047.0, 2047.0, A.max, A.min, tag="c " + tag)
-            act(s, d, F.Sign, tag="s " + tag)
-            return ("d3", h - a0), ("d2", p * NV)
-        ts(s, d, -1.0, 1.0, A.max, A.min, tag="s " + tag)
-        ts(d, d, -2047.0, 2047.0, A.max, A.min, tag="c " + tag)
-        return ("d1", p * NV), ("d2", p * NV)
+            act(d, win, F.Identity, bias=-2048.0 if k == 0 else 0.0, tag="ga" + tag)
+            dma("g", d, C(XN[k % 2], a0, a1), 256 * (a1 - a0), add=True, tag="add" + tag)
+        return ("d1", "d3")[clips(d, s, c, sg, tag)]
 
     def sweep(k, of):
         wn, xn, xo = W[(k + 1) % 4], XN[(k + 1) % 2], XN[k % 2]
+        who, sg = plan[k % 3 if k else 6]
+        cn = {}
         for si, (a0, a1) in enumerate(STR):
             blocks = [(b, min(b + 512, a1)) for b in range(a0, a1, 512)]
-            bank = [C("ps", SBANK[si] + b0 - a0, SBANK[si] + b1 - a0) for b0, b1 in blocks]
+            bank = [P(SBANK[si] + b0 - a0, b1 - b0) for b0, b1 in blocks]
             for (b0, b1), ps in zip(blocks, bank):
-                o = mm([(ps, V("im1"), C(xo, b0, b1)),
-                        (ps, raw(T.cb[0:1, :], reg=V("cb")["reg"]), raw(T.ones[0:1, 0:b1 - b0], n=b1 - b0, reg=V("ones")["reg"]))])
-                o["stop"][0] = False
-            for p in range(4):
-                cn, sn = piece(k, of, si, p, k % 3 if k else 6)
+                mm([(ps, M("im1"), C(xo, b0, b1)),
+                    (ps, raw(T.cb[0:1, :], reg=V("cb")["reg"]), raw(T.ones[0:1, 0:b1 - b0], n=b1 - b0, reg=V("ones")["reg"]))], stop=False, tag="m0")
+            for n, (p, c0, c1) in enumerate(PIECE):
+                if c1 <= a0 or a1 <= c0:
+                    continue
+                if n not in cn:
+                    cn[n] = piece(k, of, p, c0, c1, who[n], n in sg)
                 for (b0, b1), ps in zip(blocks, bank):
-                    mm([(ps, V("im64"), C(sn[0], sn[1] + b0, sn[1] + b1))], start=False, acc=(k, b0))
-                    mm([(ps, V("i16"), C(cn[0], cn[1] + b0, cn[1] + b1))], start=False, acc=(k, b0))
-            ts(C(wn, a0, a1), C("ps", SBANK[si], SBANK[si] + a1 - a0), -2048.0, 2047.0, A.max, A.min, tag="fin k%d b%d" % (k, a0))
-            act(C(xn, a0, a1), C(wn, a0, a1), F.Identity, scale=-1.0, tag="xn k%d b%d" % (k, a0))
+                    if c0 <= b0 < c1:
+                        mm([(ps, M("im64"), C("d2", p * NV + b0, p * NV + b1))], start=False, acc=(k, b0), tag="ms")
+                        mm([(ps, M("i16"), C(cn[n], p * NV + b0, p * NV + b1))], start=False, acc=(k, b0), tag="mc")
+            ts(C(wn, a0, a1), P(SBANK[si], a1 - a0), -2048.0, 2047.0, A.max, A.min, tag="fin k%d b%d" % (k, a0))
             if a0 == 0:
-                mm([(C("ps", 0, GH), V("rot"), C(xn, 0, GH))])
                 rs = "rs%d" % ((k + 1) % 2)
-                cp(V(rs), C("ps", 0, GH), tag="rot")
+                turn("ss", rs, (T[wn], C(wn, 0, GH)["reg"]), ("rs", k))
                 send(k + 1, C(wn, 0, GH), V(rs), wn, [C(W[(k + 2) % 4], NV, NW)], C(wn, NV, NW))
+            act(C(xn, a0, a1), C(wn, a0, a1), F.Identity, scale=-1.0, tag="xn k%d b%d" % (k, a0))
 
-    def relist(of):
-        dma("s", V("n32"), raw(T.fl[0:127:18, 0:4 * NV], reg=C("fl", 0, 4 * NV)["reg"]), 500000, tag="relist")
-        cp(V(of), V("n32"), tag="relisted")
-
-    def put(lose, src):
-        for r in range(4):
-            tt(C("o1", r, 32, 4), src[r], lose, A.max)
-        tt(V("o2"), V("o1"), V("dum"), A.min)
-        cp(V("ou"), V("o2"))
-        cp(IND("fl", 0, FLW, V("ou")), V("rw"), tag="scatter")
+    def put(skip, src, of, n):
+        mm(skip, tag="wrap")
+        ts(V("ls"), skip[0][0], 0.0, 4096.0, A.max, A.min, tag="put")
+        mm([(P(B4, 32), M("i1"), V("pl16"))] + [(P(B4 + 8 * r, 8), M("i1"), V("ls")) for r in range(4)], tag="wrap")
+        tt(V("o2"), P(B4, 32), V("dum"), A.min, tag="put")
+        ts(V("ou"), V("o2"), CEN, None, A.add, tag="put")
+        cp(IND("tb", 0, TW, V("ou")), V(src), tag="scatter")
+        for p in range(4):
+            dma("s", R("nf", p), rows(4 * p), 150000, grp=("relist", n), tag="relist")
+        ts(V(of), V("nf", slice(None), slice(0, 160)), CEN, None, A.add, tag="relisted")
 
     def lanes(t, of):
-        c0 = 8 * t
-        B4, B5 = 2048, 2560
-        act(C("r1", 0, 128), IND("fl", 0, FLW, C("ibu", c0, c0 + 8)), F.Identity, bias=-1024.0, tag="L1")
-        act(C("r1", 128, 256), IND("fl", 0, FLW, C("ibu", 24 + c0, 32 + c0)), F.Identity, bias=-1024.0)
-        wrap(C("ps", B4, B4 + 16), "r1", 16)
-        pa_, pc_, pac = C("ps", B4, B4 + 8), C("ps", B4 + 8, B4 + 16), C("ps", B4, B4 + 16)
-        ts(V("hi"), pac, 1016.5, 1.0 / 16, A.add, A.mult)
-        ts(V("uu"), pac, 640.0, 655360.0, A.mult, A.add)
-        ts(V("tt"), V("hi"), -10239.0, None, A.mult)
-        tt(V("vv"), C("uu", 8, 16), C("p160", 48 + c0, 56 + c0), A.add)
-        tt(V("ic"), C("tt", 8, 16), V("vv"), A.add)
-        cp(V("icu"), V("ic"))
-        lin(0, C("wh", 0, 32, 4), pa_, 1.0, 1024.0)
-        lin(0, C("wh", 3, 32, 4), pc_, 1.0, 1024.0)
-        lin(1, C("wh", 1, 32, 4), C("li", c0, c0 + 8), 1.0, 0.0)
-        lin(2, V("yy", 0, slice(1, 16, 2)), C("wh", 3, 32, 4), 1.0, -1024.0)
-        lin(2, V("yy", 0, slice(16, 32, 2)), C("wh", 3, 32, 4), 1.0, -1024.0)
-        lin(2, V("yy", 0, slice(0, 16, 2)), C("li", c0, c0 + 8), 1.0, -1024.0)
-        lin(2, V("yy", 0, slice(17, 32, 2)), C("li", c0, c0 + 8), 1.0, -1024.0)
-        lin(2, V("yy", 1), V("yy", 0), 1.0, 0.0)
-        lin(2, V("yy", slice(2, 4)), V("yy", slice(0, 2)), 1.0, 0.0)
-        tt(C("bad", 0, 16, 2), C("tt", 0, 8), C("uu", 0, 8), A.add)
-        tt(V("bc"), C("tt", 8, 16), C("uu", 8, 16), A.add)
-        cp(C("lbc", 1, 16, 2), V("bc"))
-        cp(C("lbc", 0, 16, 2), C("bb", c0, c0 + 8))
-        act(V("r2"), IND("fl", 0, FLW, V("icu")), F.Identity, bias=-1024.0, tag="L2")
-        pd_ = C("ps", B5, B5 + 8)
-        wrap(pd_, "r2", 8)
-        ts(V("h2"), pd_, 1016.5, 1.0 / 16, A.add, A.mult)
-        ts(V("u2"), pd_, 640.0, 655360.0, A.mult, A.add)
-        ts(V("t2"), V("h2"), -10239.0, None, A.mult)
-        tt(C("bad", 1, 16, 2), V("t2"), V("u2"), A.add)
-        cp(V("lad"), V("bad"))
-        lin(3, C("wh", 2, 32, 4), pd_, 1.0, 1024.0)
-        cp(V("whu"), V("wh"))
-        cp(V("rw"), IND("iw", 0, NW, V("whu")))
-        WA, WB, WD, WC = [C("wh", r, 32, 4) for r in range(4)]
-        tt(V("zz", 0, slice(32, 48, 2)), WA, WC, A.is_equal)
-        tt(V("zz", 1, slice(32, 48, 2)), WB, WD, A.is_equal)
-        tt(V("zz", 2, slice(32, 48, 2)), WC, WD, A.is_equal)
-        for r, u in enumerate((WA, WC, WD)):
-            ts(V("zz", r, slice(33, 48, 2)), u, float(NV), None, A.is_ge)
-        for p in range(4):
-            act(C("r3", 256 * p, 256 * (p + 1)), IND("fl", 160 * p, FLW, V("lad")), F.Identity, bias=-1024.0, tag="L3")
-        for p in range(4):
-            act(C("r4", 256 * p, 256 * (p + 1)), IND("fl", 160 * p, FLW, V("lbc")), F.Identity, bias=-1024.0)
-        pn = C("ps", B4, B4 + 64)
-        wrap(pn, "r3", 64)
-        tt(V("z1"), pn, V("yy", slice(None), slice(0, 16)), A.is_equal)
-        tt(V("zz", slice(None), slice(16, 32)), pn, V("yy", slice(None), slice(16, 32)), A.is_equal)
-        ts(C("sl", 0, 128, 2), pn, 1024.0, None, A.add)
-        tt(V("zz", slice(None), slice(0, 16)), V("z1"), V("wt"), A.mult)
-        tt(V("z2"), V("zz", slice(0, 2)), V("zz", slice(2, 4)), A.max)
-        tt(V("z3"), V("z2", 0), V("z2", 1), A.max)
-        tt(V("z4"), C("z3", 16, 32), C("z3", 32, 48), A.max)
-        tt(V("z5"), C("z3", 0, 16), V("z4"), A.is_gt)
-        tt(V("gd"), C("z5", 0, 16, 2), C("z5", 1, 16, 2), A.mult)
-        tt(V("ww"), V("gd"), V("wc"), A.mult, tag="good")
-        lin(4, V("ng"), V("gd"), -BIG, BIG)
-        lin(4, V("pa"), C("z3", 0, 16), -640.0, 640.0)
-        tt(V("iad"), V("pa"), V("bad"), A.add)
-        n = 0
-        for c in (0, 7, 6, 5, 4, 3, 2, 1, 0):
-            rs = (0,) if (c == 0 and n == 0) else ((1, 2, 3) if c == 0 else (0, 1, 2, 3))
-            for r in rs:
-                q = "q%d" % (n % 3)
-                ts(V(q, slice(c, 8)), C("rw", 64 * c, 512), C("wh", 4 * c + r, 4 * c + r + 1), C("ww", c, c + 1), A.is_equal, A.mult, tag="pair")
-                o = mm([(C("ps", B5 + 16 * c, B5 + 128), V("bo"), V(q, slice(c, 8), u)) for u in range(4)], start=n == 0)
-                o["stop"][0] = n == 31
-                n += 1
-        tt(V("lz"), C("ps", B5, B5 + 128), V("thr"), A.is_ge)
-        pl_ = C("ps", B4, B4 + 8)
-        wrap(pl_, "lz", 8)
-        lin(5, V("lb1"), pl_, BIG, 0.0)
-        tt(V("lb2"), V("lb1"), V("ng"), A.max)
-        iA, iD, iB, iC = C("iad", 0, 16, 2), C("iad", 1, 16, 2), C("ib", c0, c0 + 8), V("ic")
-        put(V("lb2"), [iC, iD, iB, iA])
-        relist(of)
-        pm = C("ps", B5, B5 + 64)
-        wrap(pm, "r4", 64)
-        ts(C("sl", 1, 128, 2), pm, 1024.0, None, A.add)
-        cp(C("sl", 129, 160), C("whu", 0, 31))
-        cp(C("sl", 128, 160, 4), C("whu", 3, 32, 4))
-        return [iB, iA, iC, iD]
+        GA, GC, GB, GD = (C("gg", 128 * r, 128 * (r + 1)) for r in range(4))
+        MK, MJ, ML = (R("mk", u, 128 * t, 128 * (t + 1)) for u in range(3))
+        FA, FD = C("fm", 0, 128), C("fm", 128, 256)
+        PB = C("pbu", 8 * t, 8 * t + 8)
+        tt(C("t1", 0, 128), IND("tb", 0, TW, PB), MK, A.mult, tag="L1")
+        tt(C("t1", 128, 256), IND("tb", 0, TW, PB), MJ, A.mult, tag="L1")
+        mm(wrap(P(B4, 16), "xw1", "t1", 0, 16), tag="wrap")
+        mm([(P(B4 + 16, 8), M("i1"), C("pb", 8 * t, 8 * t + 8))], tag="wrap")
+        ts(C("plu", 0, 24), P(B4, 24), CEN, None, A.add, tag="L1")
+        tt(V("t2"), IND("tb", 0, TW, C("plu", 8, 16)), ML, A.mult, tag="L2")
+        mm(wrap(P(B4 + 24, 8), "xw1", "t2", 0, 8), tag="wrap")
+        ts(C("plu", 24, 32), P(B4 + 24, 8), CEN, None, A.add, tag="L2")
+        act(V("pl16"), P(B4, 32), F.Identity, tag="pl")
+        act(V("gg"), IND("tb", 0, TW, V("plu")), F.Identity, scale=K(0), bias=K(1), tag="L3")
+        for h, (own, first, second) in enumerate(((GA, GB, GC), (GD, GC, GB))):
+            mm([(P(B6 + 128 * h, 128), M(m), u) for m, u in (("l1", own), ("l2", first), ("l3", second))], tag="good")
+        ts(V("ee"), P(B6, 256), 0.0, None, A.is_equal, tag="good")
+        mm([(P(B7, 256), M("l4"), V("ee"))], tag="good")
+        ts(V("fm"), P(B7, 256), 0.5, None, A.is_ge, tag="good")
+        mm([(P(B5, 512), M("lb"), V("gg"))], tag="rw")
+        act(V("rw"), P(B5, 512), F.Identity, tag="rw")
+        mm(wrap(P(B4, 32), "y3", "gg", 0, 32), tag="wrap")
+        act(V("wh"), P(B4, 32), F.Identity, tag="rw")
+        ts(C("whu", 0, 32), V("wh"), CEN, None, A.add, tag="whu")
+        ts(C("whu", 32, 48), V("wh", slice(0, 4, 3)), CEN, None, A.add, tag="whu")
+        mm(wrap(P(B4, 8), "y2b", "fm", 0, 8) + wrap(P(B4, 8), "y2b", "fm", 128, 8) + [(P(B4, 8), M("i1"), V("cl"))], tag="good")
+        act(V("ww"), P(B4, 8), F.Exp, scale=256.0, bias=K(4), tag="good")
+        for o, lu, lm in ((B6, "luu", "lmu"), (B7, "lul", "lml")):
+            mm([(P(o, 512), M(lu), V("gg"))] + [(P(o + 128 * r, 128), M("lt"), u) for r, u in enumerate((GC, GA, GD, GB))]
+               + [(P(o + 128 * r, 128), M(lm), u) for r, u in enumerate((FA, ML, MK, FD))], tag="new")
+        tt(V("no1"), P(B6, 512), V("gg"), A.min, tag="new")
+        tt(V("no"), P(B7, 512), V("no1"), A.max, tag="new")
+        mm([(P(B5, 128), M("lpen"), FA), (P(B5, 128), M("lpen"), FD)], stop=False, tag="pm")
+        for n in range(32):
+            c, r, q = n // 4, n % 4, "q%d" % (n % 3)
+            ts(V(q, slice(None), slice(16 * c, 128)), V("rw", slice(None), slice(16 * c, 128)), R("wh", r, c, c + 1), C("ww", c, c + 1),
+               A.is_equal, A.mult, tag="pair")
+            mm([(P(B5 + 16 * c, 128 - 16 * c), M("bo"), R(q, u, 16 * c, 128)) for u in range(4)], start=False, stop=n == 31, tag="pm")
+        tt(V("lz"), P(B5, 128), V("thr"), A.is_ge, tag="lose")
+        put(wrap(P(B4 + 64, 8), "xwp", "lz", 0, 8), "no", of, 2 * t)
+        for p, y in enumerate(("y2", "y6", "y10")):
+            mm(wrap(P(B4 + 128 + 32 * p, 32), y, "no", 0, 32), tag="sl")
+        ts(V("sl"), P(B4 + 128, 96), CEN, None, A.add, tag="sl")
 
-    def stress(k, last):
+    def stress(k, z):
         w = W[k % 4]
-        B5 = 2560
         off = 2048.0 if k == 0 else 0.0
-        act(V("xo"), IND(w, 0, NW, V("whu")), F.Identity, bias=off, scale=-1.0, tag="xo")
-        tot = C("ps", B5, B5 + 128)
-        calls = ([4] if last else []) + [0, 1, 2, 3]
-        who, sg = plan[5 if last else 4]
-        for n, p in enumerate(calls):
-            ring[1] = (ring[1] + 512) % 1536
-            d, s = C("sd", ring[1], ring[1] + 512), C("ss", ring[1], ring[1] + 512)
-            win = IND(w, 0, NW, C("sl", 32 * p, 32 * (p + 1)))
-            if who[n] == "v" and k:
-                tt(d, win, V("xo"), A.add, tag="sg")
+        act(R("xo", z), IND(w, 0, NW, C("whu", 0, 32)), F.Identity, bias=off, scale=-1.0, tag="xo")
+        who, sg = plan[4 + z]
+        who = "aaaa" if k == 0 else who
+        part = [(512 * p, 512, C("sl", 32 * p, 32 * p + 32), R("xo", z)) for p in range(3)]
+        part.append((1536, 256, C("whu", 16 + 16 * z, 32 + 16 * z), R("xo", z, 128 * z, 128 * z + 256)))
+        tot = P(B5, 128)
+        for n in (3, 0, 1, 2):
+            a, m, lst, own = part[n]
+            d, s, c = (R(u, z, a, a + m) for u in ("sd", "ss", "sc"))
+            if who[n] == "v":
+                tt(d, IND(w, 0, NW, lst), own, A.add, tag="sg")
             else:
-                act(d, win, F.Identity, bias=-off, tag="sa")
-                dma("g", d, V("xo"), 256 * 512, add=True, tag="sadd")
-            if n not in sg:
-                ts(s, d, -1.0, 1.0, A.max, A.min, tag="ss")
-                ts(d, d, -2047.0, 2047.0, A.max, A.min, tag="sc")
-            else:
-                ts(s, d, -2047.0, 2047.0, A.max, A.min, tag="sc")
-                act(d, d, F.Sign, tag="ss")
-                d, s = s, d
-            u = C("ps", 3072 + 512 * (n % 2), 3584 + 512 * (n % 2))
-            mm([(u, V("imk"), s), (u, V("i1"), d)])
+                act(d, IND(w, 0, NW, lst), F.Identity, bias=-off, tag="sa")
+                dma("g", d, own, 256 * m, add=True, tag="sadd")
+            c = (d, c)[clips(d, s, c, n in sg, "s")]
+            u = P(B6 + 512 * (n % 2), m)
+            mm([(u, M("imk"), s), (u, M("i1"), c)], tag="su")
             sq = "sq%d" % (n % 2)
-            act(V(sq), u, F.Square, tag="sq")
-            wts = [(1, "idm2"), (3, "idm2"), (0, "id2"), (2, "id2")] if p == 4 else [(r, "idf") for r in range(4)]
-            o = mm([(tot, V(m), V(sq, slice(None), r)) for r, m in wts], start=n == 0, wide=4)
-            o["stop"][0] = n == len(calls) - 1
+            act(C(sq, 0, m), u, F.Square, tag="sq")
+            mm([(tot, V("id2" if n == 3 else "idf"), C(sq, b, b + 128)) for b in range(0, m, 128)], start=n == 3, stop=n == 2, wide=4, tag="st")
         return tot
 
-    def votes(t, tot, old, of):
-        tt(V("lz"), tot, V("f1"), A.is_gt, tag="vote")
-        pv = C("ps", 2048, 2056)
-        wrap(pv, "lz", 8, "em")
-        tt(V("lb3"), pv, C("hq16", 8 * t, 8 * t + 8), A.is_lt)
-        ts(V("lb4"), V("lb3"), BIG, None, A.mult)
-        tt(V("lb3"), V("lb4"), V("lb2"), A.max)
-        put(V("lb3"), old)
-        relist(of)
+    def votes(t, tot, of):
+        tt(V("vz"), tot, V("f1"), A.is_gt, tag="vote")
+        o = P(B4 + 64, 8)
+        put(wrap(o, "xwp", "lz", 0, 8) + [(o, M("i4k"), C("hq16", 8 * t, 8 * t + 8))] + wrap(o, "xwm", "vz", 0, 8), "gg", of, 2 * t + 1)
 
     def last(k, of):
-        n = 0
-        nb = 0
-        for si, p in LAST:
-            a0, a1 = STR[si]
-            if True:
-                cn, sn = piece(k, of, si, p, 3)
-                e, tn = "e%d" % (n % 3), ("t0", "t1", "t3")[n % 3]
-                nb = 1024 * (n % 4)
-                for b0 in range(a0, a1, 512):
-                    u = C("ps", nb + b0 - a0, nb + b0 - a0 + 512)
-                    mm([(u, V("imk"), C(sn[0], sn[1] + b0, sn[1] + b0 + 512)), (u, V("i1"), C(cn[0], cn[1] + b0, cn[1] + b0 + 512))])
-                ev, tv = C(e, 0, a1 - a0), C(tn, 0, a1 - a0)
-                act(ev, C("ps", nb, nb + a1 - a0), F.Square, tag="fq")
-                act(ev, ev, F.Exp, scale=-2.0 ** -19, tag="fe")
-                tt(tv, IND("aw", 0, NW, C(of, (p * NV + a0) // 16, (p * NV + a1) // 16)), ev, A.mult, tag="mk s%d p%d" % (si, p))
-                yv = raw(T.y[:, a0:a1], reg=[("y", a0, a1, None)])
-                dma("g" if p else "s", yv, tv, 512 * (a1 - a0), add=p > 0, tag="y")
-                n += 1
+        who, sg = plan[3]
+        for n, (p, a0, a1) in enumerate(LAST):
+            cn = piece(k, of, p, a0, a1, who[n], n in sg)
+            e, tn = "e%d" % (n % 3), ("t0", "t3", "t4")[n % 3]
+            nb = 1024 * (n % 4)
+            for b0 in range(a0, a1, 512):
+                u = P(nb + b0 - a0, 512)
+                mm([(u, M("imk"), C("d2", p * NV + b0, p * NV + b0 + 512)), (u, M("i1"), C(cn, p * NV + b0, p * NV + b0 + 512))], tag="fu")
+            ev, tv = C(e, 0, a1 - a0), C(tn, 0, a1 - a0)
+            act(ev, P(nb, a1 - a0), F.Square, tag="fq")
+            act(ev, ev, F.Exp, scale=-2.0 ** -19, tag="fe")
+            tt(tv, IND("aw", 0, NW, C(of, (p * NV + a0) // 16, (p * NV + a1) // 16)), ev, A.mult, tag="mk a%d p%d" % (a0, p))
+            yv = raw(T.y[:, a0:a1], reg=[("y", a0, a1, None)])
+            dma("g" if p else "s", yv, tv, 512 * (a1 - a0), add=p > 0, tag="y")
 
     for t in range(RO):
         k = 3 * t
+        lanes(t, OF[1])
         sweep(k, OF[0])
         if t == 0:
             marks()
-        old = lanes(t, OF[1])
+        act(V("f1"), stress(k, 0), F.Identity, tag="f1")
         sweep(k + 1, OF[1])
-        tot = stress(k, False)
-        act(V("f1"), tot, F.Identity)
-        tot = stress(k + 2, True)
+        tot = stress(k + 2, 1)
+        votes(t, tot, OF[0])
         sweep(k + 2, OF[1])
-        votes(t, tot, old, OF[0])
     last(3 * RO, OF[0])
     return ops
 
 
-def emit(g, T, ops, order):
-    Q = {"g": g, "v": g.vector, "a": g.scalar, "p": g.tensor, "s": g.sync}
+def fix_stops(ops, order):
     lastacc = {}
     for i in order:
         o = ops[i]
@@ -626,6 +626,11 @@ def emit(g, T, ops, order):
             lastacc[o["acc"]] = o
     for o in lastacc.values():
         o["stop"][0] = True
+
+
+def emit(g, T, ops, order):
+    Q = {"g": g, "v": g.vector, "a": g.scalar, "p": g.tensor, "s": g.sync}
+    fix_stops(ops, order)
     mark, seq, grp, total = {}, {}, {}, {}
     nsem = [0]
     for i in order:
@@ -726,6 +731,10 @@ def emit(g, T, ops, order):
     return used
 
 
+def make_order(ops):
+    return schedule(ops, MODEL, BUMP)[0]
+
+
 ORDER = []
 
 
@@ -734,5 +743,5 @@ def rank_program(g, core, T, topo):
         return
     ops = build(g, core, T, topo, PLAN)
     if not ORDER:
-        ORDER.append(schedule(ops, MODEL, BUMP)[0])
+        ORDER.append(make_order(ops))
     emit(g, T, ops, ORDER[0])

@@ -10,13 +10,13 @@ CEN = 1024.0
 BIG = 8192.0
 SLOPE, TOPW = 17.625 / 16, 60.0
 I32, F32, F16, B16, U16 = "int32", "float32", "float16", "bfloat16", "uint16"
-MH = ["i1", "i16", "im64", "im1", "imk", "i161", "im527", "i4k", "l1", "l2", "l3", "lb", "lt", "luu", "lul"]
+MH = ["i1", "i16", "im64", "im16", "i64", "im1", "imk", "i161", "im527", "i4k", "l1", "l2", "l3", "lb", "lt", "luu", "lul"]
 MB = ["l4", "lpen", "lmu", "lml", "bo"]
 WH = ["xw1", "xwp", "xwm", "y2", "y3", "y6", "y10"]
 SB = {
     "w0": ([NW], I32), "w1": ([NW], I32), "w2": ([NW], I32), "w3": ([NW], I32),
     "tb": ([TW], F32), "aw": ([NW], B16),
-    "d1": ([4 * NV], F16), "d2": ([4 * NV], F16), "d3": ([4 * NV], F16), "xn0": ([NV], F16), "xn1": ([NV], F16),
+    "d1": ([4, NV], F16), "d2": ([4, NV], F16), "d3": ([4, NV], F16), "xn0": ([NV], F16), "xn1": ([NV], F16),
     "n32": ([664], I32), "na": ([664], F16), "nh": ([664], F16), "nf": ([4, TB], F32), "pf": ([4, TB], F32), "sf": ([2, TB], F32),
     "of0": ([640], U16), "of1": ([640], U16),
     "rs0": ([GH], I32), "rs1": ([GH], I32), "ra": ([GH], B16),
@@ -26,11 +26,11 @@ SB = {
     "tri": ([32], F32), "cw": ([8], F32), "thr": ([128], F32), "dum": ([32], F32), "cl": ([8], F16),
     "li": ([96], I32), "lu": ([72], U16), "mk": ([3, 384], B16), "hq": ([24], F16), "pbu": ([24], U16), "pb": ([24], F16),
     "t1": ([256], F16), "t2": ([128], F16), "plu": ([32], U16), "pl": ([32], F16), "gg": ([512], F16), "no1": ([512], F16),
-    "no": ([512], F16), "ee": ([256], B16), "fm": ([256], B16), "wh": ([4, 8], F32), "whu": ([48], U16), "ww": ([8], F32),
+    "no": ([512], F16), "ee": ([256], B16), "fm": ([256], B16), "wh": ([4, 8], F32), "whu": ([32], U16), "ww": ([8], F32),
     "rw": ([4, 128], F16), "q0": ([4, 128], B16), "q1": ([4, 128], B16), "q2": ([4, 128], B16),
     "lz": ([128], F16), "vz": ([128], F16), "ls": ([8], F16), "o2": ([32], F32), "ou": ([32], U16), "sl": ([96], U16),
     "xo": ([2, 512], F16), "sd": ([2, 1792], F16), "ss": ([2, 1792], F16), "sc": ([2, 1792], F16),
-    "sq0": ([512], F32), "sq1": ([512], F32), "f1": ([128], F32),
+    "sq": ([1024], F32), "f1": ([128], F32),
     "e0": ([1024], F32), "e1": ([1024], F32), "e2": ([1024], F32),
     "t0": ([1024], F32), "t3": ([1024], F32), "t4": ([1024], F32),
 }
@@ -38,20 +38,28 @@ SB["hq16"] = SB.pop("hq")
 SB["pl16"] = SB.pop("pl")
 SCRATCH = {k: ("sbuf", [128] + s, d) for k, (s, d) in SB.items()}
 SCRATCH["ps"] = ("psum", [128, 4096], F32)
+ONCE = ("mh", "mb", "wr", "y2b", "idf", "id2", "cb", "ones", "col", "mk", "aw")
 NSEM = 140
 SEMAPHORES = ["qv", "qa", "qp", "qg"] + ["arr%d" % i for i in range(11)] + ["m%d" % i for i in range(NSEM - 15)]
 
 MODEL = dict(cyc=0.95, ga=1.4, sc=3.5, pe=0.48, fix=60.0, hop=120.0, same=60.0, gi=900.0, si=100.0, dl=1800.0,
              bw=500.0, rl=2500.0, look=100.0)
 STR = [(0, 512), (512, 1536), (1536, 2560)]
-SBANK = [0, 1024, 0]
 GFILL = 1024
-PIECE = [(p, 0, 512) for p in range(4)] + [(p, 512, 2560) for p in range(2)] + [(p, a, a + 1024) for a in (512, 1536) for p in (2, 3)]
-LAST = [(0, 0, 512), (1, 0, 512), (0, 512, 1536), (0, 1536, 2560), (1, 512, 1536), (1, 1536, 2560), (2, 0, 512), (2, 512, 1536),
-        (2, 1536, 2560), (3, 512, 1536), (3, 1536, 2560), (3, 0, 512)]
-PLAN = {0: ("aaaaaaavaa", (0, 4, 8, 9)), 1: ("vvaaavvaaa", (0, 1, 8, 9)), 2: ("vavavaaava", (1, 2, 7, 8, 9)), 3: ("vvvavavaavva", (6, 7, 10, 11)),
-        4: ("aavv", (1,)), 5: ("vavv", ()), 6: ("vvvvaaaavv", (3, 5, 6, 7, 8))}
-BUMP = {"whu": 4000.0, "": -500.0, "fill": -3000.0, "m0": -1500.0, "fu": 12000.0, "arr": 500.0, "mask": 3500.0, "relist": -7000.0, "tab": 1000.0, "lose": 3500.0, "c": -500.0, "L1": 4500.0, "sl": 7500.0, "y": -2000.0, "pl": 7500.0, "relisted": -1000.0, "L2": 1000.0, "turn": 2000.0, "s": 500.0, "good": 8500.0, "ss": -500.0, "fe": 4000.0, "send": -8000.0, "sadd": -1000.0, "add": 1500.0, "wrap": -1000.0, "k": -1000.0, "xo": 500.0, "new": 1000.0}
+PIECES = {0: "001vvaaV 013aV 113aA 213aA 313aA 035aA 135aA 235aA 335aA",
+          1: "001vvvvV 013aV 113aV 213aV 313aV 035aV 135aA 235aA 335vV",
+          2: "001vvvvV 013aV 113aV 213aA 313aA 035aA 135aA 235aA 335vV",
+          3: "002vV 024vV 102vV 124aV 202aV 224aV 045aV 302aV 324aV 145aV 245aV 345aV",
+          6: "001vvvvV 013aV 113aA 213aA 313aA 035aA 135aA 235aA 335aA"}
+PLAN = {k: [(int(u[0]), 512 * int(u[1]), 512 * int(u[2]), u[3:-1], u[-1].lower()) for u in v.split()] for k, v in PIECES.items()}
+PLAN.update({"ys": "dddda", "re": "aa", 4: [("aa", "v"), ("v", "v")], 5: [("v", "v"), ("v", "v"), ("v", "v")],
+             "str": [(0, 512, 0), (512, 1536, 1024), (1536, 2048, 512), (2048, 2560, 0)]})
+BUMP = {"good": -2000.0, "send": 1000.0, "pl": -4000.0, "wrap": 500.0, "k": 1000.0, "fe": -1000.0, "vote": -1000.0, "fq": -1000.0, "tab": 5000.0}
+MODELS = [dict(MODEL, cyc=0.83, pe=0.42, ga=1.5, was=244e3), dict(MODEL, cyc=1.245, pe=0.63, ga=1.1, sc=6.0, hop=200.0, was=338e3),
+          dict(MODEL, cyc=1.2, pe=0.61, ga=1.95, gi=700.0, dl=1500.0, was=369e3),
+          dict(MODEL, cyc=0.87, pe=0.44, ga=1.3, gi=1100.0, dl=2200.0, bw=400.0, hop=200.0, rl=3000.0, was=269e3)]
+STARTS = [(c, a) for c in (0.83, 0.87, 0.91, 0.95, 1.0, 1.1) for a in (1.3, 1.4, 1.5, 1.7)]
+TRIES = 9000
 
 
 def cost(o, M):
@@ -129,6 +137,11 @@ def lists(ops, M, pr, back):
     return order, end
 
 
+def kindof(o):
+    w = o["tag"].split(" ")
+    return w[0] + (str(int(w[1][1:]) % 3 if w[1] != "k%d" % (3 * RO) else 9) if len(w) > 1 and w[1][0] == "k" else "")
+
+
 def schedule(ops, M, bump, rounds=3):
     pr = [0.0] * len(ops)
     succ = [[] for _ in ops]
@@ -137,7 +150,7 @@ def schedule(ops, M, bump, rounds=3):
             succ[j].append(o["i"])
     for o in reversed(ops):
         pr[o["i"]] = finish(o, cost(o, M), M, [0.0]) + max([pr[j] + delay(o, ops[j], M) for j in succ[o["i"]]] + [0.0])
-    add = [o.get("bump", 0.0) + bump.get(o["tag"].split(" ")[0], 0.0) for o in ops]
+    add = [o.get("bump", 0.0) + bump.get(kindof(o), 0.0) for o in ops]
     best = None
     for r in range(rounds):
         order, end = lists(ops, M, [p + a for p, a in zip(pr, add)], False)
@@ -161,10 +174,14 @@ def build(g, core, T, topo, plan):
             grids[name] = np.arange(int(np.prod(shp))).reshape(shp)
         el = grids[name][idx].reshape(-1) if idx else grids[name].reshape(-1)
         lo, hi = int(el.min()), int(el.max()) + 1
-        st = None if hi - lo == len(el) else frozenset(el.tolist())
+        cut = [0] + (np.nonzero(np.diff(el) != 1)[0] + 1).tolist() + [len(el)]
         if name == "ps":
-            lo, hi, st = lo // 512 * 512, (hi + 511) // 512 * 512, None
-        return dict(ap=T[name][(slice(None),) + idx], reg=[(name, lo, hi, st)], n=len(el), two=SCRATCH[name][2] in (F16, B16, U16),
+            reg = [(name, lo // 512 * 512, (hi + 511) // 512 * 512, None)]
+        elif len(cut) <= 5:
+            reg = [(name, int(el[a]), int(el[b - 1]) + 1, None) for a, b in zip(cut, cut[1:])]
+        else:
+            reg = [(name, lo, hi, frozenset(el.tolist()))]
+        return dict(ap=T[name][(slice(None),) + idx], reg=reg, n=len(el), two=SCRATCH[name][2] in (F16, B16, U16),
                     ps=name == "ps", ind=None)
 
     def C(name, a, b, s=None):
@@ -214,7 +231,8 @@ def build(g, core, T, topo, plan):
                     continue
                 keep.append(ent)
             book[name] = keep
-            new.append((name, (lo, hi, st, i, w, e, acc)))
+            if w or name not in ONCE:
+                new.append((name, (lo, hi, st, i, w, e, acc)))
         for name, ent in new:
             book.setdefault(name, []).append(ent)
         ops.append(dict(i=i, e=e, fn=fn, dep=dep, raw=raw, c=c, acc=acc, tag=tag, stop=[True]))
@@ -337,9 +355,9 @@ def build(g, core, T, topo, plan):
     for k, nm in enumerate(("pk", "pj", "pl", "hq")):
         dma("s", C("li", 24 * k, 24 * (k + 1)), raw(T[nm][:]), 128 * 96, grp="li")
     dma("s", C("w0", GH, NV), raw(T.x[:, GH:NV]), 128 * 4 * (NV - GH))
-    for (p, a0, a1), e in zip(PIECE, plan[6][0]):
-        if e == "v" and not any(u == "v" and (b0, b1) == (a0, a1) and q < p for (q, b0, b1), u in zip(PIECE, plan[6][0])):
-            dma("s", C("w2", a0, a1), raw(T.x[:, a0:a1]), 128 * 4 * (a1 - a0))
+    for a0 in range(0, NV, 512):
+        if any("v" in who and b0 <= a0 < b1 for _, b0, b1, who, _ in plan[6]):
+            dma("s", C("w2", a0, a0 + 512), raw(T.x[:, a0:a0 + 512]), 128 * 4 * 512, grp="w2")
     for o in ops:
         o["bump"] = o.get("bump", 0.0) + 1e5
     cp(V("of0"), C("n32", 0, 640), tag="of0")
@@ -384,9 +402,12 @@ def build(g, core, T, topo, plan):
             return act(out, in0, F.Identity, scale=s1, bias=s2, tag="k")
         return ts(out, in0, s1, s2, A.mult, o1, tag="k")
     ID, BO = (lambda a, s: C("idf", a, 128, s)), (lambda a, s: C("bof", a, 128, s))
-    for nm, val in (("i161", 161.0), ("im527", -527.0), ("imk", -1024.0), ("i16", 1.0 / 16), ("im64", -64.0), ("im1", -1.0), ("i1", 1.0),
+    for nm, val in (("i161", 161.0), ("im527", -527.0), ("imk", -1024.0), ("i16", 1.0 / 16), ("im64", -64.0), ("im16", -1.0 / 16), ("i64", 64.0), ("im1", -1.0), ("i1", 1.0),
                     ("i4k", 4096.0), ("id2", 2.0)):
-        kon(M(nm), V("idf"), val)
+        if nm in ("i161", "im527", "imk"):
+            kon(M(nm), V("idf"), val)
+        else:
+            sel(M(nm), C("tb", TW - 128, TW), [[-1, 128]], A.not_equal, val, 0, 1)
     kon(V("cb"), V("onef"), -7.5 / 16)
     kon(K(0), R4(2), -1.0, 1.0, A.add)
     kon(K(1), R4(2), 30000.0)
@@ -443,7 +464,7 @@ def build(g, core, T, topo, plan):
         act(R("mk", u), IND("cw", 0, 8, C("lu", 24 * u, 24 * u + 24)), F.Identity, tag="mask")
     act(V("hq16"), C("li", 72, 96), F.Identity, tag="k")
     for a0, a1 in STR:
-        act(C("xn0", a0, a1), C("w0", a0, a1), F.Identity, bias=2048.0, scale=-1.0, tag="xn")
+        act(C("xn0", a0, a1), C("w0", a0, a1), F.Identity, bias=-2048.0, tag="xn")
 
     def marks():
         dma("s", C("aw", 0, NV), raw(T.am[:]), 128 * 2 * NV)["rel"] = 40000.0
@@ -460,45 +481,60 @@ def build(g, core, T, topo, plan):
         ts(d, d, -2047.0, 2047.0, A.max, A.min, tag="c" + tag)
         return 0
 
-    def piece(k, of, p, a0, a1, who, sg):
-        win = IND(W[k % 4], 0, NW, C(of, (p * NV + a0) // 16, (p * NV + a1) // 16))
-        d, s, c = (C(u, p * NV + a0, p * NV + a1) for u in ("d1", "d2", "d3"))
-        tag = " k%d a%d p%d" % (k, a0, p)
-        if who == "v":
-            if k == 0:
-                tt(d, win, C("w2", a0, a1), A.subtract, tag="gv" + tag)
-            else:
-                tt(d, win, C(XN[k % 2], a0, a1), A.add, tag="gv" + tag)
+    def piece(k, of, p0, a0, a1, who, sg):
+        tag = " k%d a%d p%d" % (k, a0, p0)
+        for p, e in enumerate(who, p0):
+            win = IND(W[k % 4], 0, NW, C(of, (p * NV + a0) // 16, (p * NV + a1) // 16))
+            d = R("d1", p, a0, a1)
+            if e == "v":
+                tt(d, win, C(XN[k % 2] if k else "w2", a0, a1), A.subtract, tag="gv" + tag)
+                continue
+            act(d, win, F.Identity, bias=2048.0 if k == 0 else 0.0, scale=-1.0, tag="ga" + tag)
+            if e == "a":
+                dma("g", d, C(XN[k % 2], a0, a1), 256 * (a1 - a0), add=True, tag="add" + tag)
+                continue
+            o = 1024 if a0 >= 1536 and k < 3 * RO else B6
+            if a1 - a0 == 512:
+                o = 512 * (1 + p % 3) if a0 == 0 and k < 3 * RO else o + 512 * (p % 2)
+            for b in range(a0, a1, 512):
+                u = P(o + b - a0, 512)
+                mm([(u, M("i1"), R("d1", p, b, b + 512)), (u, M("i1"), C(XN[k % 2], b, b + 512))], tag="pd")
+            ts(R("d3", p, a0, a1), P(o, a1 - a0), -2047.0, 2047.0, A.max, A.min, tag="cp" + tag)
+        d, s, c = (V(u, slice(p0, p0 + len(who)), slice(a0, a1)) for u in ("d1", "d2", "d3"))
+        if who[0] != "p":
+            return ("d1", "d3")[clips(d, s, c, sg == "a", tag)]
+        if sg == "a":
+            act(s, c, F.Sign, tag="s" + tag)
         else:
-            act(d, win, F.Identity, bias=-2048.0 if k == 0 else 0.0, tag="ga" + tag)
-            dma("g", d, C(XN[k % 2], a0, a1), 256 * (a1 - a0), add=True, tag="add" + tag)
-        return ("d1", "d3")[clips(d, s, c, sg, tag)]
+            ts(s, c, -1.0, 1.0, A.max, A.min, tag="s" + tag)
+        return "d3"
 
     def sweep(k, of):
         wn, xn, xo = W[(k + 1) % 4], XN[(k + 1) % 2], XN[k % 2]
-        who, sg = plan[k % 3 if k else 6]
         cn = {}
-        for si, (a0, a1) in enumerate(STR):
+        for a0, a1, col in plan["str"]:
             blocks = [(b, min(b + 512, a1)) for b in range(a0, a1, 512)]
-            bank = [P(SBANK[si] + b0 - a0, b1 - b0) for b0, b1 in blocks]
+            bank = [P(col + b0 - a0, b1 - b0) for b0, b1 in blocks]
             for (b0, b1), ps in zip(blocks, bank):
-                mm([(ps, M("im1"), C(xo, b0, b1)),
+                mm([(ps, M("i1"), C(xo, b0, b1)),
                     (ps, raw(T.cb[0:1, :], reg=V("cb")["reg"]), raw(T.ones[0:1, 0:b1 - b0], n=b1 - b0, reg=V("ones")["reg"]))], stop=False, tag="m0")
-            for n, (p, c0, c1) in enumerate(PIECE):
+            for n, (p0, c0, c1, who, sg) in enumerate(plan[k % 3 if k else 6]):
                 if c1 <= a0 or a1 <= c0:
                     continue
                 if n not in cn:
-                    cn[n] = piece(k, of, p, c0, c1, who[n], n in sg)
-                for (b0, b1), ps in zip(blocks, bank):
-                    if c0 <= b0 < c1:
-                        mm([(ps, M("im64"), C("d2", p * NV + b0, p * NV + b1))], start=False, acc=(k, b0), tag="ms")
-                        mm([(ps, M("i16"), C(cn[n], p * NV + b0, p * NV + b1))], start=False, acc=(k, b0), tag="mc")
-            ts(C(wn, a0, a1), P(SBANK[si], a1 - a0), -2048.0, 2047.0, A.max, A.min, tag="fin k%d b%d" % (k, a0))
+                    cn[n] = piece(k, of, p0, c0, c1, who, sg)
+                for p, e in enumerate(who, p0):
+                    ms_, mc_ = ("im64", "i16") if e == "v" else ("i64", "im16")
+                    for (b0, b1), ps in zip(blocks, bank):
+                        if c0 <= b0 < c1:
+                            mm([(ps, M(ms_), R("d2", p, b0, b1))], start=False, acc=(k, b0), tag="ms")
+                            mm([(ps, M(mc_), R(cn[n], p, b0, b1))], start=False, acc=(k, b0), tag="mc")
+            ts(C(wn, a0, a1), P(col, a1 - a0), -2048.0, 2047.0, A.max, A.min, tag="fin k%d b%d" % (k, a0))
             if a0 == 0:
                 rs = "rs%d" % ((k + 1) % 2)
                 turn("ss", rs, (T[wn], C(wn, 0, GH)["reg"]), ("rs", k))
                 send(k + 1, C(wn, 0, GH), V(rs), wn, [C(W[(k + 2) % 4], NV, NW)], C(wn, NV, NW))
-            act(C(xn, a0, a1), C(wn, a0, a1), F.Identity, scale=-1.0, tag="xn k%d b%d" % (k, a0))
+            sel(C(xn, a0, a1), C(wn, a0, a1), [[0, a1 - a0]], A.is_gt, 0.0, 1, 0)["tag"] = "xn k%d b%d" % (k, a0)
 
     def put(skip, src, of, n):
         mm(skip, tag="wrap")
@@ -509,7 +545,10 @@ def build(g, core, T, topo, plan):
         cp(IND("tb", 0, TW, V("ou")), V(src), tag="scatter")
         for p in range(4):
             dma("s", R("nf", p), rows(4 * p), 150000, grp=("relist", n), tag="relist")
-        ts(V(of), V("nf", slice(None), slice(0, 160)), CEN, None, A.add, tag="relisted")
+        if plan["re"][n % 2] == "a":
+            act(V(of), V("nf", slice(None), slice(0, 160)), F.Identity, bias=CEN, tag="relisted")
+        else:
+            ts(V(of), V("nf", slice(None), slice(0, 160)), CEN, None, A.add, tag="relisted")
 
     def lanes(t, of):
         GA, GC, GB, GD = (C("gg", 128 * r, 128 * (r + 1)) for r in range(4))
@@ -535,8 +574,7 @@ def build(g, core, T, topo, plan):
         act(V("rw"), P(B5, 512), F.Identity, tag="rw")
         mm(wrap(P(B4, 32), "y3", "gg", 0, 32), tag="wrap")
         act(V("wh"), P(B4, 32), F.Identity, tag="rw")
-        ts(C("whu", 0, 32), V("wh"), CEN, None, A.add, tag="whu")
-        ts(C("whu", 32, 48), V("wh", slice(0, 4, 3)), CEN, None, A.add, tag="whu")
+        ts(V("whu"), V("wh"), CEN, None, A.add, tag="whu")
         mm(wrap(P(B4, 8), "y2b", "fm", 0, 8) + wrap(P(B4, 8), "y2b", "fm", 128, 8) + [(P(B4, 8), M("i1"), V("cl"))], tag="good")
         act(V("ww"), P(B4, 8), F.Exp, scale=256.0, bias=K(4), tag="good")
         for o, lu, lm in ((B6, "luu", "lmu"), (B7, "lul", "lml")):
@@ -557,50 +595,104 @@ def build(g, core, T, topo, plan):
         ts(V("sl"), P(B4 + 128, 96), CEN, None, A.add, tag="sl")
 
     def stress(k, z):
-        w = W[k % 4]
+        w, at = W[k % 4], " k%d" % k
         off = 2048.0 if k == 0 else 0.0
-        act(R("xo", z), IND(w, 0, NW, C("whu", 0, 32)), F.Identity, bias=off, scale=-1.0, tag="xo")
-        who, sg = plan[4 + z]
-        who = "aaaa" if k == 0 else who
-        part = [(512 * p, 512, C("sl", 32 * p, 32 * p + 32), R("xo", z)) for p in range(3)]
-        part.append((1536, 256, C("whu", 16 + 16 * z, 32 + 16 * z), R("xo", z, 128 * z, 128 * z + 256)))
+        own = R("xo", z)
+        act(own, IND(w, 0, NW, C("whu", 0, 32)), F.Identity, bias=off, scale=-1.0, tag="xo" + at)
         tot = P(B5, 128)
-        for n in (3, 0, 1, 2):
-            a, m, lst, own = part[n]
-            d, s, c = (R(u, z, a, a + m) for u in ("sd", "ss", "sc"))
-            if who[n] == "v":
-                tt(d, IND(w, 0, NW, lst), own, A.add, tag="sg")
+        units = plan[4 + z]
+
+        def squares(a, m, c, bank, first, last):
+            sq = C("sq", bank - B6, bank - B6 + m)
+            for b in range(0, m, 512):
+                u = P(bank + b, min(512, m - b))
+                mm([(u, M("imk"), R("ss", z, a + b, a + b + u["n"])), (u, M("i1"), R(c, z, a + b, a + b + u["n"]))], tag="su" + at)
+            act(sq, P(bank, m), F.Square, tag="sq" + at)
+            mm([(tot, V("id2" if first else "idf"), C("sq", b, b + 128)) for b in range(bank - B6, bank - B6 + m, 128)],
+               start=first, stop=last, wide=4, tag="st" + at)
+
+        def from_psum(a, m, u, sg):
+            s, c = R("ss", z, a, a + m), R("sc", z, a, a + m)
+            ts(c, u, -2047.0, 2047.0, A.max, A.min, tag="cs" + at)
+            if sg == "a":
+                act(s, c, F.Sign, tag="ss" + at)
             else:
-                act(d, IND(w, 0, NW, lst), F.Identity, bias=-off, tag="sa")
-                dma("g", d, own, 256 * m, add=True, tag="sadd")
-            c = (d, c)[clips(d, s, c, n in sg, "s")]
-            u = P(B6 + 512 * (n % 2), m)
-            mm([(u, M("imk"), s), (u, M("i1"), c)], tag="su")
-            sq = "sq%d" % (n % 2)
-            act(C(sq, 0, m), u, F.Square, tag="sq")
-            mm([(tot, V("id2" if n == 3 else "idf"), C(sq, b, b + 128)) for b in range(0, m, 128)], start=n == 3, stop=n == 2, wide=4, tag="st")
+                ts(s, c, -1.0, 1.0, A.max, A.min, tag="ss" + at)
+        u = P(B7, 256)
+        mm([(u, M("i1"), R("xo", z, 128 * z, 128 * z + 256))]
+           + [(P(B7 + 128 * j, 128), M("im1"), R("xo", z, 128 * r, 128 * r + 128)) for j, r in enumerate(((2, 3), (0, 3))[z])], tag="sp" + at)
+        from_psum(1536, 256, u, "v")
+        squares(1536, 256, "sc", B7, True, False)
+        p0 = 0
+        for who, sg in units:
+            who = who if k else who.replace("v", "a")
+            a, m = 512 * p0, 512 * len(who)
+            if "v" not in who:
+                act(R("sd", z, a, a + m), IND(w, 0, NW, C("sl", a // 16, (a + m) // 16)), F.Identity, bias=-off, tag="sa" + at)
+            for p, e in enumerate(who, p0):
+                d, lst = R("sd", z, 512 * p, 512 * p + 512), IND(w, 0, NW, C("sl", 32 * p, 32 * p + 32))
+                if e == "v":
+                    tt(d, lst, own, A.add, tag="sg" + at)
+                    continue
+                if "v" in who:
+                    act(d, lst, F.Identity, bias=-off, tag="sa" + at)
+                if e == "a":
+                    dma("g", d, own, 256 * 512, add=True, tag="sadd" + at)
+                else:
+                    u = P(B6 + 512 * (p % 2), 512)
+                    mm([(u, M("i1"), d), (u, M("i1"), own)], tag="sp" + at)
+                    from_psum(512 * p, 512, u, sg)
+            c = "sc"
+            if who[0] != "p":
+                c = ("sd", "sc")[clips(*(R(u, z, a, a + m) for u in ("sd", "ss", "sc")), sg == "a", "s" + at)]
+            p = p0
+            while p < p0 + len(who):
+                n = 2 if p % 2 == 0 and p + 2 <= p0 + len(who) else 1
+                squares(512 * p, 512 * n, c, B6 + 512 * (p % 2), False, p + n == 3)
+                p += n
+            p0 += len(who)
         return tot
 
     def votes(t, tot, of):
         tt(V("vz"), tot, V("f1"), A.is_gt, tag="vote")
         o = P(B4 + 64, 8)
-        put(wrap(o, "xwp", "lz", 0, 8) + [(o, M("i4k"), C("hq16", 8 * t, 8 * t + 8))] + wrap(o, "xwm", "vz", 0, 8), "gg", of, 2 * t + 1)
+        put([(o, M("i64"), V("ls")), (o, M("i4k"), C("hq16", 8 * t, 8 * t + 8))] + wrap(o, "xwm", "vz", 0, 8), "gg", of, 2 * t + 1)
 
     def last(k, of):
-        who, sg = plan[3]
-        for n, (p, a0, a1) in enumerate(LAST):
-            cn = piece(k, of, p, a0, a1, who[n], n in sg)
-            e, tn = "e%d" % (n % 3), ("t0", "t3", "t4")[n % 3]
-            nb = 1024 * (n % 4)
+        bank = {}
+        for n, (p, a0, a1, who, sg) in enumerate(plan[3]):
+            cn = piece(k, of, p, a0, a1, who, sg)
+            e, (tn, t0) = "e%d" % (n % 3), (("t0", 0), ("t3", 0), ("t4", 0), ("tb", 0), ("tb", 1024), ("tb", 2048))[n % 6]
+            nb = 1024 * (n % 3)
             for b0 in range(a0, a1, 512):
                 u = P(nb + b0 - a0, 512)
-                mm([(u, M("imk"), C("d2", p * NV + b0, p * NV + b0 + 512)), (u, M("i1"), C(cn, p * NV + b0, p * NV + b0 + 512))], tag="fu")
-            ev, tv = C(e, 0, a1 - a0), C(tn, 0, a1 - a0)
+                mm([(u, M("imk"), R("d2", p, b0, b0 + 512)), (u, M("i1"), R(cn, p, b0, b0 + 512))], tag="fu")
+            ev, tv = C(e, 0, a1 - a0), C(tn, t0, t0 + a1 - a0)
             act(ev, P(nb, a1 - a0), F.Square, tag="fq")
             act(ev, ev, F.Exp, scale=-2.0 ** -19, tag="fe")
             tt(tv, IND("aw", 0, NW, C(of, (p * NV + a0) // 16, (p * NV + a1) // 16)), ev, A.mult, tag="mk a%d p%d" % (a0, p))
-            yv = raw(T.y[:, a0:a1], reg=[("y", a0, a1, None)])
-            dma("g" if p else "s", yv, tv, 512 * (a1 - a0), add=p > 0, tag="y")
+            if plan["ys"][a0 // 512] == "d":
+                yv = raw(T.y[:, a0:a1], reg=[("y", a0, a1, None)])
+                dma("g" if p else "s", yv, tv, 512 * (a1 - a0), add=p > 0, tag="y")
+                continue
+            for b0 in range(a0, a1, 512):
+                new = b0 not in bank
+                bank.setdefault(b0, [B6 + 512 * (len(bank) % 2), 0])[1] += 1
+                mm([(P(bank[b0][0], 512), V("idf"), C(tn, t0 + b0 - a0, t0 + b0 - a0 + 512))], start=new, stop=False, acc=None if new else ("y", b0),
+                   wide=4, tag="ys")
+            done = [b0 for b0 in range(a0, a1, 512) if bank[b0][1] == 4]
+            if len(done) == 2 and bank[done[1]][0] == bank[done[0]][0] + 512:
+                done = [done]
+            else:
+                done = [[b0] for b0 in done]
+            for bs in done:
+                b0, b1 = bs[0], bs[-1] + 512
+                yo = C("sq", bank[b0][0] - B6, bank[b0][0] - B6 + b1 - b0)
+                if plan["ys"][b0 // 512] == "a":
+                    act(yo, P(bank[b0][0], b1 - b0), F.Identity, tag="yc")
+                else:
+                    cp(yo, P(bank[b0][0], b1 - b0), tag="yc")
+                dma("s", raw(T.y[:, b0:b1], reg=[("y", b0, b1, None)]), yo, 512 * (b1 - b0), tag="y")
 
     for t in range(RO):
         k = 3 * t
@@ -731,8 +823,126 @@ def emit(g, T, ops, order):
     return used
 
 
-def make_order(ops):
-    return schedule(ops, MODEL, BUMP)[0]
+def polish(ops, order, models, tries, seed=1):
+    n = len(ops)
+    eng = ["vapgsx".index(o["e"]) for o in ops]
+    succ = [[] for _ in ops]
+    for o in ops:
+        for j in o["dep"]:
+            succ[j].append(o["i"])
+    tab = [([cost(o, M) for o in ops], [[(j, delay(ops[j], o, M)) for j in o["dep"]] for o in ops],
+            [[(j, delay(o, ops[j], M)) for j in succ[o["i"]]] for o in ops],
+            [o["c"][1] / M["bw"] if o["c"][0] == "dma" else -1.0 for o in ops], [finish(o, 0.0, M, [0.0]) for o in ops], M["dl"]) for M in models]
+    rel = [o.get("rel", 0.0) if o["c"][0] == "arr" else 0.0 for o in ops]
+    state = [seed]
+
+    def draw(m):
+        state[0] = (state[0] * 1103515245 + 12345) % 2 ** 31
+        return (state[0] >> 8) % m
+
+    def run(order, tb, a=0, old=None):
+        co, dp, _, mv, la, dl = tb
+        e, f, why, back = [list(u) for u in old] if old else [[0.0] * n for _ in range(4)]
+        free, last, st = [0.0] * 6, [-1] * 6, back[order[a - 1]] if a else 0.0
+        for i in order[max(0, a - 200):a]:
+            free[eng[i]], last[eng[i]] = f[i], i
+        free[5], last[5] = 0.0, -1
+        for i in order[a:]:
+            q = eng[i]
+            t, w = free[q], last[q]
+            if rel[i] > t:
+                t, w = rel[i], -1
+            for j, d in dp[i]:
+                if e[j] + d > t:
+                    t, w = e[j] + d, -2 - j
+            t += co[i]
+            f[i], why[i] = t, w
+            if q != 5:
+                free[q], last[q] = t, i
+            if mv[i] >= 0:
+                st = max(st, t + dl * 0.7) + mv[i]
+                e[i] = st + dl * 0.3
+            else:
+                e[i] = t + la[i]
+            back[i] = st
+        return e, f, why, back
+
+    def adopt(order, rs):
+        pairs, tails = [], []
+        for (co, _, sc, _, _, _), (e, f, why, _) in zip(tab, rs):
+            i = e.index(max(e))
+            while why[i] != -1:
+                if why[i] >= 0:
+                    pairs.append((why[i], i))
+                i = why[i] if why[i] >= 0 else -2 - why[i]
+            q, nx = [0.0] * n, [0.0] * 6
+            for i in reversed(order):
+                t = 0.0
+                for j, d in sc[i]:
+                    if q[j] + d > t:
+                        t = q[j] + d
+                t += e[i] - f[i]
+                if eng[i] != 5:
+                    t = max(t, nx[eng[i]])
+                    nx[eng[i]] = t + co[i]
+                q[i] = t + co[i]
+            tails.append(q)
+        pos, prev, nxt, last = [0] * n, [-1] * n, [-1] * n, [-1] * 6
+        for k, v in enumerate(order):
+            pos[v], prev[v] = k, last[eng[v]]
+            if prev[v] >= 0:
+                nxt[prev[v]] = v
+            last[eng[v]] = v
+        return pairs, tails, pos, prev, nxt
+
+    def score(ms):
+        return sum(m / M["was"] for m, M in zip(ms, models)) / len(ms) + max(m / M["was"] for m, M in zip(ms, models))
+    rs = [run(order, tb) for tb in tab]
+    ms = [max(r[0]) for r in rs]
+    pairs, tails, pos, prev, nxt = adopt(order, rs)
+    for _ in range(tries):
+        j, i = pairs[draw(len(pairs))]
+        early = draw(2)
+        for _ in range((0, 0, 1, 2, 3, 5)[draw(6)]):
+            j = prev[j] if early and prev[j] >= 0 else j
+            i = nxt[i] if not early and nxt[i] >= 0 else i
+        a, b = pos[j], pos[i]
+        seg = order[a:b + 1]
+        tied = {i if early else j}
+        for v in (reversed(seg) if early else seg):
+            if v in tied:
+                tied.update(ops[v]["dep"] if early else succ[v])
+        if (j if early else i) in tied:
+            continue
+        new = [v for v in seg if (v in tied) == early] + [v for v in seg if (v in tied) != early]
+        first, end, est = {}, {}, []
+        for v in seg:
+            first.setdefault(eng[v], v)
+            end[eng[v]] = v
+        for (co, dp, sc, _, _, _), (e, f, _, _), q in zip(tab, rs, tails):
+            free = {u: (f[prev[v]] if prev[v] >= 0 and u != 5 else 0.0) for u, v in first.items()}
+            e2, top = {}, 0.0
+            for v in new:
+                t = max([free[eng[v]], rel[v]] + [e2.get(u, e[u]) + d for u, d in dp[v]]) + co[v]
+                if eng[v] != 5:
+                    free[eng[v]] = t
+                e2[v] = t = t + e[v] - f[v]
+                top = max([top, t] + [t + d + q[u] for u, d in sc[v] if pos[u] > b])
+            est.append(max([top] + [free[u] + q[nxt[v]] for u, v in end.items() if u != 5 and nxt[v] >= 0]))
+        if score(est) > score(ms) or (all(abs(x - m) < 1 for x, m in zip(est, ms)) and draw(5)):
+            continue
+        o2 = order[:a] + new + order[b + 1:]
+        r2 = [run(o2, tb, a, r) for tb, r in zip(tab, rs)]
+        m2 = [max(r[0]) for r in r2]
+        if score(m2) <= score(ms):
+            order, rs, ms = o2, r2, m2
+            pairs, tails, pos, prev, nxt = adopt(order, rs)
+    return order, score(ms)
+
+
+def make_order(ops, tries=None):
+    best = min((polish(ops, schedule(ops, dict(MODEL, cyc=c, pe=c / 2, ga=a), BUMP, 4)[0], MODELS, 0) for c, a in STARTS), key=lambda r: r[1])
+    return polish(ops, best[0], MODELS, TRIES if tries is None else tries)[0]
 
 
 ORDER = []

@@ -5,10 +5,11 @@ from concourse.mybir import AluOpType as A, ActivationFunctionType as F
 
 NV, GH, NW, RO = 2560, 256, 3072, 3
 DSH = [1, 3]
-TB, TREAL, TW = 161, 16 * 161, 3200
+TB, TREAL, TW = 161, 16 * 161, 3224
 CEN = 1024.0
 BIG = 8192.0
 SLOPE, TOPW = 17.625 / 16, 60.0
+NQ = 6
 I32, F32, F16, B16, U16 = "int32", "float32", "float16", "bfloat16", "uint16"
 MH = ["i1", "i16", "im64", "im16", "i64", "im1", "imk", "i161", "im527", "i4k", "l1", "l2", "l3", "lb", "lt", "luu", "lul"]
 MB = ["l4", "lpen", "lmu", "lml", "bo"]
@@ -17,49 +18,62 @@ SB = {
     "w0": ([NW], I32), "w1": ([NW], I32), "w2": ([NW], I32), "w3": ([NW], I32),
     "tb": ([TW], F32), "aw": ([NW], B16),
     "d1": ([4, NV], F16), "d2": ([4, NV], F16), "d3": ([4, NV], F16), "xn0": ([NV], F16), "xn1": ([NV], F16),
-    "n32": ([664], I32), "na": ([664], F16), "nh": ([664], F16), "nf": ([4, TB], F32), "pf": ([4, TB], F32), "sf": ([2, TB], F32),
+    "n32": ([664], I32), "nf": ([4, TB], F32), "pf": ([4, TB], F32), "sf": ([2, TB], F32),
     "of0": ([640], U16), "of1": ([640], U16),
     "rs0": ([GH], I32), "rs1": ([GH], I32), "ra": ([GH], B16),
     "mh": ([len(MH), 128], F16), "mb": ([len(MB), 128], B16), "wr": ([len(WH), 144], F16), "y2b": ([144], B16),
     "onef": ([128], F32), "idf": ([128], F32), "id2": ([128], F32), "bof": ([128], F32), "cb": ([128], F16), "ones": ([512], F16),
     "cf": ([TB], F32), "ki": ([2], I32), "kf": ([2], F32), "p16": ([16], F32), "r4": ([4], F32), "col": ([16], F32),
     "tri": ([32], F32), "cw": ([8], F32), "thr": ([128], F32), "dum": ([32], F32), "cl": ([8], F16),
-    "li": ([96], I32), "lu": ([72], U16), "mk": ([3, 384], B16), "hq": ([24], F16), "pbu": ([24], U16), "pb": ([24], F16),
-    "t1": ([256], F16), "t2": ([128], F16), "plu": ([32], U16), "pl": ([32], F16), "gg": ([512], F16), "no1": ([512], F16),
-    "no": ([512], F16), "ee": ([256], B16), "fm": ([256], B16), "wh": ([4, 8], F32), "whu": ([32], U16), "ww": ([8], F32),
-    "rw": ([4, 128], F16), "q0": ([4, 128], B16), "q1": ([4, 128], B16), "q2": ([4, 128], B16),
-    "lz": ([128], F16), "vz": ([128], F16), "ls": ([8], F16), "o2": ([32], F32), "ou": ([32], U16), "sl": ([96], U16),
-    "xo": ([2, 512], F16), "sd": ([2, 1792], F16), "ss": ([2, 1792], F16), "sc": ([2, 1792], F16),
+    "li": ([96], I32), "lu": ([3, 24], U16), "mk": ([3 * 384], B16), "hq16": ([24], F16), "pbu": ([24], U16), "pb": ([24], F16),
+    "t1": ([256], F16), "t2": ([128], F16), "plu": ([32], U16), "pl16": ([32], F16), "gg": ([512], F16), "no1": ([512], F16),
+    "no": ([512], F16), "ee": ([256], B16), "fm": ([256], B16), "wh": ([4, 8], F32), "ww": ([8], F32),
+    "rw": ([4, 128], F16), "qq": ([NQ * 4, 128], B16),
+    "lz": ([128], F16), "vz": ([128], F16), "ls": ([8], F16), "neg": ([32], F16), "ou": ([32], U16), "sl": ([128], U16),
+    "xo": ([2, 512], F16), "sd": ([1792], F16), "ss": ([1792], F16), "sc": ([1792], F16),
     "sq": ([1024], F32), "f1": ([128], F32),
-    "e0": ([1024], F32), "e1": ([1024], F32), "e2": ([1024], F32),
+    "eq": ([3, 1024], U16), "e0": ([1024], F32), "e1": ([1024], F32), "e2": ([1024], F32),
     "t0": ([1024], F32), "t3": ([1024], F32), "t4": ([1024], F32),
 }
-SB["hq16"] = SB.pop("hq")
-SB["pl16"] = SB.pop("pl")
 SCRATCH = {k: ("sbuf", [128] + s, d) for k, (s, d) in SB.items()}
 SCRATCH["ps"] = ("psum", [128, 4096], F32)
 ONCE = ("mh", "mb", "wr", "y2b", "idf", "id2", "cb", "ones", "col", "mk", "aw")
-NSEM = 140
-SEMAPHORES = ["qv", "qa", "qp", "qg"] + ["arr%d" % i for i in range(11)] + ["m%d" % i for i in range(NSEM - 15)]
+ARR = ["arr%d" % i for i in range(11)]
+SEMAPHORES = ["qv", "qa", "qp", "qg"] + ARR + ["m%d" % i for i in range(146 - len(ARR))]
 
 MODEL = dict(cyc=0.95, ga=1.4, sc=3.5, pe=0.48, fix=60.0, hop=120.0, same=60.0, gi=900.0, si=100.0, dl=1800.0,
-             bw=500.0, rl=2500.0, look=100.0)
+             bw=500.0, rl=2500.0, look={})
 STR = [(0, 512), (512, 1536), (1536, 2560)]
-GFILL = 1024
-PIECES = {0: "001vvaaV 013aV 113aA 213aA 313aA 035aA 135aA 235aA 335aA",
-          1: "001vvvvV 013aV 113aV 213aV 313aV 035aV 135aA 235aA 335vV",
-          2: "001vvvvV 013aV 113aV 213aA 313aA 035aA 135aA 235aA 335vV",
-          3: "002vV 024vV 102vV 124aV 202aV 224aV 045aV 302aV 324aV 145aV 245aV 345aV",
-          6: "001vvvvV 013aV 113aA 213aA 313aA 035aA 135aA 235aA 335aA"}
-PLAN = {k: [(int(u[0]), 512 * int(u[1]), 512 * int(u[2]), u[3:-1], u[-1].lower()) for u in v.split()] for k, v in PIECES.items()}
-PLAN.update({"ys": "dddda", "re": "aa", 4: [("aa", "v"), ("v", "v")], 5: [("v", "v"), ("v", "v"), ("v", "v")],
-             "str": [(0, 512, 0), (512, 1536, 1024), (1536, 2048, 512), (2048, 2560, 0)]})
+PIECES = {0: "002vvvvV 026aA 126aV 226aA 326aA 06aaA 16aaA 26aaA+ 36aaA+",
+          1: "002vvvvV 026aV 126aV 226aV 326aV 06aaA 16aaA 26aaA+ 36avV",
+          2: "002vvvvV 026aV 126vV 226aA 326aA 06aaA 16aaA 26aaA+ 36aaA",
+          3: "002avvvV 026aV 126aA 226aA 326aA 06aaA 16aaA 26aaA+ 36aaA+",
+          9: "004vV 048vV 104vV 148aV 204aV 248vV 08aaV 304aV 348aV 18avV 28aaV 38avV"}
+for _k in range(4, 9):
+    PIECES[_k] = PIECES[_k - 3]
+ENG = {"pl": "vvv", "rw": "avavav", "old": "aaa", "sl": "aaa", "f1": "aaa", "relisted": "aaaaaaaaaaaa", "of0": "v", "xn": "avv",
+       "ss": "vavvvavvvavvvvvvvvvvvvvv", "sa": "aaavvvaavvvvaavvvv"}
+
+
+def make_plan(pieces, eng=None, **more):
+    plan = {k: [(int(u[0]), 256 * int(u[1], 16), 256 * int(u[2], 16), u[3:].rstrip("+")[:-1], u.rstrip("+")[-1].lower(), 1 + u.count("+"))
+                for u in v.split()] for k, v in pieces.items()}
+    plan.update({"cast": [(0, 512), (512, 1536), (1536, 2560)], "pb": (3072, 3584), "ys": 2048, "yc": "v", "halves": 2, "merge": True,
+                 "st": [(0, 768, 1792), (0, 768, 1792)], "eng": dict(ENG, **(eng or {})),
+                 "str": [(0, 512, 0), (512, 1536, 1024), (1536, 2048, 512), (2048, 2560, 0)]})
+    plan.update(more)
+    return plan
+
+
+PLAN = make_plan(PIECES)
 BUMP = {"good": -2000.0, "send": 1000.0, "pl": -4000.0, "wrap": 500.0, "k": 1000.0, "fe": -1000.0, "vote": -1000.0, "fq": -1000.0, "tab": 5000.0}
-MODELS = [dict(MODEL, cyc=0.83, pe=0.42, ga=1.5, was=244e3), dict(MODEL, cyc=1.245, pe=0.63, ga=1.1, sc=6.0, hop=200.0, was=338e3),
-          dict(MODEL, cyc=1.2, pe=0.61, ga=1.95, gi=700.0, dl=1500.0, was=369e3),
-          dict(MODEL, cyc=0.87, pe=0.44, ga=1.3, gi=1100.0, dl=2200.0, bw=400.0, hop=200.0, rl=3000.0, was=269e3)]
+MODELS = [dict(MODEL, cyc=0.83, pe=0.42, ga=1.5, was=228e3), dict(MODEL, cyc=1.245, pe=0.63, ga=1.1, sc=6.0, hop=200.0, was=320e3),
+          dict(MODEL, cyc=1.245, pe=0.63, ga=2.08, sc=4.0, was=379e3),
+          dict(MODEL, cyc=0.9, pe=0.45, ga=1.15, sc=2.0, gi=1100.0, dl=2300.0, bw=420.0, rl=3000.0, fix=50.0, hop=150.0, was=245e3),
+          dict(MODEL, cyc=1.04, pe=0.55, ga=1.56, sc=3.8, fix=80.0, hop=180.0, same=90.0, was=291e3)]
 STARTS = [(c, a) for c in (0.83, 0.87, 0.91, 0.95, 1.0, 1.1) for a in (1.3, 1.4, 1.5, 1.7)]
-TRIES = 9000
+MID = dict(MODEL, cyc=0.9, pe=0.45, ga=1.45, look={"g": 500, "a": 300})
+PASSES, SEED = 100, 1
 
 
 def cost(o, M):
@@ -82,21 +96,23 @@ def cost(o, M):
     return 0.0
 
 
+def start_up(o, M):
+    return M["dl"] if o["c"][0] == "dma" else M["rl"] * 0.8
+
+
 def finish(o, t, M, st):
     k, n = o["c"]
-    if k == "dma":
-        st[0] = max(st[0], t + M["dl"] * 0.7) + n / M["bw"]
-        return st[0] + M["dl"] * 0.3
+    if k in ("dma", "rem"):
+        st[0] = max(st[0], t + start_up(o, M) * 0.7) + n / M["bw"]
+        return st[0] + start_up(o, M) * 0.3
     if k == "arr":
-        return t + M["rl"] * 0.5
-    if k == "rem":
-        return t + M["rl"] * 0.8
+        return t + M["rl"] * 0.3
     return t
 
 
 def delay(d, o, M):
     if d["e"] == o["e"] and d["c"][0] not in ("dma", "rem"):
-        return 0.0 if (d["e"] == "p" or d["i"] not in o["raw"]) else M["same"]
+        return 0.0 if d["e"] == "p" else M["same"]
     return M["hop"]
 
 
@@ -121,7 +137,7 @@ def lists(ops, M, pr, back):
     order, st, end = [], [0.0], [0.0] * n
     while len(order) < n:
         t, e = min((max(free[e], min(rdy[i] for i in lst)), e) for e, lst in pool.items() if lst)
-        i = max((j for j in pool[e] if rdy[j] <= t + M["look"]), key=lambda j: (pr[j], -j))
+        i = max((j for j in pool[e] if rdy[j] <= t + M["look"].get(e, 100.0)), key=lambda j: (pr[j], -j))
         pool[e].remove(i)
         t1 = max(t, rdy[i]) + co[i]
         if e != "x":
@@ -273,6 +289,15 @@ def build(g, core, T, topo, plan):
         return op("a", lambda: g.scalar.activation(out["ap"], in0["ap"], f, bias=aps(bias), scale=aps(scale)), [in0] + sc_rd(bias, scale),
                   [out], kind(out, [in0], 1.0), tag=tag)
 
+    turns = {}
+
+    def E(name):
+        turns[name] = turns.get(name, -1) + 1
+        return plan["eng"][name][turns[name]]
+
+    def plus(out, in0, c, tag):
+        return ts(out, in0, c, None, A.add, tag=tag) if E(tag) == "v" else act(out, in0, F.Identity, bias=c, tag=tag)
+
     def iota(out, pattern, base, mult, whole=False):
         def fn():
             if whole:
@@ -310,23 +335,28 @@ def build(g, core, T, topo, plan):
         o["grp"] = grp
         return o
 
-    def send(j, src0, src1, dname, guard, arrive):
+    landed = {}
+
+    def remote(sem, moves, guard, nbytes, tag):
+        n = len(moves)
+
         def fn(lsem):
             tr = []
-            for b, src in enumerate((src0, src1)):
-                dst = cores[(rank + DSH[b]) % nr]
+            for b, (dst, _, srcs, alu, out) in enumerate(moves):
                 rid, pid, _ = topo.addr(dst)
-                tr.append(RemoteDMATransfer(dst_ids=[DstId(rid=rid, pnc=pid)], dma_engine_mask=sum(1 << u for u in topo.engines(core, dst)[b::2]),
-                                            remote_sem=T.sem["arr%d" % j], src=src["ap"],
-                                            dst=C(dname, NV + b * GH, NV + (b + 1) * GH)["ap"]))
+                tr.append(RemoteDMATransfer(dst_ids=[DstId(rid=rid, pnc=pid)], dma_engine_mask=sum(1 << u for u in topo.engines(core, dst)[b::n]),
+                                            remote_sem=T.sem[sem], srcs=[s["ap"] for s in srcs], dsts=[out["ap"]], alu_op=alu))
             g.remote_dma_fused(tr, local_sem=lsem)
-        cnt = sum(len(topo.engines(core, cores[(rank + d) % nr])) // 2 for d in DSH)
-        got = sum(len(topo.engines(cores[(rank - d) % nr], core)) // 2 for d in DSH)
-        o = op("g", fn, [src0, src1], guard, ("rem", 0), tag="send %d" % j)
-        o["cnt"] = cnt
-        a = op("x", None, [], [arrive], ("arr", 0), tag="arr %d" % j)
+        o = op("g", fn, [s for m in moves for s in m[2]], guard, ("rem", nbytes), tag=tag)
+        o["cnt"] = sum(len(topo.engines(core, m[0])) // n for m in moves)
+        landed[sem] = landed.get(sem, 0) + sum(len(topo.engines(m[1], core)) // n for m in moves)
+        a = op("x", None, [], [m[4] for m in moves], ("arr", 0), tag="arr " + tag)
         a["dep"].add(o["i"])
-        a["sem"] = ("arr%d" % j, got)
+        a["sem"] = (sem, landed[sem])
+
+    def send(j, src0, src1, dname, guard):
+        remote("arr%d" % j, [(cores[(rank + DSH[b]) % nr], cores[(rank - DSH[b]) % nr], [src], 0, C(dname, NV + b * GH, NV + (b + 1) * GH))
+                             for b, src in enumerate((src0, src1))], guard, 256 * 1024, "send %d" % j)
 
     def turn(qs, name, src, grp, tag="turn"):
         nb_ = 2 if SCRATCH[name][2] == B16 else 4
@@ -346,8 +376,8 @@ def build(g, core, T, topo, plan):
 
     dma("s", C("w0", 0, GH), raw(T.x[:, 0:GH]), 128 * 1024)
     turn("as", "rs0", (T.x, []), "rs")
-    send(0, C("w0", 0, GH), V("rs0"), "w0", [], C("w0", NV, NW))
-    ops[-1]["rel"] = 7000.0
+    send(0, C("w0", 0, GH), V("rs0"), "w0", [])
+    ops[-1]["rel"] = 7500.0
     dma("a", C("n32", 0, 640), raw(T.nb[:]), 128 * 2560, grp="n32")
     dma("s", C("n32", 640, 664), raw(T.lb[:]), 128 * 96, grp="n32")
     for o in ops:
@@ -355,22 +385,22 @@ def build(g, core, T, topo, plan):
     for k, nm in enumerate(("pk", "pj", "pl", "hq")):
         dma("s", C("li", 24 * k, 24 * (k + 1)), raw(T[nm][:]), 128 * 96, grp="li")
     dma("s", C("w0", GH, NV), raw(T.x[:, GH:NV]), 128 * 4 * (NV - GH))
-    for a0 in range(0, NV, 512):
-        if any("v" in who and b0 <= a0 < b1 for _, b0, b1, who, _ in plan[6]):
-            dma("s", C("w2", a0, a0 + 512), raw(T.x[:, a0:a0 + 512]), 128 * 4 * 512, grp="w2")
+    for a0, a1 in sorted({u[1:3] for u in plan[0] if "v" in u[3]}):
+        dma("s", C("w2", a0, a1), raw(T.x[:, a0:a1]), 128 * 4 * (a1 - a0), grp="w2")
     for o in ops:
         o["bump"] = o.get("bump", 0.0) + 1e5
-    cp(V("of0"), C("n32", 0, 640), tag="of0")
+    plus(V("of0"), C("n32", 0, 640), 0.0, "of0")
     ms(V("onef"), 1.0)["bump"] = 1e5
     sel(V("idf"), V("onef"), [[-1, 128]], A.is_equal, 0.0, 0, 1)
     sel(V("bof"), V("onef"), [[-16, 8], [0, 16]], A.is_ge, 0.0, 0, 1)
     sel(V("bof"), V("bof"), [[16, 8], [0, 16]], A.is_ge, 0.0, 15, -1)
     iota(V("cf"), [[1, TB]], 0, 0)
     iota(V("ki"), [[0, 2]], 0, 1, True)
-    iota(V("dum"), [[16, 32]], TREAL - int(CEN), 1)
-    op("g", lambda: g.iota(T.tb[:, TW - GFILL:TW], [[0, GFILL]], 0, 0, allow_small_or_imprecise_dtypes=True), [], [C("tb", TW - GFILL, TW)],
-       ("gc", GFILL), tag="fill")
-    ms(C("tb", 0, TW - GFILL), 0.0, tag="fill")
+    iota(V("dum"), [[16, 32]], TREAL, 1)
+    ms(V("neg"), -1.0)
+    iota(C("tb", TREAL, TW), [[0, TW - TREAL]], 0, 0)["bump"] = 1e5
+    for r in (2, 3):
+        dma("s", raw(T.tb[r:128:4, 0:TREAL], reg=C("tb", 0, TREAL)["reg"]), C("tb", TREAL, TREAL + TREAL // 4), 330000, grp="zero", tag="zero")
     ms(V("mh", slice(MH.index("l1"), None)), 0.0)
     ms(V("mb"), 0.0)
     ms(V("wr"), 0.0)
@@ -415,7 +445,6 @@ def build(g, core, T, topo, plan):
     kon(K(3), KM, float(TB), -CEN, A.add)
     kon(K(4), KM, -SLOPE, TOPW - 512.0, A.add)
     kon(K(5), S(6), BIG / 8)
-    kon(K(6), S(6), -BIG / 8)
     kon(K(7), S(3), -1.0)
     ts(K(8), S(6), S(2), 1e28, A.subtract, A.mult, tag="k")
     ts(K(9), R4(1), R4(2), -8.0, A.add, A.mult, tag="k")
@@ -429,13 +458,12 @@ def build(g, core, T, topo, plan):
     for nm, a, s, src, f in (("l1", 0, 4, ID(0, 4), 1.0), ("l1", 1, 4, ID(0, 4), 1.0), ("l1", 2, 4, BO(2, 4), S(3)),
                              ("l2", 0, 4, BO(0, 4), K(7)), ("l2", 6, 8, BO(6, 8), K(7)), ("l3", 1, 4, BO(1, 4), K(7)), ("l3", 2, 8, BO(2, 8), K(7)),
                              ("lb", 0, 1, BO(0, 1), S(3)), ("lt", 0, 4, BO(0, 4), S(3)), ("lt", 1, 4, BO(1, 4), S(7)),
-                             ("luu", 2, 4, BO(2, 4), S(12)), ("lul", 2, 4, ID(0, 4), 1.0),
+                             ("luu", 2, 4, BO(2, 4), S(12)), ("lul", 0, 1, ID(0, 1), 1.0), ("lul", 2, 4, ID(0, 4), 1.0),
                              ("l4", 2, 16, BO(2, 16), K(10)), ("l4", 6, 16, ID(3, 16), 1.0), ("lpen", 0, 1, BO(0, 1), K(8)),
-                             ("bo", 0, 1, BO(0, 1), 1.0), ("lml", 2, 4, ID(1, 4), -BIG)):
+                             ("bo", 0, 1, BO(0, 1), 1.0), ("lml", 0, 4, ID(1, 4), BIG), ("lml", 1, 4, ID(1, 4), BIG), ("lml", 2, 4, ID(1, 4), BIG)):
         kon(M(nm, a, 128, s), src, f)
-    for nm, a, f, c in (("lmu", 0, -BIG, 5), ("lmu", 1, -BIG, 5), ("lmu", 2, BIG, 6), ("lmu", 3, 0.0, 5),
-                        ("lml", 0, BIG, 6), ("lml", 1, BIG, 6), ("lml", 3, 0.0, 6)):
-        ts(M(nm, a, 128, 4), ID(1, 4), f, K(c), A.mult, A.add, tag="k")
+    for a, f in enumerate((-BIG, -BIG, -BIG, 0.0)):
+        ts(M("lmu", a, 128, 4), ID(1, 4), f, K(5), A.mult, A.add, tag="k")
     kon(V("tri"), BO(1, 4), K(11))
     sel(V("tri"), V("tri"), [[4, 32]], A.is_gt, 0.0, 0, -1)
     sel(V("tri"), V("tri"), [[4, 32]], A.not_equal, 1.0, 0, -1)
@@ -444,11 +472,11 @@ def build(g, core, T, topo, plan):
                        ("y3", ID(3, 16), 1.0), ("y6", ID(6, 16), 1.0), ("y10", ID(10, 16), 1.0), ("y2b", ID(2, 16), 1.0)):
         ts(M(nm, 15, 143, 16), src, f, None, A.mult, tag="k")
     act(V("nf", slice(None), slice(0, 160)), C("n32", 0, 640), F.Identity, bias=-CEN, tag="tab")
-    ts(V("na"), V("n32"), float(NV), CEN, A.min, A.subtract, tag="tab")
-    ts(V("nh"), V("na"), 1.0 / 16, 1100 + 64 - 7.5 / 16, A.mult, A.add, tag="tab")
+    ts(C("sd", 0, 664), V("n32"), float(NV), CEN, A.min, A.subtract, tag="tab")
+    ts(C("ss", 0, 664), C("sd", 0, 664), 1.0 / 16, 1100 + 64 - 7.5 / 16, A.mult, A.add, tag="tab")
     for a, b in ((0, 480), (480, 664)):
         o = B6 if a == 0 else B7
-        mm([(P(o, b - a), M(m), C(s, a, b)) for m, s in (("i161", "na"), ("imk", "nh"), ("imk", "nh"), ("im527", "nh"))], tag="tab")
+        mm([(P(o, b - a), M(m), C(s, a, b)) for m, s in (("i161", "sd"), ("imk", "ss"), ("imk", "ss"), ("im527", "ss"))], tag="tab")
     c0 = TB * CEN + 2575.0 * 1100 - CEN
     act(V("pf", slice(0, 3), slice(0, 160)), P(B6, 480), F.Identity, bias=c0, tag="tab")
     act(R("pf", 3, 0, 160), P(B7, 160), F.Identity, bias=c0, tag="tab")
@@ -459,33 +487,29 @@ def build(g, core, T, topo, plan):
         dma("s", rows(4 * p + 1), R("pf", p), 200000, grp="tab", tag="tab")
     for r in range(2):
         dma("s", rows(4 * r + 3), R("sf", r), 200000, grp="tab", tag="tab")
-    cp(V("lu"), C("li", 0, 72), tag="tab")
     for u in range(3):
-        act(R("mk", u), IND("cw", 0, 8, C("lu", 24 * u, 24 * u + 24)), F.Identity, tag="mask")
+        cp(V("lu", slice(None), slice(8 * u, 8 * u + 8)), C("li", 24 * u, 24 * u + 24), tag="tab")
+    for t in range(RO):
+        act(C("mk", 384 * t, 384 * t + 384), IND("cw", 0, 8, R("lu", t)), F.Identity, tag="mask")
     act(V("hq16"), C("li", 72, 96), F.Identity, tag="k")
     for a0, a1 in STR:
-        act(C("xn0", a0, a1), C("w0", a0, a1), F.Identity, bias=-2048.0, tag="xn")
+        plus(C("xn0", a0, a1), C("w0", a0, a1), -2048.0, "xn")
 
     def marks():
         dma("s", C("aw", 0, NV), raw(T.am[:]), 128 * 2 * NV)["rel"] = 40000.0
         for o in turn("ss", "ra", (T.am, []), "ra"):
             o["rel"] = 40000.0
-        send(10, C("aw", 0, GH), V("ra"), "aw", [], C("aw", NV, NW))
+        send(10, C("aw", 0, GH), V("ra"), "aw", [])
 
-    def clips(d, s, c, by_scalar, tag):
-        if by_scalar:
-            ts(c, d, -2047.0, 2047.0, A.max, A.min, tag="c" + tag)
-            act(s, d, F.Sign, tag="s" + tag)
-            return 1
-        ts(s, d, -1.0, 1.0, A.max, A.min, tag="s" + tag)
-        ts(d, d, -2047.0, 2047.0, A.max, A.min, tag="c" + tag)
-        return 0
+    def D(name, pc, p, a, b):
+        return R(name, p, a, b)
 
-    def piece(k, of, p0, a0, a1, who, sg):
-        tag = " k%d a%d p%d" % (k, a0, p0)
+    def piece(k, of, pc):
+        p0, a0, a1, who, sg, parts = pc
         for p, e in enumerate(who, p0):
+            tag = " k%d a%d p%d" % (k, a0, p)
             win = IND(W[k % 4], 0, NW, C(of, (p * NV + a0) // 16, (p * NV + a1) // 16))
-            d = R("d1", p, a0, a1)
+            d = D("d1", pc, p, a0, a1)
             if e == "v":
                 tt(d, win, C(XN[k % 2] if k else "w2", a0, a1), A.subtract, tag="gv" + tag)
                 continue
@@ -493,66 +517,70 @@ def build(g, core, T, topo, plan):
             if e == "a":
                 dma("g", d, C(XN[k % 2], a0, a1), 256 * (a1 - a0), add=True, tag="add" + tag)
                 continue
-            o = 1024 if a0 >= 1536 and k < 3 * RO else B6
-            if a1 - a0 == 512:
-                o = 512 * (1 + p % 3) if a0 == 0 and k < 3 * RO else o + 512 * (p % 2)
+            o = plan["pb"][p % 2]
             for b in range(a0, a1, 512):
-                u = P(o + b - a0, 512)
-                mm([(u, M("i1"), R("d1", p, b, b + 512)), (u, M("i1"), C(XN[k % 2], b, b + 512))], tag="pd")
-            ts(R("d3", p, a0, a1), P(o, a1 - a0), -2047.0, 2047.0, A.max, A.min, tag="cp" + tag)
-        d, s, c = (V(u, slice(p0, p0 + len(who)), slice(a0, a1)) for u in ("d1", "d2", "d3"))
-        if who[0] != "p":
-            return ("d1", "d3")[clips(d, s, c, sg == "a", tag)]
-        if sg == "a":
-            act(s, c, F.Sign, tag="s" + tag)
-        else:
-            ts(s, c, -1.0, 1.0, A.max, A.min, tag="s" + tag)
-        return "d3"
+                u = P(o + b - a0, min(512, a1 - b))
+                mm([(u, M("i1"), D("d1", pc, p, b, b + u["n"])), (u, M("i1"), C(XN[k % 2], b, b + u["n"]))], tag="pd")
+            ts(D("d3", pc, p, a0, a1), P(o, a1 - a0), -2047.0, 2047.0, A.max, A.min, tag="cp" + tag)
+        for b in range(a0, a1, (a1 - a0) // parts):
+            tag = " k%d a%d p%d" % (k, b, p0)
+            d, s, c = (V(u, slice(p0, p0 + len(who)), slice(b, b + (a1 - a0) // parts)) for u in ("d1", "d2", "d3"))
+            if who[0] == "p":
+                d = c
+            if sg == "v":
+                ts(s, d, -1.0, 1.0, A.max, A.min, tag="s" + tag)
+            if who[0] != "p" and k < 3 * RO:
+                ts(c, d, -2047.0, 2047.0, A.max, A.min, tag="c" + tag)
+            if sg == "a":
+                act(s, d, F.Sign, tag="s" + tag)
+        return "d3" if k < 3 * RO or who[0] == "p" else "d1"
 
     def sweep(k, of):
         wn, xn, xo = W[(k + 1) % 4], XN[(k + 1) % 2], XN[k % 2]
         cn = {}
-        for a0, a1, col in plan["str"]:
+        for a0, a1, col in plan.get(("str", k % 3), plan["str"]):
             blocks = [(b, min(b + 512, a1)) for b in range(a0, a1, 512)]
             bank = [P(col + b0 - a0, b1 - b0) for b0, b1 in blocks]
             for (b0, b1), ps in zip(blocks, bank):
                 mm([(ps, M("i1"), C(xo, b0, b1)),
                     (ps, raw(T.cb[0:1, :], reg=V("cb")["reg"]), raw(T.ones[0:1, 0:b1 - b0], n=b1 - b0, reg=V("ones")["reg"]))], stop=False, tag="m0")
-            for n, (p0, c0, c1, who, sg) in enumerate(plan[k % 3 if k else 6]):
+            for n, pc in enumerate(plan[k]):
+                p0, c0, c1, who = pc[:4]
                 if c1 <= a0 or a1 <= c0:
                     continue
                 if n not in cn:
-                    cn[n] = piece(k, of, p0, c0, c1, who, sg)
+                    cn[n] = piece(k, of, pc)
                 for p, e in enumerate(who, p0):
                     ms_, mc_ = ("im64", "i16") if e == "v" else ("i64", "im16")
                     for (b0, b1), ps in zip(blocks, bank):
-                        if c0 <= b0 < c1:
-                            mm([(ps, M(ms_), R("d2", p, b0, b1))], start=False, acc=(k, b0), tag="ms")
-                            mm([(ps, M(mc_), R(cn[n], p, b0, b1))], start=False, acc=(k, b0), tag="mc")
+                        e0, e1 = max(b0, c0), min(b1, c1)
+                        if e0 < e1:
+                            mm([(P(col + e0 - a0, e1 - e0), M(ms_), D("d2", pc, p, e0, e1))], start=False, acc=(k, b0), tag="ms")
+                            mm([(P(col + e0 - a0, e1 - e0), M(mc_), D(cn[n], pc, p, e0, e1))], start=False, acc=(k, b0), tag="mc")
             ts(C(wn, a0, a1), P(col, a1 - a0), -2048.0, 2047.0, A.max, A.min, tag="fin k%d b%d" % (k, a0))
             if a0 == 0:
                 rs = "rs%d" % ((k + 1) % 2)
                 turn("ss", rs, (T[wn], C(wn, 0, GH)["reg"]), ("rs", k))
-                send(k + 1, C(wn, 0, GH), V(rs), wn, [C(W[(k + 2) % 4], NV, NW)], C(wn, NV, NW))
-            sel(C(xn, a0, a1), C(wn, a0, a1), [[0, a1 - a0]], A.is_gt, 0.0, 1, 0)["tag"] = "xn k%d b%d" % (k, a0)
+                send(k + 1, C(wn, 0, GH), V(rs), wn, [C(W[(k + 2) % 4], NV, NW)])
+            for b0, b1 in plan["cast"]:
+                if a0 < b1 <= a1:
+                    sel(C(xn, b0, b1), C(wn, b0, b1), [[0, b1 - b0]], A.is_gt, 0.0, 1, 0)["tag"] = "xn k%d b%d" % (k, b0)
 
     def put(skip, src, of, n):
         mm(skip, tag="wrap")
         ts(V("ls"), skip[0][0], 0.0, 4096.0, A.max, A.min, tag="put")
-        mm([(P(B4, 32), M("i1"), V("pl16"))] + [(P(B4 + 8 * r, 8), M("i1"), V("ls")) for r in range(4)], tag="wrap")
-        tt(V("o2"), P(B4, 32), V("dum"), A.min, tag="put")
-        ts(V("ou"), V("o2"), CEN, None, A.add, tag="put")
+        mm([(P(B4, 32), M("i1"), V("pl16")), (P(B4, 32), M("imk"), V("neg"))] + [(P(B4 + 8 * r, 8), M("i1"), V("ls")) for r in range(4)], tag="wrap")
+        tt(V("ou"), P(B4, 32), V("dum"), A.min, tag="put")
         cp(IND("tb", 0, TW, V("ou")), V(src), tag="scatter")
-        for p in range(4):
-            dma("s", R("nf", p), rows(4 * p), 150000, grp=("relist", n), tag="relist")
-        if plan["re"][n % 2] == "a":
-            act(V(of), V("nf", slice(None), slice(0, 160)), F.Identity, bias=CEN, tag="relisted")
-        else:
-            ts(V(of), V("nf", slice(None), slice(0, 160)), CEN, None, A.add, tag="relisted")
+        h = plan["halves"]
+        for u in range(h):
+            for p in range(4 * u // h, 4 * (u + 1) // h):
+                dma("s", R("nf", p), rows(4 * p), 150000, grp=("relist", n, u), tag="relist")
+            plus(C(of, 640 * u // h, 640 * (u + 1) // h), V("nf", slice(4 * u // h, 4 * (u + 1) // h), slice(0, 160)), CEN, "relisted")
 
     def lanes(t, of):
         GA, GC, GB, GD = (C("gg", 128 * r, 128 * (r + 1)) for r in range(4))
-        MK, MJ, ML = (R("mk", u, 128 * t, 128 * (t + 1)) for u in range(3))
+        MK, MJ, ML = (C("mk", 384 * t + 128 * u, 384 * t + 128 * u + 128) for u in range(3))
         FA, FD = C("fm", 0, 128), C("fm", 128, 256)
         PB = C("pbu", 8 * t, 8 * t + 8)
         tt(C("t1", 0, 128), IND("tb", 0, TW, PB), MK, A.mult, tag="L1")
@@ -563,7 +591,7 @@ def build(g, core, T, topo, plan):
         tt(V("t2"), IND("tb", 0, TW, C("plu", 8, 16)), ML, A.mult, tag="L2")
         mm(wrap(P(B4 + 24, 8), "xw1", "t2", 0, 8), tag="wrap")
         ts(C("plu", 24, 32), P(B4 + 24, 8), CEN, None, A.add, tag="L2")
-        act(V("pl16"), P(B4, 32), F.Identity, tag="pl")
+        plus(V("pl16"), P(B4, 32), 0.0, "pl")
         act(V("gg"), IND("tb", 0, TW, V("plu")), F.Identity, scale=K(0), bias=K(1), tag="L3")
         for h, (own, first, second) in enumerate(((GA, GB, GC), (GD, GC, GB))):
             mm([(P(B6 + 128 * h, 128), M(m), u) for m, u in (("l1", own), ("l2", first), ("l3", second))], tag="good")
@@ -571,87 +599,62 @@ def build(g, core, T, topo, plan):
         mm([(P(B7, 256), M("l4"), V("ee"))], tag="good")
         ts(V("fm"), P(B7, 256), 0.5, None, A.is_ge, tag="good")
         mm([(P(B5, 512), M("lb"), V("gg"))], tag="rw")
-        act(V("rw"), P(B5, 512), F.Identity, tag="rw")
+        plus(V("rw"), P(B5, 512), 0.0, "rw")
         mm(wrap(P(B4, 32), "y3", "gg", 0, 32), tag="wrap")
-        act(V("wh"), P(B4, 32), F.Identity, tag="rw")
-        ts(V("whu"), V("wh"), CEN, None, A.add, tag="whu")
+        plus(V("wh"), P(B4, 32), 0.0, "rw")
         mm(wrap(P(B4, 8), "y2b", "fm", 0, 8) + wrap(P(B4, 8), "y2b", "fm", 128, 8) + [(P(B4, 8), M("i1"), V("cl"))], tag="good")
         act(V("ww"), P(B4, 8), F.Exp, scale=256.0, bias=K(4), tag="good")
-        for o, lu, lm in ((B6, "luu", "lmu"), (B7, "lul", "lml")):
-            mm([(P(o, 512), M(lu), V("gg"))] + [(P(o + 128 * r, 128), M("lt"), u) for r, u in enumerate((GC, GA, GD, GB))]
+        for o, lu, lm in ((B6, "lul", "lml"), (B7, "luu", "lmu")):
+            mm([(P(o, 512), M(lu), V("gg"))] + [(P(o + 128 * r, 128), M("lt"), u) for r, u in enumerate((GC, GA, GD, GB)) if o == B7]
                + [(P(o + 128 * r, 128), M(lm), u) for r, u in enumerate((FA, ML, MK, FD))], tag="new")
-        tt(V("no1"), P(B6, 512), V("gg"), A.min, tag="new")
-        tt(V("no"), P(B7, 512), V("no1"), A.max, tag="new")
+        plus(V("no1"), P(B6, 512), 0.0, "old")
+        tt(V("no"), P(B7, 512), V("no1"), A.min, tag="new")
+        for p, (y, src) in enumerate((("y3", "gg"), ("y2", "no"), ("y6", "no"), ("y10", "no"))):
+            mm(wrap(P(B6 + 32 * p, 32), y, src, 0, 32), tag="sl")
+        plus(V("sl"), P(B6, 128), CEN, "sl")
         mm([(P(B5, 128), M("lpen"), FA), (P(B5, 128), M("lpen"), FD)], stop=False, tag="pm")
         for n in range(32):
-            c, r, q = n // 4, n % 4, "q%d" % (n % 3)
-            ts(V(q, slice(None), slice(16 * c, 128)), V("rw", slice(None), slice(16 * c, 128)), R("wh", r, c, c + 1), C("ww", c, c + 1),
+            c, r, q = n // 4, n % 4, 4 * (n % NQ)
+            ts(V("qq", slice(q, q + 4), slice(16 * c, 128)), V("rw", slice(None), slice(16 * c, 128)), R("wh", r, c, c + 1), C("ww", c, c + 1),
                A.is_equal, A.mult, tag="pair")
-            mm([(P(B5 + 16 * c, 128 - 16 * c), M("bo"), R(q, u, 16 * c, 128)) for u in range(4)], start=False, stop=n == 31, tag="pm")
+            mm([(P(B5 + 16 * c, 128 - 16 * c), M("bo"), R("qq", q + u, 16 * c, 128)) for u in range(4)], start=False, acc=("pm", t), tag="pm")
         tt(V("lz"), P(B5, 128), V("thr"), A.is_ge, tag="lose")
         put(wrap(P(B4 + 64, 8), "xwp", "lz", 0, 8), "no", of, 2 * t)
-        for p, y in enumerate(("y2", "y6", "y10")):
-            mm(wrap(P(B4 + 128 + 32 * p, 32), y, "no", 0, 32), tag="sl")
-        ts(V("sl"), P(B4 + 128, 96), CEN, None, A.add, tag="sl")
 
     def stress(k, z):
         w, at = W[k % 4], " k%d" % k
         off = 2048.0 if k == 0 else 0.0
         own = R("xo", z)
-        act(own, IND(w, 0, NW, C("whu", 0, 32)), F.Identity, bias=off, scale=-1.0, tag="xo" + at)
-        tot = P(B5, 128)
-        units = plan[4 + z]
-
-        def squares(a, m, c, bank, first, last):
-            sq = C("sq", bank - B6, bank - B6 + m)
-            for b in range(0, m, 512):
-                u = P(bank + b, min(512, m - b))
-                mm([(u, M("imk"), R("ss", z, a + b, a + b + u["n"])), (u, M("i1"), R(c, z, a + b, a + b + u["n"]))], tag="su" + at)
-            act(sq, P(bank, m), F.Square, tag="sq" + at)
-            mm([(tot, V("id2" if first else "idf"), C("sq", b, b + 128)) for b in range(bank - B6, bank - B6 + m, 128)],
-               start=first, stop=last, wide=4, tag="st" + at)
-
-        def from_psum(a, m, u, sg):
-            s, c = R("ss", z, a, a + m), R("sc", z, a, a + m)
-            ts(c, u, -2047.0, 2047.0, A.max, A.min, tag="cs" + at)
-            if sg == "a":
-                act(s, c, F.Sign, tag="ss" + at)
-            else:
-                ts(s, c, -1.0, 1.0, A.max, A.min, tag="ss" + at)
-        u = P(B7, 256)
-        mm([(u, M("i1"), R("xo", z, 128 * z, 128 * z + 256))]
+        who, cuts = "".join(E("sa") for p in range(3)), plan["st"][z]
+        act(own, IND(w, 0, NW, C("sl", 0, 32)), F.Identity, bias=off, scale=-1.0, tag="xo" + at)
+        mm([(P(B7, 256), M("i1"), R("xo", z, 128 * z, 128 * z + 256))]
            + [(P(B7 + 128 * j, 128), M("im1"), R("xo", z, 128 * r, 128 * r + 128)) for j, r in enumerate(((2, 3), (0, 3))[z])], tag="sp" + at)
-        from_psum(1536, 256, u, "v")
-        squares(1536, 256, "sc", B7, True, False)
-        p0 = 0
-        for who, sg in units:
-            who = who if k else who.replace("v", "a")
-            a, m = 512 * p0, 512 * len(who)
-            if "v" not in who:
-                act(R("sd", z, a, a + m), IND(w, 0, NW, C("sl", a // 16, (a + m) // 16)), F.Identity, bias=-off, tag="sa" + at)
-            for p, e in enumerate(who, p0):
-                d, lst = R("sd", z, 512 * p, 512 * p + 512), IND(w, 0, NW, C("sl", 32 * p, 32 * p + 32))
-                if e == "v":
-                    tt(d, lst, own, A.add, tag="sg" + at)
-                    continue
-                if "v" in who:
-                    act(d, lst, F.Identity, bias=-off, tag="sa" + at)
-                if e == "a":
-                    dma("g", d, own, 256 * 512, add=True, tag="sadd" + at)
-                else:
-                    u = P(B6 + 512 * (p % 2), 512)
-                    mm([(u, M("i1"), d), (u, M("i1"), own)], tag="sp" + at)
-                    from_psum(512 * p, 512, u, sg)
-            c = "sc"
-            if who[0] != "p":
-                c = ("sd", "sc")[clips(*(R(u, z, a, a + m) for u in ("sd", "ss", "sc")), sg == "a", "s" + at)]
-            p = p0
-            while p < p0 + len(who):
-                n = 2 if p % 2 == 0 and p + 2 <= p0 + len(who) else 1
-                squares(512 * p, 512 * n, c, B6 + 512 * (p % 2), False, p + n == 3)
-                p += n
-            p0 += len(who)
-        return tot
+        ts(C("sd", 0, 256), P(B7, 256), -2047.0, 2047.0, A.max, A.min, tag="cs" + at)
+        for p, e in enumerate(who):
+            d, lst = C("sd", 256 + 512 * p, 768 + 512 * p), IND(w, 0, NW, C("sl", 32 * p + 32, 32 * p + 64))
+            if e == "v":
+                tt(d, lst, own, A.add, tag="sa%s p%d" % (at, p))
+            else:
+                act(d, lst, F.Identity, bias=-off, tag="sa%s p%d" % (at, p))
+                dma("g", d, own, 256 * 512, add=True, tag="sadd%s p%d" % (at, p))
+        for a, b in zip(cuts, cuts[1:]):
+            d, s = C("sd", a, b), C("ss", a, b)
+            if E("ss") == "v":
+                ts(s, d, -1.0, 1.0, A.max, A.min, tag="ss%s a%d" % (at, a))
+            else:
+                act(s, d, F.Sign, tag="ss%s a%d" % (at, a))
+            if b > 256:
+                ts(C("sc", max(a, 256), b), C("sd", max(a, 256), b), -2047.0, 2047.0, A.max, A.min, tag="cs" + at)
+            bank = B6 if b - a > 512 or a % 1024 >= 512 else B7
+            for c in range(a, b, 512):
+                u = P(bank + c - a, min(512, b - c))
+                mm([(u, M("imk"), C("ss", c, c + u["n"]))]
+                   + [(P(bank + e0 - a, e1 - e0), M("i1"), C(nm, e0, e1)) for nm, e0, e1 in (("sd", c, min(256, b)), ("sc", max(c, 256), c + u["n"])) if e0 < e1],
+                   tag="su" + at)
+            act(C("sq", bank - B6, bank - B6 + b - a), P(bank, b - a), F.Square, tag="sq" + at)
+            mm([(P(B5, 128), V("id2" if c < 256 else "idf"), C("sq", bank - B6 + c - a, bank - B6 + c - a + 128)) for c in range(a, b, 128)],
+               start=a == 0, stop=b == 1792, wide=4, tag="st" + at)
+        return P(B5, 128)
 
     def votes(t, tot, of):
         tt(V("vz"), tot, V("f1"), A.is_gt, tag="vote")
@@ -660,39 +663,34 @@ def build(g, core, T, topo, plan):
 
     def last(k, of):
         bank = {}
-        for n, (p, a0, a1, who, sg) in enumerate(plan[3]):
-            cn = piece(k, of, p, a0, a1, who, sg)
+        for n, pc in enumerate(plan[k]):
+            p, a0, a1 = pc[:3]
+            cn = piece(k, of, pc)
             e, (tn, t0) = "e%d" % (n % 3), (("t0", 0), ("t3", 0), ("t4", 0), ("tb", 0), ("tb", 1024), ("tb", 2048))[n % 6]
             nb = 1024 * (n % 3)
             for b0 in range(a0, a1, 512):
-                u = P(nb + b0 - a0, 512)
-                mm([(u, M("imk"), R("d2", p, b0, b0 + 512)), (u, M("i1"), R(cn, p, b0, b0 + 512))], tag="fu")
+                b1 = min(a1, b0 + 512)
+                u = P(nb + b0 - a0, b1 - b0)
+                mm([(u, M("imk"), D("d2", pc, p, b0, b1)), (u, M("i1"), D(cn, pc, p, b0, b1))], tag="fu")
             ev, tv = C(e, 0, a1 - a0), C(tn, t0, t0 + a1 - a0)
-            act(ev, P(nb, a1 - a0), F.Square, tag="fq")
-            act(ev, ev, F.Exp, scale=-2.0 ** -19, tag="fe")
+            act(R("eq", n % 3, 0, a1 - a0), P(nb, a1 - a0), F.Square, scale=math.sqrt(65535.0) / 1023, tag="fq")
+            act(ev, R("eq", n % 3, 0, a1 - a0), F.Exp, scale=-2.0 ** -19 * 1023 * 1023 / 65535, tag="fe")
             tt(tv, IND("aw", 0, NW, C(of, (p * NV + a0) // 16, (p * NV + a1) // 16)), ev, A.mult, tag="mk a%d p%d" % (a0, p))
-            if plan["ys"][a0 // 512] == "d":
-                yv = raw(T.y[:, a0:a1], reg=[("y", a0, a1, None)])
+            yv = raw(T.y[:, a0:a1], reg=[("y", a0, a1, None)])
+            if a0 < plan["ys"]:
                 dma("g" if p else "s", yv, tv, 512 * (a1 - a0), add=p > 0, tag="y")
                 continue
-            for b0 in range(a0, a1, 512):
-                new = b0 not in bank
-                bank.setdefault(b0, [B6 + 512 * (len(bank) % 2), 0])[1] += 1
-                mm([(P(bank[b0][0], 512), V("idf"), C(tn, t0 + b0 - a0, t0 + b0 - a0 + 512))], start=new, stop=False, acc=None if new else ("y", b0),
-                   wide=4, tag="ys")
-            done = [b0 for b0 in range(a0, a1, 512) if bank[b0][1] == 4]
-            if len(done) == 2 and bank[done[1]][0] == bank[done[0]][0] + 512:
-                done = [done]
-            else:
-                done = [[b0] for b0 in done]
-            for bs in done:
-                b0, b1 = bs[0], bs[-1] + 512
-                yo = C("sq", bank[b0][0] - B6, bank[b0][0] - B6 + b1 - b0)
-                if plan["ys"][b0 // 512] == "a":
-                    act(yo, P(bank[b0][0], b1 - b0), F.Identity, tag="yc")
+            at = bank.setdefault(a0, [B6 + 512 * (len(bank) % 2), 0])
+            at[1] += 1
+            if at[1] < 4 or plan["yc"] == "a":
+                mm([(P(at[0], a1 - a0), V("idf"), tv)], start=at[1] == 1, stop=False, acc=None if at[1] == 1 else ("y", a0), wide=4, tag="ys")
+            if at[1] == 4:
+                yo = C("sq", at[0] - B6, at[0] - B6 + a1 - a0)
+                if plan["yc"] == "a":
+                    act(yo, P(at[0], a1 - a0), F.Identity, tag="yc")
                 else:
-                    cp(yo, P(bank[b0][0], b1 - b0), tag="yc")
-                dma("s", raw(T.y[:, b0:b1], reg=[("y", b0, b1, None)]), yo, 512 * (b1 - b0), tag="y")
+                    tt(yo, P(at[0], a1 - a0), tv, A.add, tag="yc")
+                dma("s", yv, yo, 512 * (a1 - a0), tag="y")
 
     for t in range(RO):
         k = 3 * t
@@ -700,12 +698,20 @@ def build(g, core, T, topo, plan):
         sweep(k, OF[0])
         if t == 0:
             marks()
-        act(V("f1"), stress(k, 0), F.Identity, tag="f1")
+        plus(V("f1"), stress(k, 0), 0.0, "f1")
         sweep(k + 1, OF[1])
         tot = stress(k + 2, 1)
         votes(t, tot, OF[0])
         sweep(k + 2, OF[1])
     last(3 * RO, OF[0])
+    members = {}
+    for o in ops:
+        if o.get("grp"):
+            members.setdefault(o["grp"], []).append(o["i"])
+    for o in ops:
+        for j in list(o["dep"]):
+            if ops[j].get("grp") and ops[j]["grp"] != o.get("grp"):
+                o["dep"].update(members[ops[j]["grp"]])
     return ops
 
 
@@ -730,7 +736,7 @@ def emit(g, T, ops, order):
         k = o["c"][0]
         if k == "arr":
             mark[i] = o["sem"]
-            total[o["sem"][0]] = o["sem"][1]
+            total[o["sem"][0]] = max(o["sem"][1], total.get(o["sem"][0], 0))
         elif k in ("dma", "rem"):
             key = o.get("grp") or ("own", i)
             if key not in grp:
@@ -758,7 +764,7 @@ def emit(g, T, ops, order):
         ws = {}
         for j in sorted(o["dep"], key=lambda u: -mark[u][1] if mark[u][0][0] == "q" else 0):
             s, c = mark[j]
-            if s == "q" + e and o["c"][0] not in ("dma", "rem") and (e == "p" or j not in o["raw"]):
+            if s == "qp" and e == "p":
                 continue
             if kn.get(s, 0) >= c:
                 continue
@@ -777,27 +783,28 @@ def emit(g, T, ops, order):
         pl = sorted(c for s2, c in need if s2 == s)
         for n, c in enumerate(pl):
             count[(s, c)] = n + 1
-    users = {}
+    users, raises = {}, {}
     for i in order:
+        raises.setdefault(mark[i][0], []).append(i)
         for s in waits.get(i, {}):
             users.setdefault(s, []).append(i)
-    real, base, mine, used = {}, {}, [], 0
+    real, base, mine, used = {}, {}, {}, 0
     for i in order:
         o = ops[i]
         s = mark[i][0]
         if o["c"][0] not in ("dma", "rem") or s in real:
             continue
-        own = o["e"] == "g" and o["c"][0] == "dma"
-        for n, s0 in enumerate(mine if own else []):
-            if s0 in users and clock[i].get(s0, 0) >= total[s0] and all(clock[i].get(mark[u][0], 0) >= mark[u][1] and u != i for u in users[s0]):
+        pool = mine.setdefault((o["e"] == "g", o["c"][0]), [])
+        for n, s0 in enumerate(pool if o["e"] == "g" else []):
+            if s0 in users and all(clock[j].get(s0, 0) >= total[s0] and all(clock[j].get(mark[u][0], 0) >= mark[u][1] and mark[u][0] != s for u in users[s0])
+                                   for j in raises[s]):
                 real[s], base[s] = real[s0], base[s0] + total[s0]
-                mine.pop(n)
+                pool.pop(n)
                 break
         else:
             real[s], base[s] = "m%d" % used, 0
             used += 1
-        if own:
-            mine.append(s)
+        pool.append(s)
     waited = {}
     for i in order:
         o = ops[i]
@@ -823,7 +830,7 @@ def emit(g, T, ops, order):
     return used
 
 
-def polish(ops, order, models, tries, seed=1):
+def polish(ops, order, models, tries, seed=1, heat=0.0):
     n = len(ops)
     eng = ["vapgsx".index(o["e"]) for o in ops]
     succ = [[] for _ in ops]
@@ -832,7 +839,8 @@ def polish(ops, order, models, tries, seed=1):
             succ[j].append(o["i"])
     tab = [([cost(o, M) for o in ops], [[(j, delay(ops[j], o, M)) for j in o["dep"]] for o in ops],
             [[(j, delay(o, ops[j], M)) for j in succ[o["i"]]] for o in ops],
-            [o["c"][1] / M["bw"] if o["c"][0] == "dma" else -1.0 for o in ops], [finish(o, 0.0, M, [0.0]) for o in ops], M["dl"]) for M in models]
+            [o["c"][1] / M["bw"] if o["c"][0] in ("dma", "rem") else -1.0 for o in ops], [finish(o, 0.0, M, [0.0]) for o in ops],
+            [start_up(o, M) for o in ops]) for M in models]
     rel = [o.get("rel", 0.0) if o["c"][0] == "arr" else 0.0 for o in ops]
     state = [seed]
 
@@ -860,8 +868,8 @@ def polish(ops, order, models, tries, seed=1):
             if q != 5:
                 free[q], last[q] = t, i
             if mv[i] >= 0:
-                st = max(st, t + dl * 0.7) + mv[i]
-                e[i] = st + dl * 0.3
+                st = max(st, t + dl[i] * 0.7) + mv[i]
+                e[i] = st + dl[i] * 0.3
             else:
                 e[i] = t + la[i]
             back[i] = st
@@ -900,7 +908,8 @@ def polish(ops, order, models, tries, seed=1):
     rs = [run(order, tb) for tb in tab]
     ms = [max(r[0]) for r in rs]
     pairs, tails, pos, prev, nxt = adopt(order, rs)
-    for _ in range(tries):
+    best = (order, score(ms))
+    for step in range(tries):
         j, i = pairs[draw(len(pairs))]
         early = draw(2)
         for _ in range((0, 0, 1, 2, 3, 5)[draw(6)]):
@@ -929,20 +938,227 @@ def polish(ops, order, models, tries, seed=1):
                 e2[v] = t = t + e[v] - f[v]
                 top = max([top, t] + [t + d + q[u] for u, d in sc[v] if pos[u] > b])
             est.append(max([top] + [free[u] + q[nxt[v]] for u, v in end.items() if u != 5 and nxt[v] >= 0]))
-        if score(est) > score(ms) or (all(abs(x - m) < 1 for x, m in zip(est, ms)) and draw(5)):
+        bar = score(ms) - heat * (1 - step / tries) * math.log((draw(1000) + 1) / 1001)
+        if score(est) > bar or (all(abs(x - m) < 1 for x, m in zip(est, ms)) and draw(5)):
             continue
         o2 = order[:a] + new + order[b + 1:]
         r2 = [run(o2, tb, a, r) for tb, r in zip(tab, rs)]
         m2 = [max(r[0]) for r in r2]
-        if score(m2) <= score(ms):
+        if score(m2) <= bar:
             order, rs, ms = o2, r2, m2
             pairs, tails, pos, prev, nxt = adopt(order, rs)
-    return order, score(ms)
+            if score(ms) < best[1]:
+                best = (order, score(ms))
+    return best
 
 
-def make_order(ops, tries=None):
-    best = min((polish(ops, schedule(ops, dict(MODEL, cyc=c, pe=c / 2, ga=a), BUMP, 4)[0], MODELS, 0) for c, a in STARTS), key=lambda r: r[1])
-    return polish(ops, best[0], MODELS, TRIES if tries is None else tries)[0]
+def improve(ops, order, models, passes, seed=1, tries=70, flip=None, begin=0, stop=1):
+    n, nm = len(ops), len(models) - 1
+    state = [seed]
+
+    def draw(m):
+        state[0] = (state[0] * 1103515245 + 12345) % 2 ** 31
+        return (state[0] >> 8) % m
+    above, pred, succ = [], [], [[] for _ in ops]
+    for o in ops:
+        far = 0
+        for j in o["dep"]:
+            far |= above[j]
+        pred.append([j for j in o["dep"] if not far >> j & 1])
+        for j in o["dep"]:
+            far |= 1 << j
+        above.append(far)
+        for j in pred[-1]:
+            succ[j].append(o["i"])
+    eng, rel = [0] * n, [o.get("rel", 0.0) for o in ops]
+    tab = [[[0] * n for _ in range(6)] for M in models]
+
+    def fill(i):
+        o = ops[i]
+        eng[i] = "vapgsx".index(o["e"])
+        for (co, dp, mv, la, dl, sc), M in zip(tab, models):
+            co[i], la[i], dl[i] = cost(o, M), finish(o, 0.0, M, [0.0]), start_up(o, M)
+            mv[i] = o["c"][1] / M["bw"] if o["c"][0] in ("dma", "rem") else -1.0
+            dp[i] = [(j, delay(ops[j], o, M)) for j in pred[i]]
+            sc[i] = [(j, delay(o, ops[j], M)) for j in succ[i]]
+    for i in range(n):
+        fill(i)
+
+    def run(seq, tb, e, free, st, beg=None):
+        co, dp, mv, la, dl, _ = tb
+        for i in seq:
+            q = eng[i]
+            t = free[q]
+            if rel[i] > t:
+                t = rel[i]
+            for j, d in dp[i]:
+                if e[j] + d > t:
+                    t = e[j] + d
+            if beg:
+                beg[i] = t
+            t += co[i]
+            if q != 5:
+                free[q] = t
+            if mv[i] >= 0:
+                u = t + dl[i] * 0.7
+                st = (st if st > u else u) + mv[i]
+                e[i] = st + dl[i] * 0.3
+            else:
+                e[i] = t + la[i]
+        return st
+
+    def tails(seq, tb):
+        co, _, mv, la, dl, sc = tb
+        q, qd, nx, nd = [0.0] * n, [0.0] * n, [0.0] * 6, 0.0
+        for i in reversed(seq):
+            t = max([0.0] + [q[j] + d for j, d in sc[i]])
+            if mv[i] >= 0:
+                qd[i] = nd = max(t + dl[i] * 0.3, nd) + mv[i]
+                t = nd + dl[i] * 0.7
+            else:
+                t += la[i]
+            if eng[i] != 5:
+                t = max(t, nx[eng[i]])
+                nx[eng[i]] = t + co[i]
+            q[i] = t + co[i]
+        return q, qd
+
+    def place(win, key, e, free, st):
+        co, dp, mv, la, dl, _ = tab[nm]
+        left = {i: 0 for i in win}
+        for i in win:
+            for j in succ[i]:
+                if j in left:
+                    left[j] += 1
+        ready = [i for i in win if not left[i]]
+        gs, ge, beg = [[t] for t in free] + [[st]], [[1e18] for _ in range(7)], {}
+
+        def fit(q, t, c):
+            S, E = gs[q], ge[q]
+            k = len(S) - 1
+            while k and S[k] > t:
+                k -= 1
+            while True:
+                a = S[k] if S[k] > t else t
+                if a + c <= E[k]:
+                    break
+                k += 1
+            if a - S[k] < 20.0:
+                S[k] = a + c
+            elif E[k] - a - c < 20.0:
+                E[k] = a
+            else:
+                S.insert(k + 1, a + c)
+                E.insert(k, a)
+            return a
+        while ready:
+            i = min(ready, key=key.get)
+            ready.remove(i)
+            t = rel[i]
+            for j, d in dp[i]:
+                if e[j] + d > t:
+                    t = e[j] + d
+            c = co[i]
+            if eng[i] != 5:
+                t = fit(eng[i], t, c)
+            beg[i] = t + i * 1e-6
+            if mv[i] >= 0:
+                e[i] = fit(6, t + c + dl[i] * 0.7, mv[i]) + mv[i] + dl[i] * 0.3
+            else:
+                e[i] = t + c + la[i]
+            for j in succ[i]:
+                if j in left:
+                    left[j] -= 1
+                    if not left[j]:
+                        ready.append(j)
+        return sorted(win, key=beg.get)
+
+    def score(ms):
+        r = [m / M["was"] for m, M in zip(ms, models)]
+        return sum(r) / len(r) + max(r)
+    order = list(order)
+    for _ in range(passes):
+        tl = [tails(order, tb) for tb in tab[:nm]]
+        heads = [[[0.0] * n, [0.0] * 6, 0.0] for tb in tab]
+        a = begin
+        for tb, h in zip(tab, heads):
+            h[2] = run(order[:a], tb, h[0], h[1], h[2])
+        while a < stop * n - 1:
+            b = min(n, a + 80 + draw(140))
+            win, inside = order[a:b], set(order[a:b])
+            after = set(order[b:])
+            first = {}
+            for j in order[b:b + 400]:
+                first.setdefault(eng[j], j)
+                if tab[0][2][j] >= 0:
+                    first.setdefault(6, j)
+            first.pop(5, 0)
+            fixed = [max([0.0] + [h[0][i] + d + q[j] for i in order[max(0, a - 300):a] for j, d in tb[5][i] if j in after])
+                     for tb, h, (q, _) in zip(tab, heads, tl)]
+            edge = [i for i in win if b == n or any(j in after for j in succ[i])]
+            now = []
+
+            def value(w, bar):
+                ms = []
+                for tb, (e, free, st), (q, qd), m in zip(tab, heads, tl, fixed):
+                    if now and ms and ms[-1] > now[len(ms) - 1] * 1.004:
+                        return False
+                    fr = list(free)
+                    fr.append(run(w, tb, e, fr, st))
+                    for u, j in first.items():
+                        m = max(m, fr[u] + (q[j] if u < 6 else qd[j]))
+                    for i in edge:
+                        t = e[i]
+                        if t > m:
+                            m = t
+                        for j, d in tb[5][i]:
+                            if j in after and t + d + q[j] > m:
+                                m = t + d + q[j]
+                    ms.append(m)
+                if score(ms) > bar:
+                    return False
+                now[:] = ms
+                return True
+            value(win, 9.0)
+            e, free, st = heads[nm]
+            beg = [0.0] * n
+            run(win, tab[nm], e, list(free), st, beg)
+            some = [i for i in win if eng[i] < 4]
+            for _ in range(tries):
+                key = {i: beg[i] for i in win}
+                back = flip(win, inside, draw, fill, pred, succ) if flip else None
+                for _ in range((1, 1, 2, 3)[draw(4)] if not back else draw(3) // 2):
+                    j = some[draw(len(some))]
+                    d = math.exp(4.6 + draw(1000) * 0.0037) * (2 * draw(2) - 1)
+                    key[j] += d
+                    stack = [j] if d < 0 else []
+                    while stack:
+                        u = stack.pop()
+                        for w in pred[u]:
+                            if w in inside and key[w] >= key[u]:
+                                key[w] = key[u] - 1
+                                stack.append(w)
+                new = place(win, key, e, free, st)
+                if (back or new != win) and value(new, score(now) + 1e-9):
+                    win = new
+                    run(win, tab[nm], e, list(free), st, beg)
+                elif back:
+                    back()
+            order[a:b] = win
+            step = (b - a) // 2 + 1
+            for tb, h in zip(tab, heads):
+                h[2] = run(order[a:a + step], tb, h[0], h[1], h[2])
+            a += step
+    ms = []
+    for tb in tab[:nm]:
+        e = [0.0] * n
+        run(order, tb, e, [0.0] * 6, 0.0)
+        ms.append(max(e))
+    return order, score(ms), ms
+
+
+def make_order(ops, passes=None):
+    return improve(ops, schedule(ops, MID, BUMP, 4)[0], MODELS + [MID], PASSES if passes is None else passes, SEED)[0]
 
 
 ORDER = []

import math
import numpy as np
from concourse.bass import DstId, RemoteDMATransfer
from concourse.mybir import AluOpType as A, ActivationFunctionType as F

NV, GH, NW, RO = 2560, 256, 3072, 3
DSH = [1, 3]
TB, TREAL, TW = 161, 16 * 161, 3224
CEN = 1024.0
BIG = 8192.0
SLOPE, TOPW = 17.625 / 16, 60.0
NQ = 6
I32, F32, F16, B16, U16 = "int32", "float32", "float16", "bfloat16", "uint16"
MH = ["i1", "i16", "im64", "im16", "i64", "im1", "imk", "i161", "im527", "i4k", "l1", "l2", "l3", "lb", "lt", "luu", "lul"]
MB = ["l4", "lpen", "lmu", "lml", "bo"]
WH = ["xw1", "xwp", "xwm", "y2", "y3", "y6", "y10"]
SB = {
    "w0": ([NW], I32), "w1": ([NW], I32), "w2": ([NW], I32), "w3": ([NW], I32),
    "tb": ([TW], F32), "aw": ([NW], B16),
    "d1": ([4, NV], F16), "d2": ([4, NV], F16), "d3": ([4, NV], F16), "xn0": ([NV], F16), "xn1": ([NV], F16),
    "n32": ([664], I32), "nf": ([4, TB], F32), "pf": ([4, TB], F32), "sf": ([2, TB], F32),
    "of0": ([640], U16), "of1": ([640], U16),
    "rs0": ([GH], I32), "rs1": ([GH], I32), "ra": ([GH], B16),
    "mh": ([len(MH), 128], F16), "mb": ([len(MB), 128], B16), "wr": ([len(WH), 144], F16), "y2b": ([144], B16),
    "onef": ([128], F32), "idf": ([128], F32), "id2": ([128], F32), "bof": ([128], F32), "cb": ([128], F16), "ones": ([512], F16),
    "cf": ([TB], F32), "ki": ([2], I32), "kf": ([2], F32), "p16": ([16], F32), "r4": ([4], F32), "col": ([16], F32),
    "tri": ([32], F32), "cw": ([8], F32), "thr": ([128], F32), "dum": ([32], F32), "cl": ([8], F16),
    "li": ([96], I32), "lu": ([3, 24], U16), "mk": ([3 * 384], B16), "hq16": ([24], F16), "pbu": ([24], U16), "pb": ([24], F16),
    "t1": ([256], F16), "t2": ([128], F16), "plu": ([32], U16), "pl16": ([32], F16), "gg": ([512], F16), "no1": ([512], F16),
    "no": ([512], F16), "ee": ([256], B16), "fm": ([256], B16), "wh": ([4, 8], F32), "ww": ([8], F32),
    "rw": ([4, 128], F16), "qq": ([NQ * 4, 128], B16),
    "lz": ([128], F16), "vz": ([128], F16), "ls": ([8], F16), "neg": ([32], F16), "ou": ([32], U16), "sl": ([128], U16),
    "xo": ([2, 512], F16), "sd": ([1792], F16), "ss": ([1792], F16), "sc": ([1792], F16),
    "sq": ([1024], F32), "f1": ([128], F32),
    "eq": ([3, 1024], U16), "e0": ([1024], F32), "e1": ([1024], F32), "e2": ([1024], F32),
    "t0": ([1024], F32), "t3": ([1024], F32), "t4": ([1024], F32),
}
SCRATCH = {k: ("sbuf", [128] + s, d) for k, (s, d) in SB.items()}
SCRATCH["ps"] = ("psum", [128, 4096], F32)
ONCE = ("mh", "mb", "wr", "y2b", "idf", "id2", "cb", "ones", "col", "mk", "aw")
ARR = ["arr%d" % i for i in range(11)]
SEMAPHORES = ["qv", "qa", "qp", "qg"] + ARR + ["m%d" % i for i in range(146 - len(ARR))]

MODEL = dict(cyc=0.95, ga=1.4, sc=3.5, pe=0.48, fix=60.0, hop=120.0, same=60.0, gi=900.0, si=100.0, dl=1800.0,
             bw=500.0, rl=2500.0, look={})
STR = [(0, 512), (512, 1536), (1536, 2560)]
PIECES = {0: "002vvvvV 026aA 126aV 226aA 326aA 06aaA 16aaA 26aaA+ 36aaA+",
          1: "002vvvvV 026aV 126aV 226aV 326aV 06aaA 16aaA 26aaA+ 36avV",
          2: "002vvvvV 026aV 126vV 226aA 326aA 06aaA 16aaA 26aaA+ 36aaA",
          3: "002avvvV 026aV 126aA 226aA 326aA 06aaA 16aaA 26aaA+ 36aaA+",
          9: "004vV 048vV 104vV 148aV 204aV 248vV 08aaV 304aV 348aV 18avV 28aaV 38avV"}
for _k in range(4, 9):
    PIECES[_k] = PIECES[_k - 3]
ENG = {"pl": "vvv", "rw": "avavav", "old": "aaa", "sl": "aaa", "f1": "aaa", "relisted": "aaaaaaaaaaaa", "of0": "v", "xn": "avv",
       "ss": "vavvvavvvavvvvvvvvvvvvvv", "sa": "aaavvvaavvvvaavvvv"}


def make_plan(pieces, eng=None, **more):
    plan = {k: [(int(u[0]), 256 * int(u[1], 16), 256 * int(u[2], 16), u[3:].rstrip("+")[:-1], u.rstrip("+")[-1].lower(), 1 + u.count("+"))
                for u in v.split()] for k, v in pieces.items()}
    plan.update({"cast": [(0, 512), (512, 1536), (1536, 2560)], "pb": (3072, 3584), "ys": 2048, "yc": "v", "halves": 2, "merge": True,
                 "st": [(0, 768, 1792), (0, 768, 1792)], "eng": dict(ENG, **(eng or {})),
                 "str": [(0, 512, 0), (512, 1536, 1024), (1536, 2048, 512), (2048, 2560, 0)]})
    plan.update(more)
    return plan


PLAN = make_plan(PIECES)
BUMP = {"good": -2000.0, "send": 1000.0, "pl": -4000.0, "wrap": 500.0, "k": 1000.0, "fe": -1000.0, "vote": -1000.0, "fq": -1000.0, "tab": 5000.0}
MODELS = [dict(MODEL, cyc=0.83, pe=0.42, ga=1.5, was=228e3), dict(MODEL, cyc=1.245, pe=0.63, ga=1.1, sc=6.0, hop=200.0, was=320e3),
          dict(MODEL, cyc=1.245, pe=0.63, ga=2.08, sc=4.0, was=379e3),
          dict(MODEL, cyc=0.9, pe=0.45, ga=1.15, sc=2.0, gi=1100.0, dl=2300.0, bw=420.0, rl=3000.0, fix=50.0, hop=150.0, was=245e3),
          dict(MODEL, cyc=1.04, pe=0.55, ga=1.56, sc=3.8, fix=80.0, hop=180.0, same=90.0, was=291e3)]
STARTS = [(c, a) for c in (0.83, 0.87, 0.91, 0.95, 1.0, 1.1) for a in (1.3, 1.4, 1.5, 1.7)]
MID = dict(MODEL, cyc=0.9, pe=0.45, ga=1.45, look={"g": 500, "a": 300})
PASSES, SEED = 100, 1


def cost(o, M):
    k, n = o["c"]
    c = M["cyc"]
    if k == "n":
        return M["fix"] + max(64.0, n) * c
    if k == "ga":
        return M["fix"] + n * M["ga"] * c
    if k == "sc":
        return M["fix"] + n * M["sc"] * c
    if k == "pe":
        return n * M["pe"]
    if k == "gc":
        return 170.0 + 2 * n * c
    if k == "dma":
        return M["gi"] if o["e"] == "g" else M["si"]
    if k == "rem":
        return M["gi"]
    return 0.0


def start_up(o, M):
    return M["dl"] if o["c"][0] == "dma" else M["rl"] * 0.8


def finish(o, t, M, st):
    k, n = o["c"]
    if k in ("dma", "rem"):
        st[0] = max(st[0], t + start_up(o, M) * 0.7) + n / M["bw"]
        return st[0] + start_up(o, M) * 0.3
    if k == "arr":
        return t + M["rl"] * 0.3
    return t


def delay(d, o, M):
    if d["e"] == o["e"] and d["c"][0] not in ("dma", "rem"):
        return 0.0 if d["e"] == "p" else M["same"]
    return M["hop"]


def lists(ops, M, pr, back):
    n = len(ops)
    nxt = [[] for _ in ops]
    left = [0] * n
    for o in ops:
        for j in o["dep"]:
            a, b = (o["i"], j) if back else (j, o["i"])
            nxt[a].append(b)
            left[b] += 1
    co = [cost(o, M) for o in ops]
    lat = [finish(o, 0.0, M, [0.0]) for o in ops]
    rdy = [lat[i] if back else ops[i].get("rel", 0.0) for i in range(n)]
    free, pool = {}, {}
    for o in ops:
        free[o["e"]] = 0.0
        pool.setdefault(o["e"], [])
        if not left[o["i"]]:
            pool[o["e"]].append(o["i"])
    order, st, end = [], [0.0], [0.0] * n
    while len(order) < n:
        t, e = min((max(free[e], min(rdy[i] for i in lst)), e) for e, lst in pool.items() if lst)
        i = max((j for j in pool[e] if rdy[j] <= t + M["look"].get(e, 100.0)), key=lambda j: (pr[j], -j))
        pool[e].remove(i)
        t1 = max(t, rdy[i]) + co[i]
        if e != "x":
            free[e] = t1
        end[i] = t1 if back else finish(ops[i], t1, M, st)
        order.append(i)
        for j in nxt[i]:
            d = delay(ops[j], ops[i], M) + lat[j] if back else delay(ops[i], ops[j], M)
            rdy[j] = max(rdy[j], end[i] + d)
            left[j] -= 1
            if left[j] == 0:
                pool[ops[j]["e"]].append(j)
    return order, end


def kindof(o):
    w = o["tag"].split(" ")
    return w[0] + (str(int(w[1][1:]) % 3 if w[1] != "k%d" % (3 * RO) else 9) if len(w) > 1 and w[1][0] == "k" else "")


def schedule(ops, M, bump, rounds=3):
    pr = [0.0] * len(ops)
    succ = [[] for _ in ops]
    for o in ops:
        for j in o["dep"]:
            succ[j].append(o["i"])
    for o in reversed(ops):
        pr[o["i"]] = finish(o, cost(o, M), M, [0.0]) + max([pr[j] + delay(o, ops[j], M) for j in succ[o["i"]]] + [0.0])
    add = [o.get("bump", 0.0) + bump.get(kindof(o), 0.0) for o in ops]
    best = None
    for r in range(rounds):
        order, end = lists(ops, M, [p + a for p, a in zip(pr, add)], False)
        if best is None or max(end) < best[1]:
            best = (order, max(end))
        pr = lists(ops, M, end, True)[1]
    return best


def build(g, core, T, topo, plan):
    rank = T.rank_of(core)
    cores = list(T.cores)
    nr = len(cores)
    ops = []
    book = {}
    grids = {}

    def V(name, *idx):
        shp = SCRATCH[name][1][1:]
        if name not in grids:
            grids[name] = np.arange(int(np.prod(shp))).reshape(shp)
        el = grids[name][idx].reshape(-1) if idx else grids[name].reshape(-1)
        lo, hi = int(el.min()), int(el.max()) + 1
        cut = [0] + (np.nonzero(np.diff(el) != 1)[0] + 1).tolist() + [len(el)]
        if name == "ps":
            reg = [(name, lo // 512 * 512, (hi + 511) // 512 * 512, None)]
        elif len(cut) <= 5:
            reg = [(name, int(el[a]), int(el[b - 1]) + 1, None) for a, b in zip(cut, cut[1:])]
        else:
            reg = [(name, lo, hi, frozenset(el.tolist()))]
        return dict(ap=T[name][(slice(None),) + idx], reg=reg, n=len(el), two=SCRATCH[name][2] in (F16, B16, U16),
                    ps=name == "ps", ind=None)

    def C(name, a, b, s=None):
        return V(name, slice(a, b, s))

    def R(name, r, a=None, b=None, s=None):
        return V(name, r, slice(a, b, s))

    def P(a, n):
        return C("ps", a, a + n)

    def M(name, a=None, b=None, s=None):
        for buf, names in (("mh", MH), ("mb", MB), ("wr", WH)):
            if name in names:
                return R(buf, names.index(name), a, b, s)
        return C(name, a, b, s)

    def IND(name, a, b, off):
        w = C(name, a, b)
        return dict(ap=w["ap"].indirect(off["ap"]), reg=w["reg"], n=16 * off["n"], two=False, ps=False, ind=off["reg"])

    def op(e, fn, rd, wr, c, acc=None, tag=""):
        i = len(ops)
        dep, raw = set(), set()
        acts = []
        for v in rd:
            acts += [(r, False) for r in v["reg"]] + [(r, False) for r in (v["ind"] or [])]
        for v in wr:
            acts += [(r, True) for r in v["reg"]] + [(r, False) for r in (v["ind"] or [])]
        new = []
        for (name, lo, hi, st), w in acts:
            keep = []
            for ent in book.get(name, []):
                l2, h2, s2, j, w2, e2, a2 = ent
                hit = l2 < hi and lo < h2
                if hit and st is not None and s2 is not None:
                    hit = not st.isdisjoint(s2)
                elif hit and st is not None and h2 - l2 < 600:
                    hit = any(l2 <= u < h2 for u in st)
                elif hit and s2 is not None and hi - lo < 600:
                    hit = any(lo <= u < hi for u in s2)
                if hit and (w or w2 or (name == "ps" and e != e2)) and not (acc is not None and a2 == acc):
                    dep.add(j)
                    if w2:
                        raw.add(j)
                if w and acc is None and ((st is None and lo <= l2 and h2 <= hi) or (st is not None and s2 is not None and s2 <= st)):
                    continue
                keep.append(ent)
            book[name] = keep
            if w or name not in ONCE:
                new.append((name, (lo, hi, st, i, w, e, acc)))
        for name, ent in new:
            book.setdefault(name, []).append(ent)
        ops.append(dict(i=i, e=e, fn=fn, dep=dep, raw=raw, c=c, acc=acc, tag=tag, stop=[True]))
        return ops[-1]

    def aps(x):
        return x["ap"] if isinstance(x, dict) else x

    def sc_rd(*xs):
        return [x for x in xs if isinstance(x, dict)]

    def kind(out, ins, full):
        if out["ind"] is not None:
            return ("sc", ins[0]["n"])
        if ins[0]["ind"] is not None:
            return ("ga", out["n"])
        return ("n", out["n"] * full)

    def ts(out, in0, s1, s2, o0, o1=None, tag=""):
        def fn():
            if o1 is None:
                return g.vector.tensor_scalar(out["ap"], in0["ap"], aps(s1), None, o0)
            return g.vector.tensor_scalar(out["ap"], in0["ap"], aps(s1), aps(s2), o0, o1)
        return op("v", fn, [in0] + sc_rd(s1, s2), [out], kind(out, [in0], 0.5 if out["two"] and in0["two"] else 1.0), tag=tag)

    def tt(out, in0, in1, o, tag=""):
        return op("v", lambda: g.vector.tensor_tensor(out["ap"], in0["ap"], in1["ap"], o), [in0, in1], [out],
                  kind(out, [in0], 1.0 if in0["ps"] or in1["ps"] else 2.0), tag=tag)

    def cp(out, in0, tag=""):
        return op("v", lambda: g.vector.tensor_copy(out["ap"], in0["ap"]), [in0], [out],
                  kind(out, [in0], 0.5 if out["two"] and in0["two"] else 1.0), tag=tag)

    def ms(out, val, tag="k"):
        return op("v", lambda: g.vector.memset(out["ap"], val), [], [out], ("n", out["n"] * (0.5 if out["two"] else 1.0)), tag=tag)

    def act(out, in0, f, bias=0.0, scale=1.0, tag=""):
        return op("a", lambda: g.scalar.activation(out["ap"], in0["ap"], f, bias=aps(bias), scale=aps(scale)), [in0] + sc_rd(bias, scale),
                  [out], kind(out, [in0], 1.0), tag=tag)

    turns = {}

    def E(name):
        turns[name] = turns.get(name, -1) + 1
        return plan["eng"][name][turns[name]]

    def plus(out, in0, c, tag):
        return ts(out, in0, c, None, A.add, tag=tag) if E(tag) == "v" else act(out, in0, F.Identity, bias=c, tag=tag)

    def iota(out, pattern, base, mult, whole=False):
        def fn():
            if whole:
                return g.iota(out["ap"], pattern, base, mult)
            return g.iota(out["ap"], pattern, base, mult, allow_small_or_imprecise_dtypes=True)
        return op("g", fn, [], [out], ("gc", out["n"]), tag="k")

    def sel(out, in0, pattern, cmp, fill, base, mult):
        return op("g", lambda: g.affine_select(out["ap"], in0["ap"], pattern, cmp, fill, base, mult), [in0], [out], ("gc", out["n"]), tag="k")

    def mm(trip, start=True, stop=True, acc=None, wide=1, tag=""):
        o = {}

        def fn():
            r = None
            for k, (out, l, rhs) in enumerate(trip):
                r = g.tensor.matmul(out["ap"], l["ap"], rhs["ap"], start and k == 0, o["op"]["stop"][0] and k == len(trip) - 1)
            return r
        rd = [t[1] for t in trip] + [t[2] for t in trip]
        o["op"] = op("p", fn, rd, [trip[0][0]], ("pe", sum(max(64, t[2]["n"]) * wide for t in trip)), acc=acc, tag=tag)
        o["op"]["stop"][0] = stop
        return o["op"]

    def raw(ap, n=0, reg=()):
        return dict(ap=ap, reg=list(reg), n=n, two=False, ps=False, ind=None)

    def dma(e, out, in0, nbytes, add=False, grp=None, tag=""):
        q = {"g": g, "s": g.sync, "a": g.scalar}[e]

        def fn():
            if add:
                return q.dma_start(out["ap"], in0["ap"], accum_op=A.add)
            return q.dma_start(out["ap"], in0["ap"])
        o = op(e, fn, [in0] + ([out] if add else []), [out], ("dma", nbytes * (2 if add else 1)), acc=grp, tag=tag)
        o["grp"] = grp
        return o

    landed = {}

    def remote(sem, moves, guard, nbytes, tag):
        n = len(moves)

        def fn(lsem):
            tr = []
            for b, (dst, _, srcs, alu, out) in enumerate(moves):
                rid, pid, _ = topo.addr(dst)
                tr.append(RemoteDMATransfer(dst_ids=[DstId(rid=rid, pnc=pid)], dma_engine_mask=sum(1 << u for u in topo.engines(core, dst)[b::n]),
                                            remote_sem=T.sem[sem], srcs=[s["ap"] for s in srcs], dsts=[out["ap"]], alu_op=alu))
            g.remote_dma_fused(tr, local_sem=lsem)
        o = op("g", fn, [s for m in moves for s in m[2]], guard, ("rem", nbytes), tag=tag)
        o["cnt"] = sum(len(topo.engines(core, m[0])) // n for m in moves)
        landed[sem] = landed.get(sem, 0) + sum(len(topo.engines(m[1], core)) // n for m in moves)
        a = op("x", None, [], [m[4] for m in moves], ("arr", 0), tag="arr " + tag)
        a["dep"].add(o["i"])
        a["sem"] = (sem, landed[sem])

    def send(j, src0, src1, dname, guard):
        remote("arr%d" % j, [(cores[(rank + DSH[b]) % nr], cores[(rank - DSH[b]) % nr], [src], 0, C(dname, NV + b * GH, NV + (b + 1) * GH))
                             for b, src in enumerate((src0, src1))], guard, 256 * 1024, "send %d" % j)

    def turn(qs, name, src, grp, tag="turn"):
        nb_ = 2 if SCRATCH[name][2] == B16 else 4
        return [dma(q, raw(T[name][a:b, :], reg=V(name)["reg"]), raw(src[0][c:d, 0:GH], reg=src[1]), (b - a) * GH * nb_, grp=grp, tag=tag)
                for q, (a, b, c, d) in zip(qs, ((0, 112, 16, 128), (112, 128, 0, 16)))]

    def wrap(out, mat, src, a, n):
        return [(out, M(mat, 15 - m, 143 - m), C(src, a + m, a + 16 * n, 16)) for m in range(16)]

    def rows(r):
        return raw(T.tb[r:128:16, 0:TREAL], reg=C("tb", 0, TREAL)["reg"])

    W = ["w0", "w1", "w2", "w3"]
    XN = ["xn0", "xn1"]
    OF = ["of0", "of1"]
    B4, B5, B6, B7 = 2048, 2560, 3072, 3584

    dma("s", C("w0", 0, GH), raw(T.x[:, 0:GH]), 128 * 1024)
    turn("as", "rs0", (T.x, []), "rs")
    send(0, C("w0", 0, GH), V("rs0"), "w0", [])
    ops[-1]["rel"] = 7500.0
    dma("a", C("n32", 0, 640), raw(T.nb[:]), 128 * 2560, grp="n32")
    dma("s", C("n32", 640, 664), raw(T.lb[:]), 128 * 96, grp="n32")
    for o in ops:
        o["bump"] = 1e5
    for k, nm in enumerate(("pk", "pj", "pl", "hq")):
        dma("s", C("li", 24 * k, 24 * (k + 1)), raw(T[nm][:]), 128 * 96, grp="li")
    dma("s", C("w0", GH, NV), raw(T.x[:, GH:NV]), 128 * 4 * (NV - GH))
    for a0, a1 in sorted({u[1:3] for u in plan[0] if "v" in u[3]}):
        dma("s", C("w2", a0, a1), raw(T.x[:, a0:a1]), 128 * 4 * (a1 - a0), grp="w2")
    for o in ops:
        o["bump"] = o.get("bump", 0.0) + 1e5
    plus(V("of0"), C("n32", 0, 640), 0.0, "of0")
    ms(V("onef"), 1.0)["bump"] = 1e5
    sel(V("idf"), V("onef"), [[-1, 128]], A.is_equal, 0.0, 0, 1)
    sel(V("bof"), V("onef"), [[-16, 8], [0, 16]], A.is_ge, 0.0, 0, 1)
    sel(V("bof"), V("bof"), [[16, 8], [0, 16]], A.is_ge, 0.0, 15, -1)
    iota(V("cf"), [[1, TB]], 0, 0)
    iota(V("ki"), [[0, 2]], 0, 1, True)
    iota(V("dum"), [[16, 32]], TREAL, 1)
    ms(V("neg"), -1.0)
    iota(C("tb", TREAL, TW), [[0, TW - TREAL]], 0, 0)["bump"] = 1e5
    for r in (2, 3):
        dma("s", raw(T.tb[r:128:4, 0:TREAL], reg=C("tb", 0, TREAL)["reg"]), C("tb", TREAL, TREAL + TREAL // 4), 330000, grp="zero", tag="zero")
    ms(V("mh", slice(MH.index("l1"), None)), 0.0)
    ms(V("mb"), 0.0)
    ms(V("wr"), 0.0)
    ms(V("y2b"), 0.0)
    ms(V("ones"), 1.0)
    ms(V("nf", slice(None), 160), -CEN - 1)
    ms(V("pf", slice(None), 160), 160 - CEN)
    ms(V("cw"), 0.0)
    ts(C("ki", 0, 1), C("ki", 0, 1), 15, None, A.bitwise_and, tag="k")
    ts(C("ki", 1, 2), C("ki", 1, 2), 3, None, A.bitwise_and, tag="k")
    cp(V("kf"), V("ki"), tag="k")
    KM = C("kf", 0, 1)
    ts(V("p16"), C("cf", 0, 16), KM, None, A.is_equal, tag="k")
    ts(V("r4"), C("cf", 0, 4), C("kf", 1, 2), None, A.is_equal, tag="k")

    def S(a):
        return C("p16", a, a + 1)

    def R4(r):
        return C("r4", r, r + 1)

    def K(n):
        return C("col", n, n + 1)

    def kon(out, in0, s1, s2=None, o1=A.mult):
        if s2 is None:
            return act(out, in0, F.Identity, scale=s1, tag="k")
        if o1 == A.add:
            return act(out, in0, F.Identity, scale=s1, bias=s2, tag="k")
        return ts(out, in0, s1, s2, A.mult, o1, tag="k")
    ID, BO = (lambda a, s: C("idf", a, 128, s)), (lambda a, s: C("bof", a, 128, s))
    for nm, val in (("i161", 161.0), ("im527", -527.0), ("imk", -1024.0), ("i16", 1.0 / 16), ("im64", -64.0), ("im16", -1.0 / 16), ("i64", 64.0), ("im1", -1.0), ("i1", 1.0),
                    ("i4k", 4096.0), ("id2", 2.0)):
        if nm in ("i161", "im527", "imk"):
            kon(M(nm), V("idf"), val)
        else:
            sel(M(nm), C("tb", TW - 128, TW), [[-1, 128]], A.not_equal, val, 0, 1)
    kon(V("cb"), V("onef"), -7.5 / 16)
    kon(K(0), R4(2), -1.0, 1.0, A.add)
    kon(K(1), R4(2), 30000.0)
    kon(K(2), KM, 1.0, -CEN, A.add)
    kon(K(3), KM, float(TB), -CEN, A.add)
    kon(K(4), KM, -SLOPE, TOPW - 512.0, A.add)
    kon(K(5), S(6), BIG / 8)
    kon(K(7), S(3), -1.0)
    ts(K(8), S(6), S(2), 1e28, A.subtract, A.mult, tag="k")
    ts(K(9), R4(1), R4(2), -8.0, A.add, A.mult, tag="k")
    kon(K(10), K(9), 1.0, R4(0), A.add)
    kon(K(11), R4(0), -1.0)
    kon(R("sf", 0), V("cf"), 16.0, K(2), A.add)
    kon(R("sf", 1), V("cf"), 1.0, K(3), A.add)
    kon(C("cw", 0, 4), C("p16", 1, 16, 4), 1.0, S(6), A.add)
    kon(V("cl"), C("cf", 0, 8), -16 * SLOPE / 256)
    act(V("thr"), C("cf", 0, 128), F.Exp, bias=TOPW + math.log(6.5), scale=-SLOPE, tag="k")
    for nm, a, s, src, f in (("l1", 0, 4, ID(0, 4), 1.0), ("l1", 1, 4, ID(0, 4), 1.0), ("l1", 2, 4, BO(2, 4), S(3)),
                             ("l2", 0, 4, BO(0, 4), K(7)), ("l2", 6, 8, BO(6, 8), K(7)), ("l3", 1, 4, BO(1, 4), K(7)), ("l3", 2, 8, BO(2, 8), K(7)),
                             ("lb", 0, 1, BO(0, 1), S(3)), ("lt", 0, 4, BO(0, 4), S(3)), ("lt", 1, 4, BO(1, 4), S(7)),
                             ("luu", 2, 4, BO(2, 4), S(12)), ("lul", 0, 1, ID(0, 1), 1.0), ("lul", 2, 4, ID(0, 4), 1.0),
                             ("l4", 2, 16, BO(2, 16), K(10)), ("l4", 6, 16, ID(3, 16), 1.0), ("lpen", 0, 1, BO(0, 1), K(8)),
                             ("bo", 0, 1, BO(0, 1), 1.0), ("lml", 0, 4, ID(1, 4), BIG), ("lml", 1, 4, ID(1, 4), BIG), ("lml", 2, 4, ID(1, 4), BIG)):
        kon(M(nm, a, 128, s), src, f)
    for a, f in enumerate((-BIG, -BIG, -BIG, 0.0)):
        ts(M("lmu", a, 128, 4), ID(1, 4), f, K(5), A.mult, A.add, tag="k")
    kon(V("tri"), BO(1, 4), K(11))
    sel(V("tri"), V("tri"), [[4, 32]], A.is_gt, 0.0, 0, -1)
    sel(V("tri"), V("tri"), [[4, 32]], A.not_equal, 1.0, 0, -1)
    cp(M("l4", 1, 128, 4), V("tri"), tag="k")
    for nm, src, f in (("xw1", BO(0, 16), R4(1)), ("xwp", BO(0, 16), 4096.0), ("xwm", BO(0, 16), -4096.0), ("y2", ID(2, 16), 1.0),
                       ("y3", ID(3, 16), 1.0), ("y6", ID(6, 16), 1.0), ("y10", ID(10, 16), 1.0), ("y2b", ID(2, 16), 1.0)):
        ts(M(nm, 15, 143, 16), src, f, None, A.mult, tag="k")
    act(V("nf", slice(None), slice(0, 160)), C("n32", 0, 640), F.Identity, bias=-CEN, tag="tab")
    ts(C("sd", 0, 664), V("n32"), float(NV), CEN, A.min, A.subtract, tag="tab")
    ts(C("ss", 0, 664), C("sd", 0, 664), 1.0 / 16, 1100 + 64 - 7.5 / 16, A.mult, A.add, tag="tab")
    for a, b in ((0, 480), (480, 664)):
        o = B6 if a == 0 else B7
        mm([(P(o, b - a), M(m), C(s, a, b)) for m, s in (("i161", "sd"), ("imk", "ss"), ("imk", "ss"), ("im527", "ss"))], tag="tab")
    c0 = TB * CEN + 2575.0 * 1100 - CEN
    act(V("pf", slice(0, 3), slice(0, 160)), P(B6, 480), F.Identity, bias=c0, tag="tab")
    act(R("pf", 3, 0, 160), P(B7, 160), F.Identity, bias=c0, tag="tab")
    act(V("pb"), P(B7 + 160, 24), F.Identity, bias=c0, tag="tab")
    ts(V("pbu"), V("pb"), CEN, None, A.add, tag="tab")
    for p in range(4):
        dma("s", rows(4 * p), R("nf", p), 200000, grp="tab", tag="tab")
        dma("s", rows(4 * p + 1), R("pf", p), 200000, grp="tab", tag="tab")
    for r in range(2):
        dma("s", rows(4 * r + 3), R("sf", r), 200000, grp="tab", tag="tab")
    for u in range(3):
        cp(V("lu", slice(None), slice(8 * u, 8 * u + 8)), C("li", 24 * u, 24 * u + 24), tag="tab")
    for t in range(RO):
        act(C("mk", 384 * t, 384 * t + 384), IND("cw", 0, 8, R("lu", t)), F.Identity, tag="mask")
    act(V("hq16"), C("li", 72, 96), F.Identity, tag="k")
    for a0, a1 in STR:
        plus(C("xn0", a0, a1), C("w0", a0, a1), -2048.0, "xn")

    def marks():
        dma("s", C("aw", 0, NV), raw(T.am[:]), 128 * 2 * NV)["rel"] = 40000.0
        for o in turn("ss", "ra", (T.am, []), "ra"):
            o["rel"] = 40000.0
        send(10, C("aw", 0, GH), V("ra"), "aw", [])

    def D(name, pc, p, a, b):
        return R(name, p, a, b)

    def piece(k, of, pc):
        p0, a0, a1, who, sg, parts = pc
        for p, e in enumerate(who, p0):
            tag = " k%d a%d p%d" % (k, a0, p)
            win = IND(W[k % 4], 0, NW, C(of, (p * NV + a0) // 16, (p * NV + a1) // 16))
            d = D("d1", pc, p, a0, a1)
            if e == "v":
                tt(d, win, C(XN[k % 2] if k else "w2", a0, a1), A.subtract, tag="gv" + tag)
                continue
            act(d, win, F.Identity, bias=2048.0 if k == 0 else 0.0, scale=-1.0, tag="ga" + tag)
            if e == "a":
                dma("g", d, C(XN[k % 2], a0, a1), 256 * (a1 - a0), add=True, tag="add" + tag)
                continue
            o = plan["pb"][p % 2]
            for b in range(a0, a1, 512):
                u = P(o + b - a0, min(512, a1 - b))
                mm([(u, M("i1"), D("d1", pc, p, b, b + u["n"])), (u, M("i1"), C(XN[k % 2], b, b + u["n"]))], tag="pd")
            ts(D("d3", pc, p, a0, a1), P(o, a1 - a0), -2047.0, 2047.0, A.max, A.min, tag="cp" + tag)
        for b in range(a0, a1, (a1 - a0) // parts):
            tag = " k%d a%d p%d" % (k, b, p0)
            d, s, c = (V(u, slice(p0, p0 + len(who)), slice(b, b + (a1 - a0) // parts)) for u in ("d1", "d2", "d3"))
            if who[0] == "p":
                d = c
            if sg == "v":
                ts(s, d, -1.0, 1.0, A.max, A.min, tag="s" + tag)
            if who[0] != "p" and k < 3 * RO:
                ts(c, d, -2047.0, 2047.0, A.max, A.min, tag="c" + tag)
            if sg == "a":
                act(s, d, F.Sign, tag="s" + tag)
        return "d3" if k < 3 * RO or who[0] == "p" else "d1"

    def sweep(k, of):
        wn, xn, xo = W[(k + 1) % 4], XN[(k + 1) % 2], XN[k % 2]
        cn = {}
        for a0, a1, col in plan.get(("str", k % 3), plan["str"]):
            blocks = [(b, min(b + 512, a1)) for b in range(a0, a1, 512)]
            bank = [P(col + b0 - a0, b1 - b0) for b0, b1 in blocks]
            for (b0, b1), ps in zip(blocks, bank):
                mm([(ps, M("i1"), C(xo, b0, b1)),
                    (ps, raw(T.cb[0:1, :], reg=V("cb")["reg"]), raw(T.ones[0:1, 0:b1 - b0], n=b1 - b0, reg=V("ones")["reg"]))], stop=False, tag="m0")
            for n, pc in enumerate(plan[k]):
                p0, c0, c1, who = pc[:4]
                if c1 <= a0 or a1 <= c0:
                    continue
                if n not in cn:
                    cn[n] = piece(k, of, pc)
                for p, e in enumerate(who, p0):
                    ms_, mc_ = ("im64", "i16") if e == "v" else ("i64", "im16")
                    for (b0, b1), ps in zip(blocks, bank):
                        e0, e1 = max(b0, c0), min(b1, c1)
                        if e0 < e1:
                            mm([(P(col + e0 - a0, e1 - e0), M(ms_), D("d2", pc, p, e0, e1))], start=False, acc=(k, b0), tag="ms")
                            mm([(P(col + e0 - a0, e1 - e0), M(mc_), D(cn[n], pc, p, e0, e1))], start=False, acc=(k, b0), tag="mc")
            ts(C(wn, a0, a1), P(col, a1 - a0), -2048.0, 2047.0, A.max, A.min, tag="fin k%d b%d" % (k, a0))
            if a0 == 0:
                rs = "rs%d" % ((k + 1) % 2)
                turn("ss", rs, (T[wn], C(wn, 0, GH)["reg"]), ("rs", k))
                send(k + 1, C(wn, 0, GH), V(rs), wn, [C(W[(k + 2) % 4], NV, NW)])
            for b0, b1 in plan["cast"]:
                if a0 < b1 <= a1:
                    sel(C(xn, b0, b1), C(wn, b0, b1), [[0, b1 - b0]], A.is_gt, 0.0, 1, 0)["tag"] = "xn k%d b%d" % (k, b0)

    def put(skip, src, of, n):
        mm(skip, tag="wrap")
        ts(V("ls"), skip[0][0], 0.0, 4096.0, A.max, A.min, tag="put")
        mm([(P(B4, 32), M("i1"), V("pl16")), (P(B4, 32), M("imk"), V("neg"))] + [(P(B4 + 8 * r, 8), M("i1"), V("ls")) for r in range(4)], tag="wrap")
        tt(V("ou"), P(B4, 32), V("dum"), A.min, tag="put")
        cp(IND("tb", 0, TW, V("ou")), V(src), tag="scatter")
        h = plan["halves"]
        for u in range(h):
            for p in range(4 * u // h, 4 * (u + 1) // h):
                dma("s", R("nf", p), rows(4 * p), 150000, grp=("relist", n, u), tag="relist")
            plus(C(of, 640 * u // h, 640 * (u + 1) // h), V("nf", slice(4 * u // h, 4 * (u + 1) // h), slice(0, 160)), CEN, "relisted")

    def lanes(t, of):
        GA, GC, GB, GD = (C("gg", 128 * r, 128 * (r + 1)) for r in range(4))
        MK, MJ, ML = (C("mk", 384 * t + 128 * u, 384 * t + 128 * u + 128) for u in range(3))
        FA, FD = C("fm", 0, 128), C("fm", 128, 256)
        PB = C("pbu", 8 * t, 8 * t + 8)
        tt(C("t1", 0, 128), IND("tb", 0, TW, PB), MK, A.mult, tag="L1")
        tt(C("t1", 128, 256), IND("tb", 0, TW, PB), MJ, A.mult, tag="L1")
        mm(wrap(P(B4, 16), "xw1", "t1", 0, 16), tag="wrap")
        mm([(P(B4 + 16, 8), M("i1"), C("pb", 8 * t, 8 * t + 8))], tag="wrap")
        ts(C("plu", 0, 24), P(B4, 24), CEN, None, A.add, tag="L1")
        tt(V("t2"), IND("tb", 0, TW, C("plu", 8, 16)), ML, A.mult, tag="L2")
        mm(wrap(P(B4 + 24, 8), "xw1", "t2", 0, 8), tag="wrap")
        ts(C("plu", 24, 32), P(B4 + 24, 8), CEN, None, A.add, tag="L2")
        plus(V("pl16"), P(B4, 32), 0.0, "pl")
        act(V("gg"), IND("tb", 0, TW, V("plu")), F.Identity, scale=K(0), bias=K(1), tag="L3")
        for h, (own, first, second) in enumerate(((GA, GB, GC), (GD, GC, GB))):
            mm([(P(B6 + 128 * h, 128), M(m), u) for m, u in (("l1", own), ("l2", first), ("l3", second))], tag="good")
        ts(V("ee"), P(B6, 256), 0.0, None, A.is_equal, tag="good")
        mm([(P(B7, 256), M("l4"), V("ee"))], tag="good")
        ts(V("fm"), P(B7, 256), 0.5, None, A.is_ge, tag="good")
        mm([(P(B5, 512), M("lb"), V("gg"))], tag="rw")
        plus(V("rw"), P(B5, 512), 0.0, "rw")
        mm(wrap(P(B4, 32), "y3", "gg", 0, 32), tag="wrap")
        plus(V("wh"), P(B4, 32), 0.0, "rw")
        mm(wrap(P(B4, 8), "y2b", "fm", 0, 8) + wrap(P(B4, 8), "y2b", "fm", 128, 8) + [(P(B4, 8), M("i1"), V("cl"))], tag="good")
        act(V("ww"), P(B4, 8), F.Exp, scale=256.0, bias=K(4), tag="good")
        for o, lu, lm in ((B6, "lul", "lml"), (B7, "luu", "lmu")):
            mm([(P(o, 512), M(lu), V("gg"))] + [(P(o + 128 * r, 128), M("lt"), u) for r, u in enumerate((GC, GA, GD, GB)) if o == B7]
               + [(P(o + 128 * r, 128), M(lm), u) for r, u in enumerate((FA, ML, MK, FD))], tag="new")
        plus(V("no1"), P(B6, 512), 0.0, "old")
        tt(V("no"), P(B7, 512), V("no1"), A.min, tag="new")
        for p, (y, src) in enumerate((("y3", "gg"), ("y2", "no"), ("y6", "no"), ("y10", "no"))):
            mm(wrap(P(B6 + 32 * p, 32), y, src, 0, 32), tag="sl")
        plus(V("sl"), P(B6, 128), CEN, "sl")
        mm([(P(B5, 128), M("lpen"), FA), (P(B5, 128), M("lpen"), FD)], stop=False, tag="pm")
        for n in range(32):
            c, r, q = n // 4, n % 4, 4 * (n % NQ)
            ts(V("qq", slice(q, q + 4), slice(16 * c, 128)), V("rw", slice(None), slice(16 * c, 128)), R("wh", r, c, c + 1), C("ww", c, c + 1),
               A.is_equal, A.mult, tag="pair")
            mm([(P(B5 + 16 * c, 128 - 16 * c), M("bo"), R("qq", q + u, 16 * c, 128)) for u in range(4)], start=False, acc=("pm", t), tag="pm")
        tt(V("lz"), P(B5, 128), V("thr"), A.is_ge, tag="lose")
        put(wrap(P(B4 + 64, 8), "xwp", "lz", 0, 8), "no", of, 2 * t)

    def stress(k, z):
        w, at = W[k % 4], " k%d" % k
        off = 2048.0 if k == 0 else 0.0
        own = R("xo", z)
        who, cuts = "".join(E("sa") for p in range(3)), plan["st"][z]
        act(own, IND(w, 0, NW, C("sl", 0, 32)), F.Identity, bias=off, scale=-1.0, tag="xo" + at)
        mm([(P(B7, 256), M("i1"), R("xo", z, 128 * z, 128 * z + 256))]
           + [(P(B7 + 128 * j, 128), M("im1"), R("xo", z, 128 * r, 128 * r + 128)) for j, r in enumerate(((2, 3), (0, 3))[z])], tag="sp" + at)
        ts(C("sd", 0, 256), P(B7, 256), -2047.0, 2047.0, A.max, A.min, tag="cs" + at)
        for p, e in enumerate(who):
            d, lst = C("sd", 256 + 512 * p, 768 + 512 * p), IND(w, 0, NW, C("sl", 32 * p + 32, 32 * p + 64))
            if e == "v":
                tt(d, lst, own, A.add, tag="sa%s p%d" % (at, p))
            else:
                act(d, lst, F.Identity, bias=-off, tag="sa%s p%d" % (at, p))
                dma("g", d, own, 256 * 512, add=True, tag="sadd%s p%d" % (at, p))
        for a, b in zip(cuts, cuts[1:]):
            d, s = C("sd", a, b), C("ss", a, b)
            if E("ss") == "v":
                ts(s, d, -1.0, 1.0, A.max, A.min, tag="ss%s a%d" % (at, a))
            else:
                act(s, d, F.Sign, tag="ss%s a%d" % (at, a))
            if b > 256:
                ts(C("sc", max(a, 256), b), C("sd", max(a, 256), b), -2047.0, 2047.0, A.max, A.min, tag="cs" + at)
            bank = B6 if b - a > 512 or a % 1024 >= 512 else B7
            for c in range(a, b, 512):
                u = P(bank + c - a, min(512, b - c))
                mm([(u, M("imk"), C("ss", c, c + u["n"]))]
                   + [(P(bank + e0 - a, e1 - e0), M("i1"), C(nm, e0, e1)) for nm, e0, e1 in (("sd", c, min(256, b)), ("sc", max(c, 256), c + u["n"])) if e0 < e1],
                   tag="su" + at)
            act(C("sq", bank - B6, bank - B6 + b - a), P(bank, b - a), F.Square, tag="sq" + at)
            mm([(P(B5, 128), V("id2" if c < 256 else "idf"), C("sq", bank - B6 + c - a, bank - B6 + c - a + 128)) for c in range(a, b, 128)],
               start=a == 0, stop=b == 1792, wide=4, tag="st" + at)
        return P(B5, 128)

    def votes(t, tot, of):
        tt(V("vz"), tot, V("f1"), A.is_gt, tag="vote")
        o = P(B4 + 64, 8)
        put([(o, M("i64"), V("ls")), (o, M("i4k"), C("hq16", 8 * t, 8 * t + 8))] + wrap(o, "xwm", "vz", 0, 8), "gg", of, 2 * t + 1)

    def last(k, of):
        bank = {}
        for n, pc in enumerate(plan[k]):
            p, a0, a1 = pc[:3]
            cn = piece(k, of, pc)
            e, (tn, t0) = "e%d" % (n % 3), (("t0", 0), ("t3", 0), ("t4", 0), ("tb", 0), ("tb", 1024), ("tb", 2048))[n % 6]
            nb = 1024 * (n % 3)
            for b0 in range(a0, a1, 512):
                b1 = min(a1, b0 + 512)
                u = P(nb + b0 - a0, b1 - b0)
                mm([(u, M("imk"), D("d2", pc, p, b0, b1)), (u, M("i1"), D(cn, pc, p, b0, b1))], tag="fu")
            ev, tv = C(e, 0, a1 - a0), C(tn, t0, t0 + a1 - a0)
            act(R("eq", n % 3, 0, a1 - a0), P(nb, a1 - a0), F.Square, scale=math.sqrt(65535.0) / 1023, tag="fq")
            act(ev, R("eq", n % 3, 0, a1 - a0), F.Exp, scale=-2.0 ** -19 * 1023 * 1023 / 65535, tag="fe")
            tt(tv, IND("aw", 0, NW, C(of, (p * NV + a0) // 16, (p * NV + a1) // 16)), ev, A.mult, tag="mk a%d p%d" % (a0, p))
            yv = raw(T.y[:, a0:a1], reg=[("y", a0, a1, None)])
            if a0 < plan["ys"]:
                dma("g" if p else "s", yv, tv, 512 * (a1 - a0), add=p > 0, tag="y")
                continue
            at = bank.setdefault(a0, [B6 + 512 * (len(bank) % 2), 0])
            at[1] += 1
            if at[1] < 4 or plan["yc"] == "a":
                mm([(P(at[0], a1 - a0), V("idf"), tv)], start=at[1] == 1, stop=False, acc=None if at[1] == 1 else ("y", a0), wide=4, tag="ys")
            if at[1] == 4:
                yo = C("sq", at[0] - B6, at[0] - B6 + a1 - a0)
                if plan["yc"] == "a":
                    act(yo, P(at[0], a1 - a0), F.Identity, tag="yc")
                else:
                    tt(yo, P(at[0], a1 - a0), tv, A.add, tag="yc")
                dma("s", yv, yo, 512 * (a1 - a0), tag="y")

    for t in range(RO):
        k = 3 * t
        lanes(t, OF[1])
        sweep(k, OF[0])
        if t == 0:
            marks()
        plus(V("f1"), stress(k, 0), 0.0, "f1")
        sweep(k + 1, OF[1])
        tot = stress(k + 2, 1)
        votes(t, tot, OF[0])
        sweep(k + 2, OF[1])
    last(3 * RO, OF[0])
    members = {}
    for o in ops:
        if o.get("grp"):
            members.setdefault(o["grp"], []).append(o["i"])
    for o in ops:
        for j in list(o["dep"]):
            if ops[j].get("grp") and ops[j]["grp"] != o.get("grp"):
                o["dep"].update(members[ops[j]["grp"]])
    return ops


def fix_stops(ops, order):
    lastacc = {}
    for i in order:
        o = ops[i]
        if o["e"] == "p" and o["acc"] is not None:
            o["stop"][0] = False
            lastacc[o["acc"]] = o
    for o in lastacc.values():
        o["stop"][0] = True


def emit(g, T, ops, order):
    Q = {"g": g, "v": g.vector, "a": g.scalar, "p": g.tensor, "s": g.sync}
    fix_stops(ops, order)
    mark, seq, grp, total = {}, {}, {}, {}
    nsem = [0]
    for i in order:
        o = ops[i]
        k = o["c"][0]
        if k == "arr":
            mark[i] = o["sem"]
            total[o["sem"][0]] = max(o["sem"][1], total.get(o["sem"][0], 0))
        elif k in ("dma", "rem"):
            key = o.get("grp") or ("own", i)
            if key not in grp:
                grp[key] = "m%d" % nsem[0]
                nsem[0] += 1
            total[grp[key]] = total.get(grp[key], 0) + (16 if k == "dma" else o["cnt"])
            mark[i] = (grp[key], None)
        else:
            seq[o["e"]] = seq.get(o["e"], 0) + 1
            mark[i] = ("q" + o["e"], seq[o["e"]])
    for i in order:
        if mark[i][1] is None:
            mark[i] = (mark[i][0], total[mark[i][0]])
    known = {e: {} for e in Q}
    clock = {}
    waits = {}
    need = set()
    for i in order:
        o = ops[i]
        e = o["e"]
        if e == "x":
            clock[i] = {mark[i][0]: mark[i][1]}
            continue
        kn = known[e]
        ws = {}
        for j in sorted(o["dep"], key=lambda u: -mark[u][1] if mark[u][0][0] == "q" else 0):
            s, c = mark[j]
            if s == "qp" and e == "p":
                continue
            if kn.get(s, 0) >= c:
                continue
            ws[s] = max(ws.get(s, 0), c)
            for s2, c2 in clock[j].items():
                if kn.get(s2, 0) < c2:
                    kn[s2] = c2
        waits[i] = ws
        for s, c in ws.items():
            if s[0] == "q":
                need.add((s, c))
        clock[i] = dict(kn)
        clock[i][mark[i][0]] = max(clock[i].get(mark[i][0], 0), mark[i][1])
    count = {}
    for s in ("qv", "qa", "qp", "qg"):
        pl = sorted(c for s2, c in need if s2 == s)
        for n, c in enumerate(pl):
            count[(s, c)] = n + 1
    users, raises = {}, {}
    for i in order:
        raises.setdefault(mark[i][0], []).append(i)
        for s in waits.get(i, {}):
            users.setdefault(s, []).append(i)
    real, base, mine, used = {}, {}, {}, 0
    for i in order:
        o = ops[i]
        s = mark[i][0]
        if o["c"][0] not in ("dma", "rem") or s in real:
            continue
        pool = mine.setdefault((o["e"] == "g", o["c"][0]), [])
        for n, s0 in enumerate(pool if o["e"] == "g" else []):
            if s0 in users and all(clock[j].get(s0, 0) >= total[s0] and all(clock[j].get(mark[u][0], 0) >= mark[u][1] and mark[u][0] != s for u in users[s0])
                                   for j in raises[s]):
                real[s], base[s] = real[s0], base[s0] + total[s0]
                pool.pop(n)
                break
        else:
            real[s], base[s] = "m%d" % used, 0
            used += 1
        pool.append(s)
    waited = {}
    for i in order:
        o = ops[i]
        e = o["e"]
        if e == "x":
            continue
        for s, c in waits[i].items():
            Q[e].wait_ge(T.sem[real.get(s, s)], count.get((s, c), c) + base.get(s, 0))
            waited[s] = max(waited.get(s, 0), c)
        k = o["c"][0]
        s = T.sem[real.get(mark[i][0], mark[i][0])]
        if k == "rem":
            o["fn"](s)
        elif k == "dma":
            o["fn"]().then_inc(s, 16)
        else:
            r = o["fn"]()
            if mark[i] in count:
                r.then_inc(s, 1)
    for s, c in total.items():
        if waited.get(s, 0) < c:
            g.sync.wait_ge(T.sem[real.get(s, s)], c + base.get(s, 0))
    return used


def polish(ops, order, models, tries, seed=1, heat=0.0):
    n = len(ops)
    eng = ["vapgsx".index(o["e"]) for o in ops]
    succ = [[] for _ in ops]
    for o in ops:
        for j in o["dep"]:
            succ[j].append(o["i"])
    tab = [([cost(o, M) for o in ops], [[(j, delay(ops[j], o, M)) for j in o["dep"]] for o in ops],
            [[(j, delay(o, ops[j], M)) for j in succ[o["i"]]] for o in ops],
            [o["c"][1] / M["bw"] if o["c"][0] in ("dma", "rem") else -1.0 for o in ops], [finish(o, 0.0, M, [0.0]) for o in ops],
            [start_up(o, M) for o in ops]) for M in models]
    rel = [o.get("rel", 0.0) if o["c"][0] == "arr" else 0.0 for o in ops]
    state = [seed]

    def draw(m):
        state[0] = (state[0] * 1103515245 + 12345) % 2 ** 31
        return (state[0] >> 8) % m

    def run(order, tb, a=0, old=None):
        co, dp, _, mv, la, dl = tb
        e, f, why, back = [list(u) for u in old] if old else [[0.0] * n for _ in range(4)]
        free, last, st = [0.0] * 6, [-1] * 6, back[order[a - 1]] if a else 0.0
        for i in order[max(0, a - 200):a]:
            free[eng[i]], last[eng[i]] = f[i], i
        free[5], last[5] = 0.0, -1
        for i in order[a:]:
            q = eng[i]
            t, w = free[q], last[q]
            if rel[i] > t:
                t, w = rel[i], -1
            for j, d in dp[i]:
                if e[j] + d > t:
                    t, w = e[j] + d, -2 - j
            t += co[i]
            f[i], why[i] = t, w
            if q != 5:
                free[q], last[q] = t, i
            if mv[i] >= 0:
                st = max(st, t + dl[i] * 0.7) + mv[i]
                e[i] = st + dl[i] * 0.3
            else:
                e[i] = t + la[i]
            back[i] = st
        return e, f, why, back

    def adopt(order, rs):
        pairs, tails = [], []
        for (co, _, sc, _, _, _), (e, f, why, _) in zip(tab, rs):
            i = e.index(max(e))
            while why[i] != -1:
                if why[i] >= 0:
                    pairs.append((why[i], i))
                i = why[i] if why[i] >= 0 else -2 - why[i]
            q, nx = [0.0] * n, [0.0] * 6
            for i in reversed(order):
                t = 0.0
                for j, d in sc[i]:
                    if q[j] + d > t:
                        t = q[j] + d
                t += e[i] - f[i]
                if eng[i] != 5:
                    t = max(t, nx[eng[i]])
                    nx[eng[i]] = t + co[i]
                q[i] = t + co[i]
            tails.append(q)
        pos, prev, nxt, last = [0] * n, [-1] * n, [-1] * n, [-1] * 6
        for k, v in enumerate(order):
            pos[v], prev[v] = k, last[eng[v]]
            if prev[v] >= 0:
                nxt[prev[v]] = v
            last[eng[v]] = v
        return pairs, tails, pos, prev, nxt

    def score(ms):
        return sum(m / M["was"] for m, M in zip(ms, models)) / len(ms) + max(m / M["was"] for m, M in zip(ms, models))
    rs = [run(order, tb) for tb in tab]
    ms = [max(r[0]) for r in rs]
    pairs, tails, pos, prev, nxt = adopt(order, rs)
    best = (order, score(ms))
    for step in range(tries):
        j, i = pairs[draw(len(pairs))]
        early = draw(2)
        for _ in range((0, 0, 1, 2, 3, 5)[draw(6)]):
            j = prev[j] if early and prev[j] >= 0 else j
            i = nxt[i] if not early and nxt[i] >= 0 else i
        a, b = pos[j], pos[i]
        seg = order[a:b + 1]
        tied = {i if early else j}
        for v in (reversed(seg) if early else seg):
            if v in tied:
                tied.update(ops[v]["dep"] if early else succ[v])
        if (j if early else i) in tied:
            continue
        new = [v for v in seg if (v in tied) == early] + [v for v in seg if (v in tied) != early]
        first, end, est = {}, {}, []
        for v in seg:
            first.setdefault(eng[v], v)
            end[eng[v]] = v
        for (co, dp, sc, _, _, _), (e, f, _, _), q in zip(tab, rs, tails):
            free = {u: (f[prev[v]] if prev[v] >= 0 and u != 5 else 0.0) for u, v in first.items()}
            e2, top = {}, 0.0
            for v in new:
                t = max([free[eng[v]], rel[v]] + [e2.get(u, e[u]) + d for u, d in dp[v]]) + co[v]
                if eng[v] != 5:
                    free[eng[v]] = t
                e2[v] = t = t + e[v] - f[v]
                top = max([top, t] + [t + d + q[u] for u, d in sc[v] if pos[u] > b])
            est.append(max([top] + [free[u] + q[nxt[v]] for u, v in end.items() if u != 5 and nxt[v] >= 0]))
        bar = score(ms) - heat * (1 - step / tries) * math.log((draw(1000) + 1) / 1001)
        if score(est) > bar or (all(abs(x - m) < 1 for x, m in zip(est, ms)) and draw(5)):
            continue
        o2 = order[:a] + new + order[b + 1:]
        r2 = [run(o2, tb, a, r) for tb, r in zip(tab, rs)]
        m2 = [max(r[0]) for r in r2]
        if score(m2) <= bar:
            order, rs, ms = o2, r2, m2
            pairs, tails, pos, prev, nxt = adopt(order, rs)
            if score(ms) < best[1]:
                best = (order, score(ms))
    return best


def improve(ops, order, models, passes, seed=1, tries=70, flip=None, begin=0, stop=1):
    n, nm = len(ops), len(models) - 1
    state = [seed]

    def draw(m):
        state[0] = (state[0] * 1103515245 + 12345) % 2 ** 31
        return (state[0] >> 8) % m
    above, pred, succ = [], [], [[] for _ in ops]
    for o in ops:
        far = 0
        for j in o["dep"]:
            far |= above[j]
        pred.append([j for j in o["dep"] if not far >> j & 1])
        for j in o["dep"]:
            far |= 1 << j
        above.append(far)
        for j in pred[-1]:
            succ[j].append(o["i"])
    eng, rel = [0] * n, [o.get("rel", 0.0) for o in ops]
    tab = [[[0] * n for _ in range(6)] for M in models]

    def fill(i):
        o = ops[i]
        eng[i] = "vapgsx".index(o["e"])
        for (co, dp, mv, la, dl, sc), M in zip(tab, models):
            co[i], la[i], dl[i] = cost(o, M), finish(o, 0.0, M, [0.0]), start_up(o, M)
            mv[i] = o["c"][1] / M["bw"] if o["c"][0] in ("dma", "rem") else -1.0
            dp[i] = [(j, delay(ops[j], o, M)) for j in pred[i]]
            sc[i] = [(j, delay(o, ops[j], M)) for j in succ[i]]
    for i in range(n):
        fill(i)

    def run(seq, tb, e, free, st, beg=None):
        co, dp, mv, la, dl, _ = tb
        for i in seq:
            q = eng[i]
            t = free[q]
            if rel[i] > t:
                t = rel[i]
            for j, d in dp[i]:
                if e[j] + d > t:
                    t = e[j] + d
            if beg:
                beg[i] = t
            t += co[i]
            if q != 5:
                free[q] = t
            if mv[i] >= 0:
                u = t + dl[i] * 0.7
                st = (st if st > u else u) + mv[i]
                e[i] = st + dl[i] * 0.3
            else:
                e[i] = t + la[i]
        return st

    def tails(seq, tb):
        co, _, mv, la, dl, sc = tb
        q, qd, nx, nd = [0.0] * n, [0.0] * n, [0.0] * 6, 0.0
        for i in reversed(seq):
            t = max([0.0] + [q[j] + d for j, d in sc[i]])
            if mv[i] >= 0:
                qd[i] = nd = max(t + dl[i] * 0.3, nd) + mv[i]
                t = nd + dl[i] * 0.7
            else:
                t += la[i]
            if eng[i] != 5:
                t = max(t, nx[eng[i]])
                nx[eng[i]] = t + co[i]
            q[i] = t + co[i]
        return q, qd

    def place(win, key, e, free, st):
        co, dp, mv, la, dl, _ = tab[nm]
        left = {i: 0 for i in win}
        for i in win:
            for j in succ[i]:
                if j in left:
                    left[j] += 1
        ready = [i for i in win if not left[i]]
        gs, ge, beg = [[t] for t in free] + [[st]], [[1e18] for _ in range(7)], {}

        def fit(q, t, c):
            S, E = gs[q], ge[q]
            k = len(S) - 1
            while k and S[k] > t:
                k -= 1
            while True:
                a = S[k] if S[k] > t else t
                if a + c <= E[k]:
                    break
                k += 1
            if a - S[k] < 20.0:
                S[k] = a + c
            elif E[k] - a - c < 20.0:
                E[k] = a
            else:
                S.insert(k + 1, a + c)
                E.insert(k, a)
            return a
        while ready:
            i = min(ready, key=key.get)
            ready.remove(i)
            t = rel[i]
            for j, d in dp[i]:
                if e[j] + d > t:
                    t = e[j] + d
            c = co[i]
            if eng[i] != 5:
                t = fit(eng[i], t, c)
            beg[i] = t + i * 1e-6
            if mv[i] >= 0:
                e[i] = fit(6, t + c + dl[i] * 0.7, mv[i]) + mv[i] + dl[i] * 0.3
            else:
                e[i] = t + c + la[i]
            for j in succ[i]:
                if j in left:
                    left[j] -= 1
                    if not left[j]:
                        ready.append(j)
        return sorted(win, key=beg.get)

    def score(ms):
        r = [m / M["was"] for m, M in zip(ms, models)]
        return sum(r) / len(r) + max(r)
    order = list(order)
    for _ in range(passes):
        tl = [tails(order, tb) for tb in tab[:nm]]
        heads = [[[0.0] * n, [0.0] * 6, 0.0] for tb in tab]
        a = begin
        for tb, h in zip(tab, heads):
            h[2] = run(order[:a], tb, h[0], h[1], h[2])
        while a < stop * n - 1:
            b = min(n, a + 80 + draw(140))
            win, inside = order[a:b], set(order[a:b])
            after = set(order[b:])
            first = {}
            for j in order[b:b + 400]:
                first.setdefault(eng[j], j)
                if tab[0][2][j] >= 0:
                    first.setdefault(6, j)
            first.pop(5, 0)
            fixed = [max([0.0] + [h[0][i] + d + q[j] for i in order[max(0, a - 300):a] for j, d in tb[5][i] if j in after])
                     for tb, h, (q, _) in zip(tab, heads, tl)]
            edge = [i for i in win if b == n or any(j in after for j in succ[i])]
            now = []

            def value(w, bar):
                ms = []
                for tb, (e, free, st), (q, qd), m in zip(tab, heads, tl, fixed):
                    if now and ms and ms[-1] > now[len(ms) - 1] * 1.004:
                        return False
                    fr = list(free)
                    fr.append(run(w, tb, e, fr, st))
                    for u, j in first.items():
                        m = max(m, fr[u] + (q[j] if u < 6 else qd[j]))
                    for i in edge:
                        t = e[i]
                        if t > m:
                            m = t
                        for j, d in tb[5][i]:
                            if j in after and t + d + q[j] > m:
                                m = t + d + q[j]
                    ms.append(m)
                if score(ms) > bar:
                    return False
                now[:] = ms
                return True
            value(win, 9.0)
            e, free, st = heads[nm]
            beg = [0.0] * n
            run(win, tab[nm], e, list(free), st, beg)
            some = [i for i in win if eng[i] < 4]
            for _ in range(tries):
                key = {i: beg[i] for i in win}
                back = flip(win, inside, draw, fill, pred, succ) if flip else None
                for _ in range((1, 1, 2, 3)[draw(4)] if not back else draw(3) // 2):
                    j = some[draw(len(some))]
                    d = math.exp(4.6 + draw(1000) * 0.0037) * (2 * draw(2) - 1)
                    key[j] += d
                    stack = [j] if d < 0 else []
                    while stack:
                        u = stack.pop()
                        for w in pred[u]:
                            if w in inside and key[w] >= key[u]:
                                key[w] = key[u] - 1
                                stack.append(w)
                new = place(win, key, e, free, st)
                if (back or new != win) and value(new, score(now) + 1e-9):
                    win = new
                    run(win, tab[nm], e, list(free), st, beg)
                elif back:
                    back()
            order[a:b] = win
            step = (b - a) // 2 + 1
            for tb, h in zip(tab, heads):
                h[2] = run(order[a:a + step], tb, h[0], h[1], h[2])
            a += step
    ms = []
    for tb in tab[:nm]:
        e = [0.0] * n
        run(order, tb, e, [0.0] * 6, 0.0)
        ms.append(max(e))
    return order, score(ms), ms


def make_order(ops, passes=None):
    return improve(ops, schedule(ops, MID, BUMP, 4)[0], MODELS + [MID], PASSES if passes is None else passes, SEED)[0]


ORDER = []


def rank_program(g, core, T, topo):
    if T.rank_of(core) is None:
        return
    ops = build(g, core, T, topo, PLAN)
    if not ORDER:
        ORDER.append(make_order(ops))
    emit(g, T, ops, ORDER[0])
